import numpy as np
import ml_dtypes


def mxq(x, axis, fmt="e4m3"):
    dtype, down = {"e4m3": (ml_dtypes.float8_e4m3fn, 7), "e5m2": (ml_dtypes.float8_e5m2, 14)}[fmt]
    v = np.moveaxis(np.asarray(x, np.float32).astype(ml_dtypes.bfloat16).astype(np.float64), axis, -1)
    blocks = v.reshape(v.shape[:-1] + (-1, 32))
    amax = np.abs(blocks).max(-1, keepdims=True)
    byte = np.maximum(np.where(amax > 0, np.frexp(amax)[1] - 1 + 127, 0) - down, 1)
    scale = np.exp2(byte - 127.0)
    codes = (blocks / scale).astype(np.float32).astype(dtype).astype(np.float64)
    return np.moveaxis((codes * scale).reshape(v.shape), -1, axis)


WIDE = False


def mx_kscale(k):
    if not WIDE:
        return np.ones(k)
    levels = np.array([10, -10, 5, -5, 0])
    if k % 512:
        return np.exp2(np.random.permutation(np.resize(levels, k // 32))).repeat(32)
    a = np.empty((k // 512, 16))
    for p in range(k // 512):
        a[p, :8] = np.random.permutation(np.resize(levels, 8))
        for g in range(8):
            far = levels[np.abs(levels - a[p, g]) >= 10]
            a[p, g + 8] = far[np.random.randint(len(far))]
    return np.exp2(a.ravel()).repeat(32)


def f64(x):
    return np.asarray(x).astype(np.float64)


def striped(idx):
    return np.tile(idx.reshape(-1, 16).T, (8, 1)).astype(np.uint16)


def unstriped(offs):
    return offs[:16].T.reshape(-1).astype(np.int64)


E2M1 = np.array([0.0, 0.5, 1.0, 1.5, 2.0, 3.0, 4.0, 6.0, -0.0, -0.5, -1.0, -1.5, -2.0, -3.0, -4.0, -6.0])


def pack_weight(w, fmt):
    k, n = w.shape
    w = f64(np.asarray(w, np.float32).astype(ml_dtypes.bfloat16)).reshape(k // 32, 32, n)
    amax = np.abs(w).max(1)
    if fmt == "e4m3":
        byte = np.frexp(amax)[1] - 1 + 127 - 7
    else:
        mant, ex = np.frexp(amax / 6.0)
        byte = np.where(mant > 0.5, ex, ex - 1) + 127
    byte = np.clip(np.where(amax > 0, byte, 1), 1, 254)
    scaled = (w * np.exp2(127.0 - byte)[:, None, :]).reshape(k, n).astype(np.float32)
    by_word = np.ascontiguousarray(scaled.reshape(k // 512, 128, 4, n).transpose(0, 1, 3, 2))
    if fmt == "e4m3":
        words = by_word.astype(ml_dtypes.float8_e4m3fn).view(np.uint8)
    else:
        c = by_word.astype(ml_dtypes.float4_e2m1fn).view(np.uint8) & 0xF
        words = (c[..., 0::2] | (c[..., 1::2] << 4)).reshape(k // 512, 128, 2 * n)
    return np.ascontiguousarray(words), np.ascontiguousarray(byte.astype(np.uint8).reshape(k // 512, 16, n))


def unpack_weight(words, scales, fmt):
    g, _, n = scales.shape
    words = np.ascontiguousarray(words).reshape(g, 128, n, -1)
    if fmt == "e4m3":
        vals = words.view(ml_dtypes.float8_e4m3fn).astype(np.float64)
    else:
        nib = np.empty((g, 128, n, 4), np.uint8)
        nib[..., 0::2] = words & 0xF
        nib[..., 1::2] = words >> 4
        vals = E2M1[nib]
    vals = vals * np.repeat(np.exp2(scales.astype(np.float64) - 127.0), 8, axis=1)[..., None]
    return vals.transpose(0, 1, 3, 2).reshape(g * 512, n)


def gelu(v):
    return 0.5 * v * (1.0 + np.tanh(np.sqrt(2.0 / np.pi) * (v + 0.044715 * v**3)))


K, H, T, S, T2, S2, T3, P = 1536, 512, 4096, 1024, 2048, 512, 2048, 1024

def setup_inputs():
    n = np.random.standard_normal
    s = mx_kscale(K)[:, None]
    u = mx_kscale(H)[:, None]
    tab_words, tab_scales = pack_weight(n((K, T)) * s, "e4m3")
    w2_words, w2_scales = pack_weight(n((K, H)) / np.sqrt(K) / s * u.T, "e2m1")
    tab2_words, tab2_scales = pack_weight(n((H, T3)) / np.sqrt(H) / u, "e4m3")
    return {
        "tab_words": tab_words, "tab_scales": tab_scales,
        "offs": striped(np.random.permutation(T)[:S]),
        "w1": (n((K, H)) / np.sqrt(K) / s).astype(np.float32),
        "w2_words": w2_words, "w2_scales": w2_scales,
        "gain": (np.random.uniform(0.7, 1.7, H) * u[:, 0]).astype(np.float32),
        "page0": (n((H, T2)) * u).astype(np.float32),
        "wgs": np.exp(0.3 * n((128, S))).astype(np.float32),
        "offs3": striped(np.random.permutation(T2)[:S]),
        "tab2_words": tab2_words, "tab2_scales": tab2_scales,
        "offs2": striped(np.random.permutation(T3)[:S2]),
        "aff": (0.5 * n(S2)).astype(np.float32),
        "lod": (0.6 * n((S2, P)) - 0.4).astype(np.float32),
        "offs4": striped(np.random.permutation(T2)[:P]),
    }

def reference(tab_words, tab_scales, offs, w1, w2_words, w2_scales, gain, page0, wgs, offs3,
              tab2_words, tab2_scales, offs2, aff, lod, offs4):
    v = unpack_weight(tab_words, tab_scales, "e4m3")[:, unstriped(offs)]
    w2 = unpack_weight(w2_words, w2_scales, "e2m1")
    a = mxq(f64(w1), 0, "e4m3").T @ v
    b = w2.T @ v
    h = f64(gain)[:, None] * (a / (1.0 + np.exp(-a))) + b
    page = f64(page0).copy()
    page[:, unstriped(offs3)] = np.tile(f64(wgs), (H // 128, 1)) * h
    v2 = unpack_weight(tab2_words, tab2_scales, "e4m3")[:, unstriped(offs2)]
    e = v2.T @ mxq(page, 0, "e4m3")
    x = e[:, unstriped(offs4)]
    return np.maximum(x + f64(aff)[:, None], f64(lod))

@@ -1,0 +1,292 @@
+from contextlib import ExitStack
+
+import concourse.mybir as mybir
+
+K, H, T, S, T2, S2, T3, M = 1536, 512, 4096, 1024, 2048, 512, 2048, 1024
+FLOPS = 2 * (2 * K * H * S + H * S2 * T2)
+
+F32 = mybir.dt.float32
+BF16 = mybir.dt.bfloat16
+I32 = mybir.dt.int32
+U32 = mybir.dt.uint32
+U16 = mybir.dt.uint16
+U8 = mybir.dt.uint8
+FP8X4 = mybir.dt.float8_e4m3fn_x4
+FP4X4 = mybir.dt.float4_e2m1fn_x4
+ALU = mybir.AluOpType
+ACT = mybir.ActivationFunctionType
+
+P = 128
+PACK = 4
+PASSES = K // (P * PACK)
+NB = 512
+QUADS = 4
+SHIFT_ROWS = 112
+
+
+def tile_list_antivenom_panel_scores_kernel(
+    tc, tab_words, tab_scales, offs, w1, w2_words, w2_scales, gain, page0, wgs, offs3,
+    tab2_words, tab2_scales, offs2, aff, lod, offs4, out,
+):
+    nc = tc.nc
+    with ExitStack() as ctx:
+        lists = ctx.enter_context(tc.tile_pool(name="lists", bufs=1))
+        sb = ctx.enter_context(tc.tile_pool(name="sb", bufs=1))
+        psum = ctx.enter_context(tc.psum_pool(name="psum", bufs=1))
+
+        def tile(shape, dtype, name, tag=None):
+            return sb.tile(shape, dtype, name=name, tag=tag or name, align_bytes=64)
+
+        def bank(i, name):
+            return psum.tile([P, NB], F32, name=name, tag="bank%d" % i)
+
+        def half(i):
+            return slice(i * NB, (i + 1) * NB)
+
+        def list_half(i):
+            return slice(i * NB // 16, (i + 1) * NB // 16)
+
+        idx = lists.tile([P, S // 16], U16, name="idx")
+        idx2 = lists.tile([P, S2 // 16], U16, name="idx2")
+        idx3 = lists.tile([P, S // 16], U16, name="idx3")
+        idx4 = lists.tile([P, M // 16], U16, name="idx4")
+
+        tab_sc = tile([P, T], U8, "tab_sc")
+        w2_sc_raw = tile([P, PASSES, H], U8, "w2_sc_raw")
+        tab2_sc = tile([P, T3], U8, "tab2_sc")
+        v_sc_low = tile([P, PASSES - 1, S], U8, "v_sc_low")
+        nc.vector.memset(tab_sc[:].bitcast(I32), 0)
+        nc.vector.memset(w2_sc_raw[:].bitcast(I32), 0)
+        nc.vector.memset(v_sc_low[:].bitcast(I32), 0)
+        nc.vector.memset(tab2_sc[:].bitcast(I32), 0)
+        for q in range(QUADS):
+            nc.gpsimd.dma_start(
+                out=tab_sc[32 * q : 32 * q + 4 * PASSES, :].bitcast(I32),
+                in_=tab_scales[:, 4 * q : 4 * q + 4, :].bitcast(I32),
+            )
+        for q in range(QUADS):
+            nc.gpsimd.dma_start(
+                out=w2_sc_raw[32 * q : 32 * q + 4, :, :].bitcast(I32),
+                in_=w2_scales[:, 4 * q : 4 * q + 4, :].rearrange("a r n -> r a n").bitcast(I32),
+            )
+
+        nc.sync.dma_start(idx[:], offs)
+        w2_raw = tile([P, PASSES, 2 * H], U8, "w2_raw")
+        nc.sync.dma_start(out=w2_raw[:].bitcast(I32), in_=w2_words.rearrange("a p n -> p a n").bitcast(I32))
+        w1_raw, tab_w = [], []
+        for a in range(PASSES):
+            raw = tile([P, PACK, H], F32, "w1_raw%d" % a)
+            nc.sync.dma_start(out=raw[:], in_=w1[a * 512 : (a + 1) * 512, :].rearrange("(p j) c -> p j c", j=PACK))
+            w1_raw.append(raw)
+            words = tile([P, T], I32, "tab_w%d" % a)
+            nc.sync.dma_start(out=words[:], in_=tab_words[a].rearrange("p t i -> p (t i)").bitcast(I32))
+            tab_w.append(words)
+        gain_sb = tile([P, PACK], F32, "gain_sb")
+        nc.sync.dma_start(out=gain_sb[:], in_=gain.rearrange("(p t) -> p t", t=PACK))
+        nc.sync.dma_start(idx3[:], offs3)
+        page_rows = page0.rearrange("(p t) c -> t p c", t=PACK)
+        wgs_rows = wgs.rearrange("(m t) j -> m t j", t=PACK)
+        page = [tile([P, T2], F32, "page%d" % t) for t in range(PACK)]
+        wgs_first = tile([P, S], F32, "wgs_first")
+        wgs_rest = tile([P, PACK - 1, S], F32, "wgs_rest")
+        nc.sync.dma_start(out=page[0][:], in_=page_rows[0])
+        for q in range(QUADS):
+            nc.sync.dma_start(out=wgs_first[32 * q : 32 * q + 32, :], in_=wgs_rows[:, 0, :])
+        nc.sync.dma_start(out=page[1][:], in_=page_rows[1])
+        for q in range(QUADS):
+            nc.sync.dma_start(out=wgs_rest[32 * q : 32 * q + 32, :, :], in_=wgs_rows[:, 1:PACK, :])
+        for t in range(2, PACK):
+            nc.sync.dma_start(out=page[t][:], in_=page_rows[t])
+        nc.sync.dma_start(idx2[:], offs2)
+        nc.sync.dma_start(idx4[:], offs4)
+        tab2_w = tile([P, T3], I32, "tab2_w")
+        nc.sync.dma_start(out=tab2_w[:], in_=tab2_words[0].rearrange("p t i -> p (t i)").bitcast(I32))
+        aff_sb = tile([P, S2 // P], F32, "aff_sb")
+        with nc.allow_non_contiguous_dma(reason="one offset for each partition and tile of antibodies"):
+            nc.sync.dma_start(out=aff_sb[:], in_=aff.rearrange("(c p) -> p c", p=P))
+
+        v_sc = tile([P, S], U8, "v_sc")
+        nc.vector.tensor_copy(v_sc[:], tab_sc[:].indirect(idx[:]))
+        for a in range(1, PASSES):
+            nc.gpsimd.dma_start(
+                out=v_sc_low[0:SHIFT_ROWS, a - 1, :].bitcast(I32),
+                in_=v_sc[4 * a : 4 * a + SHIFT_ROWS, :].bitcast(I32),
+            )
+        for q in range(QUADS):
+            nc.gpsimd.dma_start(
+                out=tab2_sc[32 * q : 32 * q + 4, :].bitcast(I32),
+                in_=tab2_scales[0, 4 * q : 4 * q + 4, :].bitcast(I32),
+            )
+
+        def v_plane(a, cols):
+            return v_sc[:, cols] if a == 0 else v_sc_low[:, a - 1, cols]
+
+        w2_c = tile([P, PASSES, 2 * H], U8, "w2_c")
+        w2_s = tile([P, PASSES, H], U8, "w2_s")
+        nc.vector.tensor_copy(
+            out=w2_c[:].bitcast(U16).rearrange("p a (t m) -> p a m t", t=PACK),
+            in_=w2_raw[:].bitcast(U16).rearrange("p a (m t) -> p a m t", t=PACK),
+        )
+        nc.vector.tensor_copy(
+            out=w2_s[:].rearrange("p a (t m) -> p a m t", t=PACK),
+            in_=w2_sc_raw[:].rearrange("p a (m t) -> p a m t", t=PACK),
+        )
+
+        w1_c, w1_s, v_w = [], [], []
+        acc = {}
+
+        def first_stage_pass(t, hf, a):
+            if a == 0:
+                base = (t % 2) * 4 + hf * 2
+                acc[t, hf] = (bank(base, "acc_a%d%d" % (t, hf)), bank(base + 1, "acc_b%d%d" % (t, hf)))
+            acc_a, acc_b = acc[t, hf]
+            ch = slice(t * P, (t + 1) * P)
+            moving = v_w[a][:, half(hf)].bitcast(FP8X4)
+            nc.tensor.matmul_mx(
+                out=acc_a[:], lhsT=w1_c[a][:, ch].bitcast(FP8X4), lhsT_scale=w1_s[a][:, ch],
+                rhs=moving, rhs_scale=v_plane(a, half(hf)), start=(a == 0), stop=(a == PASSES - 1),
+            )
+            nc.tensor.matmul_mx(
+                out=acc_b[:], lhsT=w2_c[:, a, 2 * t * P : 2 * (t + 1) * P].bitcast(FP4X4), lhsT_scale=w2_s[:, a, ch],
+                rhs=moving, rhs_scale=v_plane(a, half(hf)), start=(a == 0), stop=(a == PASSES - 1),
+            )
+
+        for a in range(PASSES):
+            grouped = tile([P, H * PACK], BF16, "w1_grouped%d" % a, tag="w1_grouped%d" % (a % 2))
+            nc.scalar.copy(
+                out=grouped[:].rearrange("p (t m j) -> p m j t", t=PACK, j=PACK),
+                in_=w1_raw[a][:].rearrange("p j (m t) -> p m j t", t=PACK),
+            )
+            codes = tile([P, H], U32, "w1_c%d" % a)
+            scales = tile([P, H], U8, "w1_s%d" % a)
+            nc.vector.quantize_mx(out=codes[:].bitcast(FP8X4), scales=scales[:], in_=grouped[:])
+            w1_c.append(codes)
+            w1_s.append(scales)
+            picked = tile([P, S], U32, "v_w%d" % a)
+            v_w.append(picked)
+            window = tab_w[a][:].bitcast(U32)
+            if a < PASSES - 1:
+                nc.vector.tensor_copy(picked[:], window.indirect(idx[:]))
+            else:
+                for hf in range(2):
+                    nc.vector.tensor_copy(picked[:, half(hf)], window.indirect(idx[:, list_half(hf)]))
+            for t in range(2):
+                for hf in range(2):
+                    first_stage_pass(t, hf, a)
+
+        lod_rows = lod.rearrange("(c p) m -> p c m", p=P)
+        lod_sb = []
+        for i in range(2):
+            floor = tile([P, 2, M], F32, "lod%d" % i, tag="w1_raw%d" % i)
+            nc.sync.dma_start(out=floor[:], in_=lod_rows[:, 2 * i : 2 * i + 2, :])
+            lod_sb.append(floor)
+
+        h = {}
+        page_bf = [tile([P, NB, PACK], BF16, "page_bf%d" % c) for c in range(T2 // NB)]
+
+        def make_h(t, hf):
+            if hf == 0:
+                h[t] = tile([P, S], F32, "h%d" % t, tag="h%d" % (t % 2))
+            acc_a, acc_b = acc[t, hf]
+            act = tile([P, NB], F32, "silu%d%d" % (t, hf), tag="silu%d%d" % (t % 2, hf))
+            nc.scalar.activation(out=act[:], in_=acc_a[:], func=ACT.Silu)
+            nc.vector.scalar_tensor_tensor(
+                out=h[t][:, half(hf)], in0=act[:], scalar=gain_sb[:, t : t + 1], in1=acc_b[:],
+                op0=ALU.mult, op1=ALU.add,
+            )
+            if t + 2 < PACK:
+                for a in range(PASSES):
+                    first_stage_pass(t + 2, hf, a)
+
+        def weights(t):
+            return wgs_first[:] if t == 0 else wgs_rest[:, t - 1, :]
+
+        def scatter(t, hf=None):
+            if hf is None:
+                nc.vector.tensor_tensor(page[t][:].indirect(idx3[:]), h[t][:], weights(t), ALU.mult)
+            else:
+                nc.vector.tensor_tensor(
+                    page[t][:].indirect(idx3[:, list_half(hf)]), h[t][:, half(hf)], weights(t)[:, half(hf)], ALU.mult
+                )
+
+        def round_plane(t, c):
+            nc.scalar.copy(out=page_bf[c][:, :, t], in_=page[t][:, half(c)])
+
+        make_h(0, 0)
+        scatter(0, 0)
+        make_h(0, 1)
+        make_h(1, 0)
+        scatter(0, 1)
+        make_h(1, 1)
+        for t in range(1, PACK):
+            if t + 1 < PACK:
+                make_h(t + 1, 0)
+            scatter(t)
+            if t + 1 < PACK:
+                make_h(t + 1, 1)
+            for c in range(T2 // NB):
+                round_plane(t - 1, c)
+
+        v2_w = tile([P, S2], U32, "v2_w", tag="h1")
+        v2_s = tile([P, S2], U8, "v2_s", tag="wgs_rest")
+        nc.vector.tensor_copy(v2_w[:], tab2_w[:].bitcast(U32).indirect(idx2[:]))
+        nc.vector.tensor_copy(v2_s[:], tab2_sc[:].indirect(idx2[:]))
+
+        e_tags = ["tab_w0", "tab_w1", "tab_w2", "w1_raw2"]
+        e = [tile([P, T2], F32, "e%d" % n, tag=e_tags[n]) for n in range(S2 // P)]
+        page_c, page_s = [], []
+
+        def scores(n, c):
+            ps = bank((n % 2) * 4 + c, "score%d%d" % (n, c))
+            rows = slice(n * P, (n + 1) * P)
+            nc.tensor.matmul_mx(
+                out=ps[:], lhsT=v2_w[:, rows].bitcast(FP8X4), lhsT_scale=v2_s[:, rows],
+                rhs=page_c[c][:].bitcast(FP8X4), rhs_scale=page_s[c][:], start=True, stop=True,
+            )
+            if n == 0:
+                nc.vector.tensor_copy(out=e[n][:, half(c)], in_=ps[:])
+            else:
+                nc.scalar.copy(out=e[n][:, half(c)], in_=ps[:])
+
+        for c in range(T2 // NB):
+            round_plane(PACK - 1, c)
+        for c in range(T2 // NB):
+            codes = tile([P, NB], U32, "page_c%d" % c)
+            scales = tile([P, NB], U8, "page_s%d" % c)
+            nc.vector.quantize_mx(
+                out=codes[:].bitcast(FP8X4), scales=scales[:], in_=page_bf[c][:].rearrange("p c t -> p (c t)")
+            )
+            page_c.append(codes)
+            page_s.append(scales)
+            scores(0, c)
+        for n in range(1, S2 // P):
+            for c in range(T2 // NB):
+                scores(n, c)
+
+        x_tags = ["v_w0", "v_w1", "v_w2", "w1_grouped0"]
+        x = [tile([P, M], F32, "x%d" % n, tag=x_tags[n]) for n in range(S2 // P)]
+        last = S2 // P - 1
+
+        def pick(n, hf=None):
+            if hf is None:
+                nc.vector.tensor_copy(x[n][:], e[n][:].indirect(idx4[:]))
+            else:
+                nc.vector.tensor_copy(x[n][:, half(hf)], e[n][:].indirect(idx4[:, list_half(hf)]))
+
+        def finish(n, cols):
+            nc.vector.scalar_tensor_tensor(
+                out=x[n][:, cols], in0=x[n][:, cols], scalar=aff_sb[:, n : n + 1], in1=lod_sb[n // 2][:, n % 2, cols],
+                op0=ALU.add, op1=ALU.max,
+            )
+            nc.sync.dma_start(out=out[n * P : (n + 1) * P, cols], in_=x[n][:, cols])
+
+        whole = slice(0, M)
+        pick(0)
+        for n in range(1, last):
+            pick(n)
+            finish(n - 1, whole)
+        pick(last, 0)
+        finish(last - 1, whole)
+        pick(last, 1)
+        finish(last, half(0))
+        finish(last, half(1))

@@ -57,33 +57,43 @@ def tile_list_antivenom_panel_scores_kernel(
         v_sc_low = tile([P, PASSES - 1, S], U8, "v_sc_low")
         nc.vector.memset(tab_sc[:].bitcast(I32), 0)
         nc.vector.memset(w2_sc_raw[:].bitcast(I32), 0)
-        nc.vector.memset(v_sc_low[:].bitcast(I32), 0)
         nc.vector.memset(tab2_sc[:].bitcast(I32), 0)
         for q in range(QUADS):
-            nc.gpsimd.dma_start(
+            nc.scalar.dma_start(
                 out=tab_sc[32 * q : 32 * q + 4 * PASSES, :].bitcast(I32),
                 in_=tab_scales[:, 4 * q : 4 * q + 4, :].bitcast(I32),
             )
         for q in range(QUADS):
-            nc.gpsimd.dma_start(
+            nc.scalar.dma_start(
                 out=w2_sc_raw[32 * q : 32 * q + 4, :, :].bitcast(I32),
                 in_=w2_scales[:, 4 * q : 4 * q + 4, :].rearrange("a r n -> r a n").bitcast(I32),
             )
 
-        nc.sync.dma_start(idx[:], offs)
+        w1_raw = [tile([P, PACK, H], F32, "w1_raw%d" % a) for a in range(PASSES)]
+        tab_w = [tile([P, T], I32, "tab_w%d" % a) for a in range(PASSES)]
         w2_raw = tile([P, PASSES, 2 * H], U8, "w2_raw")
-        nc.sync.dma_start(out=w2_raw[:].bitcast(I32), in_=w2_words.rearrange("a p n -> p a n").bitcast(I32))
-        w1_raw, tab_w = [], []
-        for a in range(PASSES):
-            raw = tile([P, PACK, H], F32, "w1_raw%d" % a)
-            nc.sync.dma_start(out=raw[:], in_=w1[a * 512 : (a + 1) * 512, :].rearrange("(p j) c -> p j c", j=PACK))
-            w1_raw.append(raw)
-            words = tile([P, T], I32, "tab_w%d" % a)
-            nc.sync.dma_start(out=words[:], in_=tab_words[a].rearrange("p t i -> p (t i)").bitcast(I32))
-            tab_w.append(words)
         gain_sb = tile([P, PACK], F32, "gain_sb")
+        aff_sb = tile([P, S2 // P], F32, "aff_sb")
+
+        def load_w1(a):
+            nc.sync.dma_start(out=w1_raw[a][:], in_=w1[a * 512 : (a + 1) * 512, :].rearrange("(p j) c -> p j c", j=PACK))
+
+        def load_tab(a):
+            nc.sync.dma_start(out=tab_w[a][:], in_=tab_words[a].rearrange("p t i -> p (t i)").bitcast(I32))
+
+        load_w1(0)
+        nc.sync.dma_start(idx[:], offs)
         nc.sync.dma_start(out=gain_sb[:], in_=gain.rearrange("(p t) -> p t", t=PACK))
         nc.sync.dma_start(idx3[:], offs3)
+        nc.sync.dma_start(idx2[:], offs2)
+        nc.sync.dma_start(idx4[:], offs4)
+        with nc.allow_non_contiguous_dma(reason="one offset for each partition and tile of antibodies"):
+            nc.sync.dma_start(out=aff_sb[:], in_=aff.rearrange("(c p) -> p c", p=P))
+        nc.sync.dma_start(out=w2_raw[:].bitcast(I32), in_=w2_words.rearrange("a p n -> p a n").bitcast(I32))
+        load_tab(0)
+        for a in range(1, PASSES):
+            load_w1(a)
+            load_tab(a)
         page_rows = page0.rearrange("(p t) c -> t p c", t=PACK)
         wgs_rows = wgs.rearrange("(m t) j -> m t j", t=PACK)
         page = [tile([P, T2], F32, "page%d" % t) for t in range(PACK)]
@@ -95,27 +105,22 @@ def tile_list_antivenom_panel_scores_kernel(
         nc.sync.dma_start(out=page[1][:], in_=page_rows[1])
         for q in range(QUADS):
             nc.sync.dma_start(out=wgs_rest[32 * q : 32 * q + 32, :, :], in_=wgs_rows[:, 1:PACK, :])
-        for t in range(2, PACK):
-            nc.sync.dma_start(out=page[t][:], in_=page_rows[t])
-        nc.sync.dma_start(idx2[:], offs2)
-        nc.sync.dma_start(idx4[:], offs4)
+        nc.sync.dma_start(out=page[2][:], in_=page_rows[2])
         tab2_w = tile([P, T3], I32, "tab2_w")
         nc.sync.dma_start(out=tab2_w[:], in_=tab2_words[0].rearrange("p t i -> p (t i)").bitcast(I32))
-        aff_sb = tile([P, S2 // P], F32, "aff_sb")
-        with nc.allow_non_contiguous_dma(reason="one offset for each partition and tile of antibodies"):
-            nc.sync.dma_start(out=aff_sb[:], in_=aff.rearrange("(c p) -> p c", p=P))
+        for q in range(QUADS):
+            nc.sync.dma_start(
+                out=tab2_sc[32 * q : 32 * q + 4, :].bitcast(I32),
+                in_=tab2_scales[0, 4 * q : 4 * q + 4, :].bitcast(I32),
+            )
+        nc.sync.dma_start(out=page[3][:], in_=page_rows[3])
 
         v_sc = tile([P, S], U8, "v_sc")
         nc.vector.tensor_copy(v_sc[:], tab_sc[:].indirect(idx[:]))
         for a in range(1, PASSES):
-            nc.gpsimd.dma_start(
+            nc.scalar.dma_start(
                 out=v_sc_low[0:SHIFT_ROWS, a - 1, :].bitcast(I32),
                 in_=v_sc[4 * a : 4 * a + SHIFT_ROWS, :].bitcast(I32),
-            )
-        for q in range(QUADS):
-            nc.gpsimd.dma_start(
-                out=tab2_sc[32 * q : 32 * q + 4, :].bitcast(I32),
-                in_=tab2_scales[0, 4 * q : 4 * q + 4, :].bitcast(I32),
             )
 
         def v_plane(a, cols):
@@ -144,7 +149,7 @@ def tile_list_antivenom_panel_scores_kernel(
             moving = v_w[a][:, half(hf)].bitcast(FP8X4)
             nc.tensor.matmul_mx(
                 out=acc_a[:], lhsT=w1_c[a][:, ch].bitcast(FP8X4), lhsT_scale=w1_s[a][:, ch],
-                rhs=moving, rhs_scale=v_plane(a, half(hf)), start=(a == 0), stop=(a == PASSES - 1),
+                rhs=moving, rhs_scale=v_sc[4 * a : P, half(hf)], start=(a == 0), stop=(a == PASSES - 1),
             )
             nc.tensor.matmul_mx(
                 out=acc_b[:], lhsT=w2_c[:, a, 2 * t * P : 2 * (t + 1) * P].bitcast(FP4X4), lhsT_scale=w2_s[:, a, ch],
@@ -210,7 +215,14 @@ def tile_list_antivenom_panel_scores_kernel(
                 )
 
         def round_plane(t, c):
-            nc.scalar.copy(out=page_bf[c][:, :, t], in_=page[t][:, half(c)])
+            if t == PACK - 1 and c == 1:
+                nc.vector.tensor_copy(out=page_bf[c][:, :, t], in_=page[t][:, half(c)])
+            elif t == PACK - 2 and c == 1:
+                nc.scalar.copy(
+                    out=page_bf[c][:, :, t : t + 2], in_=page[t][:, half(c)].unsqueeze(2).to_broadcast([P, NB, 2])
+                )
+            else:
+                nc.scalar.copy(out=page_bf[c][:, :, t], in_=page[t][:, half(c)])
 
         make_h(0, 0)
         scatter(0, 0)
@@ -227,6 +239,7 @@ def tile_list_antivenom_panel_scores_kernel(
             for c in range(T2 // NB):
                 round_plane(t - 1, c)
 
+        round_plane(PACK - 1, 1)
         v2_w = tile([P, S2], U32, "v2_w", tag="h1")
         v2_s = tile([P, S2], U8, "v2_s", tag="wgs_rest")
         nc.vector.tensor_copy(v2_w[:], tab2_w[:].bitcast(U32).indirect(idx2[:]))
@@ -234,21 +247,24 @@ def tile_list_antivenom_panel_scores_kernel(
 
         e_tags = ["tab_w0", "tab_w1", "tab_w2", "w1_raw2"]
         e = [tile([P, T2], F32, "e%d" % n, tag=e_tags[n]) for n in range(S2 // P)]
-        page_c, page_s = [], []
+        page_c, page_s, first = [], [], []
 
         def scores(n, c):
-            ps = bank((n % 2) * 4 + c, "score%d%d" % (n, c))
+            ps = bank((c, 4 + c, 3 - c, 3 - c)[n], "score%d%d" % (n, c))
             rows = slice(n * P, (n + 1) * P)
             nc.tensor.matmul_mx(
                 out=ps[:], lhsT=v2_w[:, rows].bitcast(FP8X4), lhsT_scale=v2_s[:, rows],
                 rhs=page_c[c][:].bitcast(FP8X4), rhs_scale=page_s[c][:], start=True, stop=True,
             )
-            if n == 0:
+            return ps
+
+        def empty(n, c, ps):
+            if n == 0 and c == T2 // NB - 1:
                 nc.vector.tensor_copy(out=e[n][:, half(c)], in_=ps[:])
             else:
                 nc.scalar.copy(out=e[n][:, half(c)], in_=ps[:])
 
-        for c in range(T2 // NB):
+        for c in (0, 2, 3):
             round_plane(PACK - 1, c)
         for c in range(T2 // NB):
             codes = tile([P, NB], U32, "page_c%d" % c)
@@ -258,10 +274,13 @@ def tile_list_antivenom_panel_scores_kernel(
             )
             page_c.append(codes)
             page_s.append(scales)
-            scores(0, c)
+            first.append(scores(0, c))
+            if c > 0:
+                empty(0, c - 1, first[c - 1])
+        empty(0, T2 // NB - 1, first[-1])
         for n in range(1, S2 // P):
             for c in range(T2 // NB):
-                scores(n, c)
+                empty(n, c, scores(n, c))
 
         x_tags = ["v_w0", "v_w1", "v_w2", "w1_grouped0"]
         x = [tile([P, M], F32, "x%d" % n, tag=x_tags[n]) for n in range(S2 // P)]

@@ -21,6 +21,7 @@ PACK = 4
 PASSES = K // (P * PACK)
 NB = 512
 QUADS = 4
+CHUNKS = T2 // NB
 SHIFT_ROWS = 112
 
 
@@ -59,12 +60,12 @@ def tile_list_antivenom_panel_scores_kernel(
         nc.vector.memset(w2_sc_raw[:].bitcast(I32), 0)
         nc.vector.memset(tab2_sc[:].bitcast(I32), 0)
         for q in range(QUADS):
-            nc.scalar.dma_start(
+            nc.gpsimd.dma_start(
                 out=tab_sc[32 * q : 32 * q + 4 * PASSES, :].bitcast(I32),
                 in_=tab_scales[:, 4 * q : 4 * q + 4, :].bitcast(I32),
             )
         for q in range(QUADS):
-            nc.scalar.dma_start(
+            nc.gpsimd.dma_start(
                 out=w2_sc_raw[32 * q : 32 * q + 4, :, :].bitcast(I32),
                 in_=w2_scales[:, 4 * q : 4 * q + 4, :].rearrange("a r n -> r a n").bitcast(I32),
             )
@@ -83,29 +84,30 @@ def tile_list_antivenom_panel_scores_kernel(
 
         load_w1(0)
         nc.sync.dma_start(idx[:], offs)
-        nc.sync.dma_start(out=gain_sb[:], in_=gain.rearrange("(p t) -> p t", t=PACK))
-        nc.sync.dma_start(idx3[:], offs3)
-        nc.sync.dma_start(idx2[:], offs2)
-        nc.sync.dma_start(idx4[:], offs4)
-        with nc.allow_non_contiguous_dma(reason="one offset for each partition and tile of antibodies"):
-            nc.sync.dma_start(out=aff_sb[:], in_=aff.rearrange("(c p) -> p c", p=P))
         nc.sync.dma_start(out=w2_raw[:].bitcast(I32), in_=w2_words.rearrange("a p n -> p a n").bitcast(I32))
         load_tab(0)
         for a in range(1, PASSES):
             load_w1(a)
             load_tab(a)
+        nc.sync.dma_start(out=gain_sb[:], in_=gain.rearrange("(p t) -> p t", t=PACK))
+        nc.sync.dma_start(idx3[:], offs3)
         page_rows = page0.rearrange("(p t) c -> t p c", t=PACK)
         wgs_rows = wgs.rearrange("(m t) j -> m t j", t=PACK)
         page = [tile([P, T2], F32, "page%d" % t) for t in range(PACK)]
-        wgs_first = tile([P, S], F32, "wgs_first")
-        wgs_rest = tile([P, PACK - 1, S], F32, "wgs_rest")
+        wgs_sb = [tile([P, S], F32, "wgs%d" % t) for t in range(PACK)]
+
+        def load_wgs(t, cols):
+            for q in (0, 2, 1, 3):
+                nc.sync.dma_start(out=wgs_sb[t][32 * q : 32 * q + 32, cols], in_=wgs_rows[:, t, cols])
+
         nc.sync.dma_start(out=page[0][:], in_=page_rows[0])
-        for q in range(QUADS):
-            nc.sync.dma_start(out=wgs_first[32 * q : 32 * q + 32, :], in_=wgs_rows[:, 0, :])
-        nc.sync.dma_start(out=page[1][:], in_=page_rows[1])
-        for q in range(QUADS):
-            nc.sync.dma_start(out=wgs_rest[32 * q : 32 * q + 32, :, :], in_=wgs_rows[:, 1:PACK, :])
-        nc.sync.dma_start(out=page[2][:], in_=page_rows[2])
+        load_wgs(0, half(0))
+        load_wgs(0, half(1))
+        for t in range(1, PACK - 1):
+            nc.sync.dma_start(out=page[t][:], in_=page_rows[t])
+            load_wgs(t, slice(0, S))
+        nc.sync.dma_start(idx2[:], offs2)
+        nc.sync.dma_start(idx4[:], offs4)
         tab2_w = tile([P, T3], I32, "tab2_w")
         nc.sync.dma_start(out=tab2_w[:], in_=tab2_words[0].rearrange("p t i -> p (t i)").bitcast(I32))
         for q in range(QUADS):
@@ -113,12 +115,13 @@ def tile_list_antivenom_panel_scores_kernel(
                 out=tab2_sc[32 * q : 32 * q + 4, :].bitcast(I32),
                 in_=tab2_scales[0, 4 * q : 4 * q + 4, :].bitcast(I32),
             )
-        nc.sync.dma_start(out=page[3][:], in_=page_rows[3])
+        nc.sync.dma_start(out=page[PACK - 1][:], in_=page_rows[PACK - 1])
+        load_wgs(PACK - 1, slice(0, S))
 
         v_sc = tile([P, S], U8, "v_sc")
         nc.vector.tensor_copy(v_sc[:], tab_sc[:].indirect(idx[:]))
         for a in range(1, PASSES):
-            nc.scalar.dma_start(
+            nc.gpsimd.dma_start(
                 out=v_sc_low[0:SHIFT_ROWS, a - 1, :].bitcast(I32),
                 in_=v_sc[4 * a : 4 * a + SHIFT_ROWS, :].bitcast(I32),
             )
@@ -185,6 +188,8 @@ def tile_list_antivenom_panel_scores_kernel(
             floor = tile([P, 2, M], F32, "lod%d" % i, tag="w1_raw%d" % i)
             nc.sync.dma_start(out=floor[:], in_=lod_rows[:, 2 * i : 2 * i + 2, :])
             lod_sb.append(floor)
+        with nc.allow_non_contiguous_dma(reason="one offset for each partition and tile of antibodies"):
+            nc.sync.dma_start(out=aff_sb[:], in_=aff.rearrange("(c p) -> p c", p=P))
 
         h = {}
         page_bf = [tile([P, NB, PACK], BF16, "page_bf%d" % c) for c in range(T2 // NB)]
@@ -204,7 +209,7 @@ def tile_list_antivenom_panel_scores_kernel(
                     first_stage_pass(t + 2, hf, a)
 
         def weights(t):
-            return wgs_first[:] if t == 0 else wgs_rest[:, t - 1, :]
+            return wgs_sb[t][:]
 
         def scatter(t, hf=None):
             if hf is None:
@@ -241,56 +246,60 @@ def tile_list_antivenom_panel_scores_kernel(
 
         round_plane(PACK - 1, 1)
         v2_w = tile([P, S2], U32, "v2_w", tag="h1")
-        v2_s = tile([P, S2], U8, "v2_s", tag="wgs_rest")
+        v2_s = tile([P, S2], U8, "v2_s", tag="wgs3")
         nc.vector.tensor_copy(v2_w[:], tab2_w[:].bitcast(U32).indirect(idx2[:]))
         nc.vector.tensor_copy(v2_s[:], tab2_sc[:].indirect(idx2[:]))
 
         e_tags = ["tab_w0", "tab_w1", "tab_w2", "w1_raw2"]
         e = [tile([P, T2], F32, "e%d" % n, tag=e_tags[n]) for n in range(S2 // P)]
-        page_c, page_s, first = [], [], []
+        page_c = [tile([P, NB], U32, "page_c%d" % c) for c in range(CHUNKS)]
+        page_s = [tile([P, NB], U8, "page_s%d" % c) for c in range(CHUNKS)]
 
-        def scores(n, c):
-            ps = bank((c, 4 + c, 3 - c, 3 - c)[n], "score%d%d" % (n, c))
+        def quantize(c, cols):
+            nc.vector.quantize_mx(
+                out=page_c[c][:, cols].bitcast(FP8X4), scales=page_s[c][:, cols],
+                in_=page_bf[c][:, cols, :].rearrange("p c t -> p (c t)"),
+            )
+
+        def scores(n, c, cols, b):
+            ps = bank(b, "score%d%d%d" % (n, c, cols.start))
             rows = slice(n * P, (n + 1) * P)
             nc.tensor.matmul_mx(
-                out=ps[:], lhsT=v2_w[:, rows].bitcast(FP8X4), lhsT_scale=v2_s[:, rows],
-                rhs=page_c[c][:].bitcast(FP8X4), rhs_scale=page_s[c][:], start=True, stop=True,
+                out=ps[:, cols], lhsT=v2_w[:, rows].bitcast(FP8X4), lhsT_scale=v2_s[:, rows],
+                rhs=page_c[c][:, cols].bitcast(FP8X4), rhs_scale=page_s[c][:, cols], start=True, stop=True,
             )
-            return ps
+            return ps[:, cols]
 
-        def empty(n, c, ps):
-            if n == 0 and c == T2 // NB - 1:
-                nc.vector.tensor_copy(out=e[n][:, half(c)], in_=ps[:])
-            else:
-                nc.scalar.copy(out=e[n][:, half(c)], in_=ps[:])
+        def place(n, c, cols):
+            return e[n][:, c * NB + cols.start : c * NB + cols.stop]
 
-        for c in (0, 2, 3):
-            round_plane(PACK - 1, c)
-        for c in range(T2 // NB):
-            codes = tile([P, NB], U32, "page_c%d" % c)
-            scales = tile([P, NB], U8, "page_s%d" % c)
-            nc.vector.quantize_mx(
-                out=codes[:].bitcast(FP8X4), scales=scales[:], in_=page_bf[c][:].rearrange("p c t -> p (c t)")
-            )
-            page_c.append(codes)
-            page_s.append(scales)
-            first.append(scores(0, c))
-            if c > 0:
-                empty(0, c - 1, first[c - 1])
-        empty(0, T2 // NB - 1, first[-1])
+        full = slice(0, NB)
+        ends = [slice(0, NB // 2), slice(NB // 2, NB)]
+        last_c = CHUNKS - 1
+        round_plane(PACK - 1, 0)
+        round_plane(PACK - 1, 2)
+        for cols in ends:
+            nc.scalar.copy(out=page_bf[last_c][:, cols, PACK - 1], in_=page[PACK - 1][:, half(last_c)][:, cols])
+        for c in range(last_c):
+            quantize(c, full)
+            nc.scalar.copy(out=place(0, c, full), in_=scores(0, c, full, c))
+        tails = []
+        for i, cols in enumerate(ends):
+            quantize(last_c, cols)
+            tails.append(scores(0, last_c, cols, last_c + i))
+        for cols, ps in zip(ends, tails):
+            nc.vector.tensor_copy(out=place(0, last_c, cols), in_=ps)
         for n in range(1, S2 // P):
-            for c in range(T2 // NB):
-                empty(n, c, scores(n, c))
+            for c in range(CHUNKS):
+                b = (5, 6, 7, 0)[c] if n == 1 else 4 - c
+                nc.scalar.copy(out=place(n, c, full), in_=scores(n, c, full, b))
 
         x_tags = ["v_w0", "v_w1", "v_w2", "w1_grouped0"]
         x = [tile([P, M], F32, "x%d" % n, tag=x_tags[n]) for n in range(S2 // P)]
         last = S2 // P - 1
 
-        def pick(n, hf=None):
-            if hf is None:
-                nc.vector.tensor_copy(x[n][:], e[n][:].indirect(idx4[:]))
-            else:
-                nc.vector.tensor_copy(x[n][:, half(hf)], e[n][:].indirect(idx4[:, list_half(hf)]))
+        def pick(n, cols):
+            nc.vector.tensor_copy(x[n][:, cols], e[n][:].indirect(idx4[:, cols.start // 16 : cols.stop // 16]))
 
         def finish(n, cols):
             nc.vector.scalar_tensor_tensor(
@@ -299,13 +308,10 @@ def tile_list_antivenom_panel_scores_kernel(
             )
             nc.sync.dma_start(out=out[n * P : (n + 1) * P, cols], in_=x[n][:, cols])
 
-        whole = slice(0, M)
-        pick(0)
-        for n in range(1, last):
-            pick(n)
-            finish(n - 1, whole)
-        pick(last, 0)
-        finish(last - 1, whole)
-        pick(last, 1)
-        finish(last, half(0))
-        finish(last, half(1))
+        pieces = [(n, slice(0, M)) for n in range(last)]
+        pieces.extend((last, cols) for cols in (slice(0, M // 2), slice(M // 2, 3 * M // 4), slice(3 * M // 4, M)))
+        pick(*pieces[0])
+        for done, ahead in zip(pieces, pieces[1:]):
+            pick(*ahead)
+            finish(*done)
+        finish(*pieces[-1])

@@ -84,13 +84,13 @@ def tile_list_antivenom_panel_scores_kernel(
 
         load_w1(0)
         nc.sync.dma_start(idx[:], offs)
+        nc.sync.dma_start(out=gain_sb[:], in_=gain.rearrange("(p t) -> p t", t=PACK))
+        nc.sync.dma_start(idx3[:], offs3)
         nc.sync.dma_start(out=w2_raw[:].bitcast(I32), in_=w2_words.rearrange("a p n -> p a n").bitcast(I32))
         load_tab(0)
         for a in range(1, PASSES):
             load_w1(a)
             load_tab(a)
-        nc.sync.dma_start(out=gain_sb[:], in_=gain.rearrange("(p t) -> p t", t=PACK))
-        nc.sync.dma_start(idx3[:], offs3)
         page_rows = page0.rearrange("(p t) c -> t p c", t=PACK)
         wgs_rows = wgs.rearrange("(m t) j -> m t j", t=PACK)
         page = [tile([P, T2], F32, "page%d" % t) for t in range(PACK)]
@@ -132,12 +132,12 @@ def tile_list_antivenom_panel_scores_kernel(
         w2_c = tile([P, PASSES, 2 * H], U8, "w2_c")
         w2_s = tile([P, PASSES, H], U8, "w2_s")
         nc.vector.tensor_copy(
-            out=w2_c[:].bitcast(U16).rearrange("p a (t m) -> p a m t", t=PACK),
-            in_=w2_raw[:].bitcast(U16).rearrange("p a (m t) -> p a m t", t=PACK),
+            out=w2_c[:].bitcast(U16).rearrange("p a (t m) -> p a t m", t=PACK),
+            in_=w2_raw[:].bitcast(U16).rearrange("p a (m t) -> p a t m", t=PACK),
         )
         nc.vector.tensor_copy(
-            out=w2_s[:].rearrange("p a (t m) -> p a m t", t=PACK),
-            in_=w2_sc_raw[:].rearrange("p a (m t) -> p a m t", t=PACK),
+            out=w2_s[:].rearrange("p a (t m) -> p a t m", t=PACK),
+            in_=w2_sc_raw[:].rearrange("p a (m t) -> p a t m", t=PACK),
         )
 
         w1_c, w1_s, v_w = [], [], []
@@ -162,8 +162,8 @@ def tile_list_antivenom_panel_scores_kernel(
         for a in range(PASSES):
             grouped = tile([P, H * PACK], BF16, "w1_grouped%d" % a, tag="w1_grouped%d" % (a % 2))
             nc.scalar.copy(
-                out=grouped[:].rearrange("p (t m j) -> p m j t", t=PACK, j=PACK),
-                in_=w1_raw[a][:].rearrange("p j (m t) -> p m j t", t=PACK),
+                out=grouped[:].rearrange("p (t m j) -> p m t j", t=PACK, j=PACK),
+                in_=w1_raw[a][:].rearrange("p j (m t) -> p m t j", t=PACK),
             )
             codes = tile([P, H], U32, "w1_c%d" % a)
             scales = tile([P, H], U8, "w1_s%d" % a)

@@ -56,18 +56,13 @@ def tile_list_antivenom_panel_scores_kernel(
         w2_sc_raw = tile([P, PASSES, H], U8, "w2_sc_raw")
         tab2_sc = tile([P, T3], U8, "tab2_sc")
         v_sc_low = tile([P, PASSES - 1, S], U8, "v_sc_low")
-        nc.vector.memset(tab_sc[:].bitcast(I32), 0)
         nc.vector.memset(w2_sc_raw[:].bitcast(I32), 0)
+        nc.vector.memset(tab_sc[:].bitcast(I32), 0)
         nc.vector.memset(tab2_sc[:].bitcast(I32), 0)
         for q in range(QUADS):
             nc.gpsimd.dma_start(
                 out=tab_sc[32 * q : 32 * q + 4 * PASSES, :].bitcast(I32),
                 in_=tab_scales[:, 4 * q : 4 * q + 4, :].bitcast(I32),
-            )
-        for q in range(QUADS):
-            nc.gpsimd.dma_start(
-                out=w2_sc_raw[32 * q : 32 * q + 4, :, :].bitcast(I32),
-                in_=w2_scales[:, 4 * q : 4 * q + 4, :].rearrange("a r n -> r a n").bitcast(I32),
             )
 
         w1_raw = [tile([P, PACK, H], F32, "w1_raw%d" % a) for a in range(PASSES)]
@@ -82,15 +77,21 @@ def tile_list_antivenom_panel_scores_kernel(
         def load_tab(a):
             nc.sync.dma_start(out=tab_w[a][:], in_=tab_words[a].rearrange("p t i -> p (t i)").bitcast(I32))
 
-        load_w1(0)
         nc.sync.dma_start(idx[:], offs)
+        load_w1(0)
+        load_w1(1)
+        for q in range(QUADS):
+            nc.sync.dma_start(
+                out=w2_sc_raw[32 * q : 32 * q + 4, :, :].bitcast(I32),
+                in_=w2_scales[:, 4 * q : 4 * q + 4, :].rearrange("a r n -> r a n").bitcast(I32),
+            )
+        load_tab(0)
+        nc.sync.dma_start(out=w2_raw[:].bitcast(I32), in_=w2_words.rearrange("a p n -> p a n").bitcast(I32))
         nc.sync.dma_start(out=gain_sb[:], in_=gain.rearrange("(p t) -> p t", t=PACK))
         nc.sync.dma_start(idx3[:], offs3)
-        nc.sync.dma_start(out=w2_raw[:].bitcast(I32), in_=w2_words.rearrange("a p n -> p a n").bitcast(I32))
-        load_tab(0)
-        for a in range(1, PASSES):
-            load_w1(a)
-            load_tab(a)
+        load_tab(1)
+        load_w1(2)
+        load_tab(2)
         page_rows = page0.rearrange("(p t) c -> t p c", t=PACK)
         wgs_rows = wgs.rearrange("(m t) j -> m t j", t=PACK)
         page = [tile([P, T2], F32, "page%d" % t) for t in range(PACK)]

@@ -195,6 +195,8 @@ def tile_list_antivenom_panel_scores_kernel(
         h = {}
         page_bf = [tile([P, NB, PACK], BF16, "page_bf%d" % c) for c in range(T2 // NB)]
 
+        staged = tile([P, PACK, NB], BF16, "staged")
+
         def make_h(t, hf):
             if hf == 0:
                 h[t] = tile([P, S], F32, "h%d" % t, tag="h%d" % (t % 2))
@@ -221,12 +223,13 @@ def tile_list_antivenom_panel_scores_kernel(
                 )
 
         def round_plane(t, c):
-            if t == PACK - 1 and c == 1:
-                nc.vector.tensor_copy(out=page_bf[c][:, :, t], in_=page[t][:, half(c)])
-            elif t == PACK - 2 and c == 1:
-                nc.scalar.copy(
-                    out=page_bf[c][:, :, t : t + 2], in_=page[t][:, half(c)].unsqueeze(2).to_broadcast([P, NB, 2])
-                )
+            if c == 1:
+                nc.scalar.copy(out=staged[:, t, :], in_=page[t][:, half(c)])
+                if t == PACK - 1:
+                    nc.vector.tensor_copy(
+                        out=page_bf[c][:].rearrange("p (c i) t -> p c t i", i=PACK),
+                        in_=staged[:].rearrange("p t (c i) -> p c t i", i=PACK),
+                    )
             else:
                 nc.scalar.copy(out=page_bf[c][:, :, t], in_=page[t][:, half(c)])
 
@@ -245,7 +248,6 @@ def tile_list_antivenom_panel_scores_kernel(
             for c in range(T2 // NB):
                 round_plane(t - 1, c)
 
-        round_plane(PACK - 1, 1)
         v2_w = tile([P, S2], U32, "v2_w", tag="h1")
         v2_s = tile([P, S2], U8, "v2_s", tag="wgs3")
         nc.vector.tensor_copy(v2_w[:], tab2_w[:].bitcast(U32).indirect(idx2[:]))
@@ -277,6 +279,7 @@ def tile_list_antivenom_panel_scores_kernel(
         full = slice(0, NB)
         ends = [slice(0, NB // 2), slice(NB // 2, NB)]
         last_c = CHUNKS - 1
+        round_plane(PACK - 1, 1)
         round_plane(PACK - 1, 0)
         round_plane(PACK - 1, 2)
         for cols in ends:

@@ -23,6 +23,8 @@ NB = 512
 QUADS = 4
 CHUNKS = T2 // NB
 SHIFT_ROWS = 112
+FIRST = 320
+WOVEN = 640
 
 
 def tile_list_antivenom_panel_scores_kernel(
@@ -33,6 +35,7 @@ def tile_list_antivenom_panel_scores_kernel(
     with ExitStack() as ctx:
         lists = ctx.enter_context(tc.tile_pool(name="lists", bufs=1))
         sb = ctx.enter_context(tc.tile_pool(name="sb", bufs=1))
+        late = ctx.enter_context(tc.tile_pool(name="late", bufs=1))
         psum = ctx.enter_context(tc.psum_pool(name="psum", bufs=1))
 
         def tile(shape, dtype, name, tag=None):
@@ -102,8 +105,8 @@ def tile_list_antivenom_panel_scores_kernel(
                 nc.sync.dma_start(out=wgs_sb[t][32 * q : 32 * q + 32, cols], in_=wgs_rows[:, t, cols])
 
         nc.sync.dma_start(out=page[0][:], in_=page_rows[0])
-        load_wgs(0, half(0))
-        load_wgs(0, half(1))
+        load_wgs(0, slice(0, FIRST))
+        load_wgs(0, slice(FIRST, S))
         for t in range(1, PACK - 1):
             nc.sync.dma_start(out=page[t][:], in_=page_rows[t])
             load_wgs(t, slice(0, S))
@@ -193,9 +196,10 @@ def tile_list_antivenom_panel_scores_kernel(
             nc.sync.dma_start(out=aff_sb[:], in_=aff.rearrange("(c p) -> p c", p=P))
 
         h = {}
-        page_bf = [tile([P, NB, PACK], BF16, "page_bf%d" % c) for c in range(T2 // NB)]
+        page_bf = [tile([P, NB, PACK], BF16, "page_bf%d" % c) for c in range(T2 // NB - 1)]
+        page_bf.append(late.tile([P, NB, PACK], BF16, name="page_bf_last", align_bytes=64, offset=0))
 
-        staged = tile([P, PACK, NB], BF16, "staged")
+        staged = tile([P, PACK, WOVEN], BF16, "staged")
 
         def make_h(t, hf):
             if hf == 0:
@@ -214,44 +218,50 @@ def tile_list_antivenom_panel_scores_kernel(
         def weights(t):
             return wgs_sb[t][:]
 
-        def scatter(t, hf=None):
-            if hf is None:
-                nc.vector.tensor_tensor(page[t][:].indirect(idx3[:]), h[t][:], weights(t), ALU.mult)
-            else:
-                nc.vector.tensor_tensor(
-                    page[t][:].indirect(idx3[:, list_half(hf)]), h[t][:, half(hf)], weights(t)[:, half(hf)], ALU.mult
-                )
+        def scatter(t, cols):
+            nc.vector.tensor_tensor(
+                page[t][:].indirect(idx3[:, cols.start // 16 : cols.stop // 16]), h[t][:, cols], weights(t)[:, cols], ALU.mult
+            )
+
+        extra = WOVEN - NB
 
         def round_plane(t, c):
             if c == 1:
-                nc.scalar.copy(out=staged[:, t, :], in_=page[t][:, half(c)])
+                nc.scalar.copy(out=staged[:, t, :], in_=page[t][:, NB : NB + WOVEN])
                 if t == PACK - 1:
-                    nc.vector.tensor_copy(
-                        out=page_bf[c][:].rearrange("p (c i) t -> p c t i", i=PACK),
-                        in_=staged[:].rearrange("p t (c i) -> p c t i", i=PACK),
-                    )
+                    for dst, src in ((page_bf[1][:], staged[:, :, 0:NB]), (page_bf[2][:, 0:extra, :], staged[:, :, NB:WOVEN])):
+                        nc.vector.tensor_copy(
+                            out=dst.rearrange("p (c i) t -> p c t i", i=PACK),
+                            in_=src.rearrange("p t (c i) -> p c t i", i=PACK),
+                        )
+            elif c == 2:
+                nc.scalar.copy(out=page_bf[c][:, extra:NB, t], in_=page[t][:, NB + WOVEN : 3 * NB])
             else:
                 nc.scalar.copy(out=page_bf[c][:, :, t], in_=page[t][:, half(c)])
 
         make_h(0, 0)
-        scatter(0, 0)
+        scatter(0, slice(0, FIRST))
         make_h(0, 1)
         make_h(1, 0)
-        scatter(0, 1)
+        scatter(0, slice(FIRST, S))
         make_h(1, 1)
         for t in range(1, PACK):
             if t + 1 < PACK:
                 make_h(t + 1, 0)
-            scatter(t)
+            scatter(t, slice(0, S))
             if t + 1 < PACK:
                 make_h(t + 1, 1)
             for c in range(T2 // NB):
                 round_plane(t - 1, c)
 
-        v2_w = tile([P, S2], U32, "v2_w", tag="h1")
-        v2_s = tile([P, S2], U8, "v2_s", tag="wgs3")
-        nc.vector.tensor_copy(v2_w[:], tab2_w[:].bitcast(U32).indirect(idx2[:]))
-        nc.vector.tensor_copy(v2_s[:], tab2_sc[:].indirect(idx2[:]))
+        v2_w = [tile([P, S2 // 2], U32, "v2_w0", tag="h1"), late.tile([P, S2 // 2], U32, name="v2_w1", align_bytes=64, offset=0)]
+        v2_s = [tile([P, S2 // 2], U8, "v2_s0", tag="wgs3"), late.tile([P, S2 // 2], U8, name="v2_s1", align_bytes=64, offset=2 * S2)]
+
+        def pick_antibodies(i):
+            nc.vector.tensor_copy(v2_w[i][:], tab2_w[:].bitcast(U32).indirect(idx2[:, 16 * i : 16 * (i + 1)]))
+            nc.vector.tensor_copy(v2_s[i][:], tab2_sc[:].indirect(idx2[:, 16 * i : 16 * (i + 1)]))
+
+        pick_antibodies(0)
 
         e_tags = ["tab_w0", "tab_w1", "tab_w2", "w1_raw2"]
         e = [tile([P, T2], F32, "e%d" % n, tag=e_tags[n]) for n in range(S2 // P)]
@@ -266,9 +276,9 @@ def tile_list_antivenom_panel_scores_kernel(
 
         def scores(n, c, cols, b):
             ps = bank(b, "score%d%d%d" % (n, c, cols.start))
-            rows = slice(n * P, (n + 1) * P)
+            rows = slice((n % 2) * P, (n % 2 + 1) * P)
             nc.tensor.matmul_mx(
-                out=ps[:, cols], lhsT=v2_w[:, rows].bitcast(FP8X4), lhsT_scale=v2_s[:, rows],
+                out=ps[:, cols], lhsT=v2_w[n // 2][:, rows].bitcast(FP8X4), lhsT_scale=v2_s[n // 2][:, rows],
                 rhs=page_c[c][:, cols].bitcast(FP8X4), rhs_scale=page_s[c][:, cols], start=True, stop=True,
             )
             return ps[:, cols]
@@ -291,8 +301,9 @@ def tile_list_antivenom_panel_scores_kernel(
         for i, cols in enumerate(ends):
             quantize(last_c, cols)
             tails.append(scores(0, last_c, cols, last_c + i))
-        for cols, ps in zip(ends, tails):
-            nc.vector.tensor_copy(out=place(0, last_c, cols), in_=ps)
+        pick_antibodies(1)
+        nc.scalar.copy(out=place(0, last_c, ends[0]), in_=tails[0])
+        nc.vector.tensor_copy(out=place(0, last_c, ends[1]), in_=tails[1])
         for n in range(1, S2 // P):
             for c in range(CHUNKS):
                 b = (5, 6, 7, 0)[c] if n == 1 else 4 - c

@@ -24,7 +24,7 @@ QUADS = 4
 CHUNKS = T2 // NB
 SHIFT_ROWS = 112
 FIRST = 320
-WOVEN = 640
+WOVEN = 768
 
 
 def tile_list_antivenom_panel_scores_kernel(
@@ -59,13 +59,18 @@ def tile_list_antivenom_panel_scores_kernel(
         w2_sc_raw = tile([P, PASSES, H], U8, "w2_sc_raw")
         tab2_sc = tile([P, T3], U8, "tab2_sc")
         v_sc_low = tile([P, PASSES - 1, S], U8, "v_sc_low")
-        nc.vector.memset(w2_sc_raw[:].bitcast(I32), 0)
         nc.vector.memset(tab_sc[:].bitcast(I32), 0)
+        nc.vector.memset(w2_sc_raw[:].bitcast(I32), 0)
         nc.vector.memset(tab2_sc[:].bitcast(I32), 0)
         for q in range(QUADS):
             nc.gpsimd.dma_start(
                 out=tab_sc[32 * q : 32 * q + 4 * PASSES, :].bitcast(I32),
                 in_=tab_scales[:, 4 * q : 4 * q + 4, :].bitcast(I32),
+            )
+        for q in range(QUADS):
+            nc.gpsimd.dma_start(
+                out=tab2_sc[32 * q : 32 * q + 4, :].bitcast(I32),
+                in_=tab2_scales[0, 4 * q : 4 * q + 4, :].bitcast(I32),
             )
 
         w1_raw = [tile([P, PACK, H], F32, "w1_raw%d" % a) for a in range(PASSES)]
@@ -81,17 +86,18 @@ def tile_list_antivenom_panel_scores_kernel(
             nc.sync.dma_start(out=tab_w[a][:], in_=tab_words[a].rearrange("p t i -> p (t i)").bitcast(I32))
 
         nc.sync.dma_start(idx[:], offs)
+        nc.sync.dma_start(out=w2_raw[:].bitcast(I32), in_=w2_words.rearrange("a p n -> p a n").bitcast(I32))
         load_w1(0)
-        load_w1(1)
         for q in range(QUADS):
             nc.sync.dma_start(
                 out=w2_sc_raw[32 * q : 32 * q + 4, :, :].bitcast(I32),
                 in_=w2_scales[:, 4 * q : 4 * q + 4, :].rearrange("a r n -> r a n").bitcast(I32),
             )
-        load_tab(0)
-        nc.sync.dma_start(out=w2_raw[:].bitcast(I32), in_=w2_words.rearrange("a p n -> p a n").bitcast(I32))
+        load_w1(1)
         nc.sync.dma_start(out=gain_sb[:], in_=gain.rearrange("(p t) -> p t", t=PACK))
         nc.sync.dma_start(idx3[:], offs3)
+        nc.sync.dma_start(idx2[:], offs2)
+        load_tab(0)
         load_tab(1)
         load_w1(2)
         load_tab(2)
@@ -110,28 +116,11 @@ def tile_list_antivenom_panel_scores_kernel(
         for t in range(1, PACK - 1):
             nc.sync.dma_start(out=page[t][:], in_=page_rows[t])
             load_wgs(t, slice(0, S))
-        nc.sync.dma_start(idx2[:], offs2)
         nc.sync.dma_start(idx4[:], offs4)
         tab2_w = tile([P, T3], I32, "tab2_w")
         nc.sync.dma_start(out=tab2_w[:], in_=tab2_words[0].rearrange("p t i -> p (t i)").bitcast(I32))
-        for q in range(QUADS):
-            nc.sync.dma_start(
-                out=tab2_sc[32 * q : 32 * q + 4, :].bitcast(I32),
-                in_=tab2_scales[0, 4 * q : 4 * q + 4, :].bitcast(I32),
-            )
         nc.sync.dma_start(out=page[PACK - 1][:], in_=page_rows[PACK - 1])
         load_wgs(PACK - 1, slice(0, S))
-
-        v_sc = tile([P, S], U8, "v_sc")
-        nc.vector.tensor_copy(v_sc[:], tab_sc[:].indirect(idx[:]))
-        for a in range(1, PASSES):
-            nc.gpsimd.dma_start(
-                out=v_sc_low[0:SHIFT_ROWS, a - 1, :].bitcast(I32),
-                in_=v_sc[4 * a : 4 * a + SHIFT_ROWS, :].bitcast(I32),
-            )
-
-        def v_plane(a, cols):
-            return v_sc[:, cols] if a == 0 else v_sc_low[:, a - 1, cols]
 
         w2_c = tile([P, PASSES, 2 * H], U8, "w2_c")
         w2_s = tile([P, PASSES, H], U8, "w2_s")
@@ -143,6 +132,17 @@ def tile_list_antivenom_panel_scores_kernel(
             out=w2_s[:].rearrange("p a (t m) -> p a t m", t=PACK),
             in_=w2_sc_raw[:].rearrange("p a (m t) -> p a t m", t=PACK),
         )
+
+        v_sc = tile([P, S], U8, "v_sc")
+        nc.vector.tensor_copy(v_sc[:], tab_sc[:].indirect(idx[:]))
+        for a in range(1, PASSES):
+            nc.gpsimd.dma_start(
+                out=v_sc_low[0:SHIFT_ROWS, a - 1, :].bitcast(I32),
+                in_=v_sc[4 * a : 4 * a + SHIFT_ROWS, :].bitcast(I32),
+            )
+
+        def v_plane(a, cols):
+            return v_sc[:, cols] if a == 0 else v_sc_low[:, a - 1, cols]
 
         w1_c, w1_s, v_w = [], [], []
         acc = {}
@@ -163,7 +163,10 @@ def tile_list_antivenom_panel_scores_kernel(
                 rhs=moving, rhs_scale=v_plane(a, half(hf)), start=(a == 0), stop=(a == PASSES - 1),
             )
 
+        v2_s = tile([P, S2], U8, "v2_s")
         for a in range(PASSES):
+            if a == 1:
+                nc.vector.tensor_copy(v2_s[:], tab2_sc[:].indirect(idx2[:]))
             grouped = tile([P, H * PACK], BF16, "w1_grouped%d" % a, tag="w1_grouped%d" % (a % 2))
             nc.scalar.copy(
                 out=grouped[:].rearrange("p (t m j) -> p m t j", t=PACK, j=PACK),
@@ -255,11 +258,9 @@ def tile_list_antivenom_panel_scores_kernel(
                 round_plane(t - 1, c)
 
         v2_w = [tile([P, S2 // 2], U32, "v2_w0", tag="h1"), late.tile([P, S2 // 2], U32, name="v2_w1", align_bytes=64, offset=0)]
-        v2_s = [tile([P, S2 // 2], U8, "v2_s0", tag="wgs3"), late.tile([P, S2 // 2], U8, name="v2_s1", align_bytes=64, offset=2 * S2)]
 
         def pick_antibodies(i):
             nc.vector.tensor_copy(v2_w[i][:], tab2_w[:].bitcast(U32).indirect(idx2[:, 16 * i : 16 * (i + 1)]))
-            nc.vector.tensor_copy(v2_s[i][:], tab2_sc[:].indirect(idx2[:, 16 * i : 16 * (i + 1)]))
 
         pick_antibodies(0)
 
@@ -278,7 +279,7 @@ def tile_list_antivenom_panel_scores_kernel(
             ps = bank(b, "score%d%d%d" % (n, c, cols.start))
             rows = slice((n % 2) * P, (n % 2 + 1) * P)
             nc.tensor.matmul_mx(
-                out=ps[:, cols], lhsT=v2_w[n // 2][:, rows].bitcast(FP8X4), lhsT_scale=v2_s[n // 2][:, rows],
+                out=ps[:, cols], lhsT=v2_w[n // 2][:, rows].bitcast(FP8X4), lhsT_scale=v2_s[:, n * P : (n + 1) * P],
                 rhs=page_c[c][:, cols].bitcast(FP8X4), rhs_scale=page_s[c][:, cols], start=True, stop=True,
             )
             return ps[:, cols]
@@ -302,7 +303,7 @@ def tile_list_antivenom_panel_scores_kernel(
             quantize(last_c, cols)
             tails.append(scores(0, last_c, cols, last_c + i))
         pick_antibodies(1)
-        nc.scalar.copy(out=place(0, last_c, ends[0]), in_=tails[0])
+        nc.vector.tensor_copy(out=place(0, last_c, ends[0]), in_=tails[0])
         nc.vector.tensor_copy(out=place(0, last_c, ends[1]), in_=tails[1])
         for n in range(1, S2 // P):
             for c in range(CHUNKS):

@@ -23,8 +23,8 @@ NB = 512
 QUADS = 4
 CHUNKS = T2 // NB
 SHIFT_ROWS = 112
-FIRST = 320
-WOVEN = 768
+FIRST = 256
+WOVEN = 640
 
 
 def tile_list_antivenom_panel_scores_kernel(
@@ -35,7 +35,6 @@ def tile_list_antivenom_panel_scores_kernel(
     with ExitStack() as ctx:
         lists = ctx.enter_context(tc.tile_pool(name="lists", bufs=1))
         sb = ctx.enter_context(tc.tile_pool(name="sb", bufs=1))
-        late = ctx.enter_context(tc.tile_pool(name="late", bufs=1))
         psum = ctx.enter_context(tc.psum_pool(name="psum", bufs=1))
 
         def tile(shape, dtype, name, tag=None):
@@ -116,11 +115,11 @@ def tile_list_antivenom_panel_scores_kernel(
         for t in range(1, PACK - 1):
             nc.sync.dma_start(out=page[t][:], in_=page_rows[t])
             load_wgs(t, slice(0, S))
-        nc.sync.dma_start(idx4[:], offs4)
-        tab2_w = tile([P, T3], I32, "tab2_w")
-        nc.sync.dma_start(out=tab2_w[:], in_=tab2_words[0].rearrange("p t i -> p (t i)").bitcast(I32))
         nc.sync.dma_start(out=page[PACK - 1][:], in_=page_rows[PACK - 1])
         load_wgs(PACK - 1, slice(0, S))
+        tab2_w = tile([P, T3], I32, "tab2_w")
+        nc.sync.dma_start(out=tab2_w[:], in_=tab2_words[0].rearrange("p t i -> p (t i)").bitcast(I32))
+        nc.sync.dma_start(idx4[:], offs4)
 
         w2_c = tile([P, PASSES, 2 * H], U8, "w2_c")
         w2_s = tile([P, PASSES, H], U8, "w2_s")
@@ -199,8 +198,7 @@ def tile_list_antivenom_panel_scores_kernel(
             nc.sync.dma_start(out=aff_sb[:], in_=aff.rearrange("(c p) -> p c", p=P))
 
         h = {}
-        page_bf = [tile([P, NB, PACK], BF16, "page_bf%d" % c) for c in range(T2 // NB - 1)]
-        page_bf.append(late.tile([P, NB, PACK], BF16, name="page_bf_last", align_bytes=64, offset=0))
+        page_bf = [tile([P, NB, PACK], BF16, "page_bf%d" % c) if c != 1 else None for c in range(T2 // NB)]
 
         staged = tile([P, PACK, WOVEN], BF16, "staged")
 
@@ -209,11 +207,13 @@ def tile_list_antivenom_panel_scores_kernel(
                 h[t] = tile([P, S], F32, "h%d" % t, tag="h%d" % (t % 2))
             acc_a, acc_b = acc[t, hf]
             act = tile([P, NB], F32, "silu%d%d" % (t, hf), tag="silu%d%d" % (t % 2, hf))
-            nc.scalar.activation(out=act[:], in_=acc_a[:], func=ACT.Silu)
-            nc.vector.scalar_tensor_tensor(
-                out=h[t][:, half(hf)], in0=act[:], scalar=gain_sb[:, t : t + 1], in1=acc_b[:],
-                op0=ALU.mult, op1=ALU.add,
-            )
+            cuts = (0, FIRST, NB) if (t, hf) == (0, 0) else (0, NB)
+            for lo, hi in zip(cuts, cuts[1:]):
+                nc.scalar.activation(out=act[:, lo:hi], in_=acc_a[:, lo:hi], func=ACT.Silu)
+                nc.vector.scalar_tensor_tensor(
+                    out=h[t][:, hf * NB + lo : hf * NB + hi], in0=act[:, lo:hi], scalar=gain_sb[:, t : t + 1],
+                    in1=acc_b[:, lo:hi], op0=ALU.mult, op1=ALU.add,
+                )
             if t + 2 < PACK:
                 for a in range(PASSES):
                     first_stage_pass(t + 2, hf, a)
@@ -257,12 +257,9 @@ def tile_list_antivenom_panel_scores_kernel(
             for c in range(T2 // NB):
                 round_plane(t - 1, c)
 
-        v2_w = [tile([P, S2 // 2], U32, "v2_w0", tag="h1"), late.tile([P, S2 // 2], U32, name="v2_w1", align_bytes=64, offset=0)]
-
-        def pick_antibodies(i):
-            nc.vector.tensor_copy(v2_w[i][:], tab2_w[:].bitcast(U32).indirect(idx2[:, 16 * i : 16 * (i + 1)]))
-
-        pick_antibodies(0)
+        v2_w = tile([P, S2], U32, "v2_w", tag="h1")
+        nc.vector.tensor_copy(v2_w[:], tab2_w[:].bitcast(U32).indirect(idx2[:]))
+        page_bf[1] = tile([P, NB, PACK], BF16, "page_bf1", tag="tab2_w")
 
         e_tags = ["tab_w0", "tab_w1", "tab_w2", "w1_raw2"]
         e = [tile([P, T2], F32, "e%d" % n, tag=e_tags[n]) for n in range(S2 // P)]
@@ -277,9 +274,9 @@ def tile_list_antivenom_panel_scores_kernel(
 
         def scores(n, c, cols, b):
             ps = bank(b, "score%d%d%d" % (n, c, cols.start))
-            rows = slice((n % 2) * P, (n % 2 + 1) * P)
+            rows = slice(n * P, (n + 1) * P)
             nc.tensor.matmul_mx(
-                out=ps[:, cols], lhsT=v2_w[n // 2][:, rows].bitcast(FP8X4), lhsT_scale=v2_s[:, n * P : (n + 1) * P],
+                out=ps[:, cols], lhsT=v2_w[:, rows].bitcast(FP8X4), lhsT_scale=v2_s[:, n * P : (n + 1) * P],
                 rhs=page_c[c][:, cols].bitcast(FP8X4), rhs_scale=page_s[c][:, cols], start=True, stop=True,
             )
             return ps[:, cols]
@@ -302,7 +299,6 @@ def tile_list_antivenom_panel_scores_kernel(
         for i, cols in enumerate(ends):
             quantize(last_c, cols)
             tails.append(scores(0, last_c, cols, last_c + i))
-        pick_antibodies(1)
         nc.vector.tensor_copy(out=place(0, last_c, ends[0]), in_=tails[0])
         nc.vector.tensor_copy(out=place(0, last_c, ends[1]), in_=tails[1])
         for n in range(1, S2 // P):

@@ -24,7 +24,9 @@ QUADS = 4
 CHUNKS = T2 // NB
 SHIFT_ROWS = 112
 FIRST = 256
-WOVEN = 640
+AB_ROW = 12
+PIECES = ((0, 512), (512, 1280), (1280, 1536), (1536, 1792), (1792, 2048))
+PAIRED = 2
 
 
 def tile_list_antivenom_panel_scores_kernel(
@@ -68,7 +70,7 @@ def tile_list_antivenom_panel_scores_kernel(
             )
         for q in range(QUADS):
             nc.gpsimd.dma_start(
-                out=tab2_sc[32 * q : 32 * q + 4, :].bitcast(I32),
+                out=tab2_sc[32 * q + AB_ROW : 32 * q + AB_ROW + 4, :].bitcast(I32),
                 in_=tab2_scales[0, 4 * q : 4 * q + 4, :].bitcast(I32),
             )
 
@@ -198,9 +200,8 @@ def tile_list_antivenom_panel_scores_kernel(
             nc.sync.dma_start(out=aff_sb[:], in_=aff.rearrange("(c p) -> p c", p=P))
 
         h = {}
-        page_bf = [tile([P, NB, PACK], BF16, "page_bf%d" % c) if c != 1 else None for c in range(T2 // NB)]
-
-        staged = tile([P, PACK, WOVEN], BF16, "staged")
+        page_bf = [tile([P, hi - lo, PACK], BF16, "page_bf%d" % i) if i != 1 else None for i, (lo, hi) in enumerate(PIECES)]
+        pairs = [tile([P, 2, hi - lo, 2], BF16, "pairs%d" % i) for i, (lo, hi) in enumerate(PIECES[:PAIRED])]
 
         def make_h(t, hf):
             if hf == 0:
@@ -226,21 +227,16 @@ def tile_list_antivenom_panel_scores_kernel(
                 page[t][:].indirect(idx3[:, cols.start // 16 : cols.stop // 16]), h[t][:, cols], weights(t)[:, cols], ALU.mult
             )
 
-        extra = WOVEN - NB
+        def round_plane(t):
+            for i, (lo, hi) in enumerate(PIECES):
+                dst = pairs[i][:, t // 2, :, t % 2] if i < PAIRED else page_bf[i][:, :, t]
+                nc.scalar.copy(out=dst, in_=page[t][:, lo:hi])
 
-        def round_plane(t, c):
-            if c == 1:
-                nc.scalar.copy(out=staged[:, t, :], in_=page[t][:, NB : NB + WOVEN])
-                if t == PACK - 1:
-                    for dst, src in ((page_bf[1][:], staged[:, :, 0:NB]), (page_bf[2][:, 0:extra, :], staged[:, :, NB:WOVEN])):
-                        nc.vector.tensor_copy(
-                            out=dst.rearrange("p (c i) t -> p c t i", i=PACK),
-                            in_=src.rearrange("p t (c i) -> p c t i", i=PACK),
-                        )
-            elif c == 2:
-                nc.scalar.copy(out=page_bf[c][:, extra:NB, t], in_=page[t][:, NB + WOVEN : 3 * NB])
-            else:
-                nc.scalar.copy(out=page_bf[c][:, :, t], in_=page[t][:, half(c)])
+        def weave(i):
+            nc.vector.tensor_copy(
+                out=page_bf[i][:].rearrange("p c t -> p (c t)").bitcast(I32).rearrange("p (c u) -> p c u", u=2),
+                in_=pairs[i][:].rearrange("p u c e -> p u (c e)").bitcast(I32).rearrange("p u c -> p c u"),
+            )
 
         make_h(0, 0)
         scatter(0, slice(0, FIRST))
@@ -251,32 +247,40 @@ def tile_list_antivenom_panel_scores_kernel(
         for t in range(1, PACK):
             if t + 1 < PACK:
                 make_h(t + 1, 0)
-            scatter(t, slice(0, S))
-            if t + 1 < PACK:
+            if t + 2 == PACK:
                 make_h(t + 1, 1)
-            for c in range(T2 // NB):
-                round_plane(t - 1, c)
+            scatter(t, slice(0, S))
+            if t + 2 < PACK:
+                make_h(t + 1, 1)
+            round_plane(t - 1)
 
-        v2_w = tile([P, S2], U32, "v2_w", tag="h1")
-        nc.vector.tensor_copy(v2_w[:], tab2_w[:].bitcast(U32).indirect(idx2[:]))
-        page_bf[1] = tile([P, NB, PACK], BF16, "page_bf1", tag="tab2_w")
+        v2_w = []
+
+        def gather_antibodies(i, tag):
+            picked = tile([P, S2 // 2], U32, "v2_w%d" % i, tag=tag)
+            nc.vector.tensor_copy(picked[:], tab2_w[:].bitcast(U32).indirect(idx2[:, i * S2 // 32 : (i + 1) * S2 // 32]))
+            v2_w.append(picked)
+
+        gather_antibodies(0, "h0")
 
         e_tags = ["tab_w0", "tab_w1", "tab_w2", "w1_raw2"]
         e = [tile([P, T2], F32, "e%d" % n, tag=e_tags[n]) for n in range(S2 // P)]
         page_c = [tile([P, NB], U32, "page_c%d" % c) for c in range(CHUNKS)]
         page_s = [tile([P, NB], U8, "page_s%d" % c) for c in range(CHUNKS)]
 
-        def quantize(c, cols):
+        def quantize(i, lo, hi):
+            c, cols = lo // NB, slice(lo % NB, lo % NB + hi - lo)
             nc.vector.quantize_mx(
                 out=page_c[c][:, cols].bitcast(FP8X4), scales=page_s[c][:, cols],
-                in_=page_bf[c][:, cols, :].rearrange("p c t -> p (c t)"),
+                in_=page_bf[i][:, lo - PIECES[i][0] : hi - PIECES[i][0], :].rearrange("p c t -> p (c t)"),
             )
 
-        def scores(n, c, cols, b):
-            ps = bank(b, "score%d%d%d" % (n, c, cols.start))
-            rows = slice(n * P, (n + 1) * P)
+        def scores(n, c, cols, b, ps=None):
+            if ps is None:
+                ps = bank(b, "score%d%d%d" % (n, c, cols.start))
+            rows = slice(n % 2 * P, (n % 2 + 1) * P)
             nc.tensor.matmul_mx(
-                out=ps[:, cols], lhsT=v2_w[:, rows].bitcast(FP8X4), lhsT_scale=v2_s[:, n * P : (n + 1) * P],
+                out=ps[:, cols], lhsT=v2_w[n // 2][:, rows].bitcast(FP8X4), lhsT_scale=v2_s[AB_ROW:P, n * P : (n + 1) * P],
                 rhs=page_c[c][:, cols].bitcast(FP8X4), rhs_scale=page_s[c][:, cols], start=True, stop=True,
             )
             return ps[:, cols]
@@ -287,23 +291,28 @@ def tile_list_antivenom_panel_scores_kernel(
         full = slice(0, NB)
         ends = [slice(0, NB // 2), slice(NB // 2, NB)]
         last_c = CHUNKS - 1
-        round_plane(PACK - 1, 1)
-        round_plane(PACK - 1, 0)
-        round_plane(PACK - 1, 2)
-        for cols in ends:
-            nc.scalar.copy(out=page_bf[last_c][:, cols, PACK - 1], in_=page[PACK - 1][:, half(last_c)][:, cols])
-        for c in range(last_c):
-            quantize(c, full)
-            nc.scalar.copy(out=place(0, c, full), in_=scores(0, c, full, c))
-        tails = []
+        round_plane(PACK - 1)
+        weave(0)
+        quantize(0, 0, 512)
+        page_bf[1] = tile([P, PIECES[1][1] - PIECES[1][0], PACK], BF16, "page_bf1", tag="pairs0")
+        weave(1)
+        quantize(2, 1280, 1536)
+        quantize(1, 512, 1024)
+        quantize(1, 1024, 1280)
+        quantize(3, 1536, 1792)
+        quantize(4, 1792, 2048)
+        gather_antibodies(1, "page_bf3")
+        third = bank(2, "score02")
+        nc.scalar.copy(out=place(0, 0, full), in_=scores(0, 0, full, 0))
+        scores(0, 2, ends[1], 2, third)
+        nc.scalar.copy(out=place(0, 1, full), in_=scores(0, 1, full, 1))
+        scores(0, 2, ends[0], 2, third)
+        nc.scalar.copy(out=place(0, 2, full), in_=third[:])
         for i, cols in enumerate(ends):
-            quantize(last_c, cols)
-            tails.append(scores(0, last_c, cols, last_c + i))
-        nc.vector.tensor_copy(out=place(0, last_c, ends[0]), in_=tails[0])
-        nc.vector.tensor_copy(out=place(0, last_c, ends[1]), in_=tails[1])
+            nc.vector.tensor_copy(out=place(0, last_c, cols), in_=scores(0, last_c, cols, last_c + i))
         for n in range(1, S2 // P):
             for c in range(CHUNKS):
-                b = (5, 6, 7, 0)[c] if n == 1 else 4 - c
+                b = (5, 3, 4, 6)[c] if n == 1 else (7, 0, 1, 2)[c]
                 nc.scalar.copy(out=place(n, c, full), in_=scores(n, c, full, b))
 
         x_tags = ["v_w0", "v_w1", "v_w2", "w1_grouped0"]

@@ -22,7 +22,7 @@ PASSES = K // (P * PACK)
 NB = 512
 QUADS = 4
 CHUNKS = T2 // NB
-SHIFT_ROWS = 112
+SHIFT_ROWS = 100
 FIRST = 256
 AB_ROW = 12
 PIECES = ((0, 512), (512, 1280), (1280, 1536), (1536, 1792), (1792, 2048))
@@ -89,10 +89,10 @@ def tile_list_antivenom_panel_scores_kernel(
         nc.sync.dma_start(idx[:], offs)
         nc.sync.dma_start(out=w2_raw[:].bitcast(I32), in_=w2_words.rearrange("a p n -> p a n").bitcast(I32))
         load_w1(0)
-        for q in range(QUADS):
+        for r in range(4):
             nc.sync.dma_start(
-                out=w2_sc_raw[32 * q : 32 * q + 4, :, :].bitcast(I32),
-                in_=w2_scales[:, 4 * q : 4 * q + 4, :].rearrange("a r n -> r a n").bitcast(I32),
+                out=w2_sc_raw[r:P:32, :, :].bitcast(I32),
+                in_=w2_scales.rearrange("a (q r) n -> r q a n", r=4)[r].bitcast(I32),
             )
         load_w1(1)
         nc.sync.dma_start(out=gain_sb[:], in_=gain.rearrange("(p t) -> p t", t=PACK))

@@ -1,6 +1,7 @@
 from contextlib import ExitStack
 
 import concourse.mybir as mybir
+from concourse.masks import make_identity
 
 K, H, T, S, T2, S2, T3, M = 1536, 512, 4096, 1024, 2048, 512, 2048, 1024
 FLOPS = 2 * (2 * K * H * S + H * S2 * T2)
@@ -219,6 +220,42 @@ def tile_list_antivenom_panel_scores_kernel(
                 for a in range(PASSES):
                     first_stage_pass(t + 2, hf, a)
 
+        ident = tile([P, P], F32, "ident", tag="tab2_sc")
+        make_identity(nc, ident[:])
+        turned = {}
+
+        def blocks():
+            return [slice(i * P, (i + 1) * P) for i in range(NB // P)]
+
+        def sum_turned(t, hf):
+            acc_a, acc_b = acc[t, hf]
+            base = (t % 2) * 4 + hf * 2
+            act = tile([P, NB], F32, "silu%d%d" % (t, hf), tag="silu%d%d" % (t % 2, hf))
+            gained = tile([P, NB], F32, "gained%d%d" % (t, hf), tag="gained%d" % hf if t == 2 else "w1_grouped%d" % hf)
+            resid = tile([P, NB], F32, "resid%d%d" % (t, hf))
+            nc.scalar.activation(out=act[:], in_=acc_a[:], func=ACT.Silu)
+            nc.scalar.activation(out=gained[:], in_=act[:], func=ACT.Copy, scale=gain_sb[:, t : t + 1])
+            nc.scalar.copy(out=resid[:], in_=acc_b[:])
+            ps = bank(base, "sum_turned%d%d" % (t, hf))
+            for blk in blocks():
+                nc.tensor.matmul(ps[:, blk], lhsT=gained[:, blk], rhs=ident[:], is_transpose=True, start=True, stop=False)
+                nc.tensor.matmul(ps[:, blk], lhsT=resid[:, blk], rhs=ident[:], is_transpose=True, start=False, stop=True)
+            turned[t, hf] = ps
+
+        def turn_back(t, hf):
+            base = (t % 2) * 4 + hf * 2
+            rows = tile([P, NB], F32, "turned%d%d" % (t, hf), tag="silu%d%d" % (t % 2, hf))
+            nc.scalar.copy(out=rows[:], in_=turned[t, hf][:])
+            ps = bank(base + 1, "back%d%d" % (t, hf))
+            for blk in blocks():
+                nc.tensor.transpose(ps[:, blk], rows[:, blk], ident[:])
+            turned[t, hf] = ps
+
+        def take_h(t, hf):
+            if hf == 0:
+                h[t] = tile([P, S], F32, "h%d" % t, tag="h%d" % (t % 2))
+            nc.scalar.copy(out=h[t][:, half(hf)], in_=turned[t, hf][:])
+
         def weights(t):
             return wgs_sb[t][:]
 
@@ -244,15 +281,18 @@ def tile_list_antivenom_panel_scores_kernel(
         make_h(1, 0)
         scatter(0, slice(FIRST, S))
         make_h(1, 1)
-        for t in range(1, PACK):
-            if t + 1 < PACK:
-                make_h(t + 1, 0)
-            if t + 2 == PACK:
-                make_h(t + 1, 1)
-            scatter(t, slice(0, S))
-            if t + 2 < PACK:
-                make_h(t + 1, 1)
-            round_plane(t - 1)
+        scatter(1, slice(0, S))
+        for step in (sum_turned, turn_back, take_h):
+            for hf in range(2):
+                step(2, hf)
+        round_plane(0)
+        for step in (sum_turned, turn_back, take_h):
+            for hf in range(2):
+                step(PACK - 1, hf)
+        scatter(2, slice(0, S))
+        round_plane(1)
+        scatter(3, slice(0, S))
+        round_plane(2)
 
         v2_w = []
 

@@ -232,7 +232,7 @@ def tile_list_antivenom_panel_scores_kernel(
             base = (t % 2) * 4 + hf * 2
             act = tile([P, NB], F32, "silu%d%d" % (t, hf), tag="silu%d%d" % (t % 2, hf))
             gained = tile([P, NB], F32, "gained%d%d" % (t, hf), tag="gained%d" % hf if t == 2 else "w1_grouped%d" % hf)
-            resid = tile([P, NB], F32, "resid%d%d" % (t, hf))
+            resid = tile([P, NB], F32, "resid%d%d" % (t, hf), tag="resid%d" % hf if t == 2 else "w1_c%d" % hf)
             nc.scalar.activation(out=act[:], in_=acc_a[:], func=ACT.Silu)
             nc.scalar.activation(out=gained[:], in_=act[:], func=ACT.Copy, scale=gain_sb[:, t : t + 1])
             nc.scalar.copy(out=resid[:], in_=acc_b[:])
@@ -264,10 +264,22 @@ def tile_list_antivenom_panel_scores_kernel(
                 page[t][:].indirect(idx3[:, cols.start // 16 : cols.stop // 16]), h[t][:, cols], weights(t)[:, cols], ALU.mult
             )
 
+        first_plain = PIECES[PAIRED][0]
+        staged = tile([P, PACK - 1, T2 - first_plain], BF16, "staged")
+
         def round_plane(t):
-            for i, (lo, hi) in enumerate(PIECES):
-                dst = pairs[i][:, t // 2, :, t % 2] if i < PAIRED else page_bf[i][:, :, t]
-                nc.scalar.copy(out=dst, in_=page[t][:, lo:hi])
+            for i, (lo, hi) in enumerate(PIECES[:PAIRED]):
+                nc.scalar.copy(out=pairs[i][:, t // 2, :, t % 2], in_=page[t][:, lo:hi])
+            if t < PACK - 1:
+                nc.scalar.copy(out=staged[:, t, :], in_=page[t][:, first_plain:T2])
+            for i, (lo, hi) in list(enumerate(PIECES))[PAIRED:]:
+                if t == PACK - 2:
+                    nc.scalar.copy(
+                        out=page_bf[i][:, :, 0 : PACK - 1].rearrange("p (c i) t -> p c t i", i=PACK),
+                        in_=staged[:, :, lo - first_plain : hi - first_plain].rearrange("p t (c i) -> p c t i", i=PACK),
+                    )
+                elif t == PACK - 1:
+                    nc.scalar.copy(out=page_bf[i][:, :, t], in_=page[t][:, lo:hi])
 
         def weave(i):
             nc.vector.tensor_copy(

@@ -26,8 +26,8 @@ CHUNKS = T2 // NB
 SHIFT_ROWS = 100
 FIRST = 256
 AB_ROW = 12
-PIECES = ((0, 512), (512, 1280), (1280, 1536), (1536, 1792), (1792, 2048))
-PAIRED = 2
+PIECES = ((0, 256), (256, 768), (768, 1280), (1280, 1536), (1536, 1792), (1792, 2048))
+PAIRED = 3
 
 
 def tile_list_antivenom_panel_scores_kernel(
@@ -201,7 +201,7 @@ def tile_list_antivenom_panel_scores_kernel(
             nc.sync.dma_start(out=aff_sb[:], in_=aff.rearrange("(c p) -> p c", p=P))
 
         h = {}
-        page_bf = [tile([P, hi - lo, PACK], BF16, "page_bf%d" % i) if i != 1 else None for i, (lo, hi) in enumerate(PIECES)]
+        page_bf = [tile([P, hi - lo, PACK], BF16, "page_bf%d" % i) if i not in (1, 2) else None for i, (lo, hi) in enumerate(PIECES)]
         pairs = [tile([P, 2, hi - lo, 2], BF16, "pairs%d" % i) for i, (lo, hi) in enumerate(PIECES[:PAIRED])]
 
         def make_h(t, hf):
@@ -345,21 +345,24 @@ def tile_list_antivenom_panel_scores_kernel(
         last_c = CHUNKS - 1
         round_plane(PACK - 1)
         weave(0)
-        quantize(0, 0, 512)
+        quantize(0, 0, 256)
         page_bf[1] = tile([P, PIECES[1][1] - PIECES[1][0], PACK], BF16, "page_bf1", tag="pairs0")
         weave(1)
-        quantize(2, 1280, 1536)
-        quantize(1, 512, 1024)
-        quantize(1, 1024, 1280)
-        quantize(3, 1536, 1792)
-        quantize(4, 1792, 2048)
-        gather_antibodies(1, "page_bf3")
-        third = bank(2, "score02")
-        nc.scalar.copy(out=place(0, 0, full), in_=scores(0, 0, full, 0))
-        scores(0, 2, ends[1], 2, third)
-        nc.scalar.copy(out=place(0, 1, full), in_=scores(0, 1, full, 1))
-        scores(0, 2, ends[0], 2, third)
-        nc.scalar.copy(out=place(0, 2, full), in_=third[:])
+        page_bf[2] = tile([P, PIECES[2][1] - PIECES[2][0], PACK], BF16, "page_bf2", tag="page_bf0")
+        weave(2)
+        quantize(1, 256, 512)
+        quantize(1, 512, 768)
+        quantize(3, 1280, 1536)
+        quantize(2, 768, 1024)
+        quantize(2, 1024, 1280)
+        quantize(4, 1536, 1792)
+        quantize(5, 1792, 2048)
+        gather_antibodies(1, "page_bf4")
+        thirds = [bank(c, "score0%d" % c) for c in range(last_c)]
+        for c, i in ((0, 0), (0, 1), (1, 0), (2, 1), (1, 1), (2, 0)):
+            scores(0, c, ends[i], c, thirds[c])
+        for c in range(last_c):
+            nc.scalar.copy(out=place(0, c, full), in_=thirds[c][:])
         for i, cols in enumerate(ends):
             nc.vector.tensor_copy(out=place(0, last_c, cols), in_=scores(0, last_c, cols, last_c + i))
         for n in range(1, S2 // P):

@@ -23,9 +23,11 @@ PASSES = K // (P * PACK)
 NB = 512
 QUADS = 4
 CHUNKS = T2 // NB
-SHIFT_ROWS = 100
+BLOCKS = S // P
 FIRST = 256
-AB_ROW = 12
+AB_ROW = 4
+SCALE_ROWS = (8, 72)
+VECTOR_BLOCKS = 6
 PIECES = ((0, 256), (256, 768), (768, 1280), (1280, 1536), (1536, 1792), (1792, 2048))
 PAIRED = 3
 
@@ -52,22 +54,22 @@ def tile_list_antivenom_panel_scores_kernel(
         def list_half(i):
             return slice(i * NB // 16, (i + 1) * NB // 16)
 
+        def block(i):
+            return slice(i * P, (i + 1) * P)
+
         idx = lists.tile([P, S // 16], U16, name="idx")
         idx2 = lists.tile([P, S2 // 16], U16, name="idx2")
         idx3 = lists.tile([P, S // 16], U16, name="idx3")
         idx4 = lists.tile([P, M // 16], U16, name="idx4")
 
         tab_sc = tile([P, T], U8, "tab_sc")
-        w2_sc_raw = tile([P, PASSES, H], U8, "w2_sc_raw")
         tab2_sc = tile([P, T3], U8, "tab2_sc")
-        v_sc_low = tile([P, PASSES - 1, S], U8, "v_sc_low")
         nc.vector.memset(tab_sc[:].bitcast(I32), 0)
-        nc.vector.memset(w2_sc_raw[:].bitcast(I32), 0)
         nc.vector.memset(tab2_sc[:].bitcast(I32), 0)
-        for q in range(QUADS):
+        by_row = tab_scales.rearrange("a q t -> q a t")
+        for u, row in enumerate(SCALE_ROWS):
             nc.gpsimd.dma_start(
-                out=tab_sc[32 * q : 32 * q + 4 * PASSES, :].bitcast(I32),
-                in_=tab_scales[:, 4 * q : 4 * q + 4, :].bitcast(I32),
+                out=tab_sc[row : row + 8 * PASSES, :].bitcast(I32), in_=by_row[8 * u : 8 * u + 8].bitcast(I32)
             )
         for q in range(QUADS):
             nc.gpsimd.dma_start(
@@ -75,34 +77,31 @@ def tile_list_antivenom_panel_scores_kernel(
                 in_=tab2_scales[0, 4 * q : 4 * q + 4, :].bitcast(I32),
             )
 
-        w1_raw = [tile([P, PACK, H], F32, "w1_raw%d" % a) for a in range(PASSES)]
         tab_w = [tile([P, T], I32, "tab_w%d" % a) for a in range(PASSES)]
-        w2_raw = tile([P, PASSES, 2 * H], U8, "w2_raw")
+        w1_raw = [tile([P, PACK, H], F32, "w1_raw%d" % a) for a in range(PASSES)]
+        w2_c = tile([P, PASSES, 2 * H], U8, "w2_c")
+        w2_s = tile([P, PASSES, H], U8, "w2_s")
         gain_sb = tile([P, PACK], F32, "gain_sb")
         aff_sb = tile([P, S2 // P], F32, "aff_sb")
-
-        def load_w1(a):
-            nc.sync.dma_start(out=w1_raw[a][:], in_=w1[a * 512 : (a + 1) * 512, :].rearrange("(p j) c -> p j c", j=PACK))
 
         def load_tab(a):
             nc.sync.dma_start(out=tab_w[a][:], in_=tab_words[a].rearrange("p t i -> p (t i)").bitcast(I32))
 
         nc.sync.dma_start(idx[:], offs)
-        nc.sync.dma_start(out=w2_raw[:].bitcast(I32), in_=w2_words.rearrange("a p n -> p a n").bitcast(I32))
-        load_w1(0)
-        for r in range(4):
-            nc.sync.dma_start(
-                out=w2_sc_raw[r:P:32, :, :].bitcast(I32),
-                in_=w2_scales.rearrange("a (q r) n -> r q a n", r=4)[r].bitcast(I32),
-            )
-        load_w1(1)
-        nc.sync.dma_start(out=gain_sb[:], in_=gain.rearrange("(p t) -> p t", t=PACK))
-        nc.sync.dma_start(idx3[:], offs3)
         nc.sync.dma_start(idx2[:], offs2)
         load_tab(0)
+        nc.sync.dma_start(out=w2_c[:].bitcast(I32), in_=w2_words.rearrange("a p n -> p a n").bitcast(I32))
+        for r in range(4):
+            nc.sync.dma_start(
+                out=w2_s[r:P:32, :, :].bitcast(I32),
+                in_=w2_scales.rearrange("a (q r) n -> r q a n", r=4)[r].bitcast(I32),
+            )
         load_tab(1)
-        load_w1(2)
         load_tab(2)
+        nc.sync.dma_start(out=gain_sb[:], in_=gain.rearrange("(p t) -> p t", t=PACK))
+        nc.sync.dma_start(idx3[:], offs3)
+        for a in range(PASSES):
+            nc.sync.dma_start(out=w1_raw[a][:], in_=w1[a * 512 : (a + 1) * 512, :].rearrange("(p j) c -> p j c", j=PACK))
         page_rows = page0.rearrange("(p t) c -> t p c", t=PACK)
         wgs_rows = wgs.rearrange("(m t) j -> m t j", t=PACK)
         page = [tile([P, T2], F32, "page%d" % t) for t in range(PACK)]
@@ -115,81 +114,112 @@ def tile_list_antivenom_panel_scores_kernel(
         nc.sync.dma_start(out=page[0][:], in_=page_rows[0])
         load_wgs(0, slice(0, FIRST))
         load_wgs(0, slice(FIRST, S))
-        for t in range(1, PACK - 1):
+        for t in range(1, PACK):
             nc.sync.dma_start(out=page[t][:], in_=page_rows[t])
             load_wgs(t, slice(0, S))
-        nc.sync.dma_start(out=page[PACK - 1][:], in_=page_rows[PACK - 1])
-        load_wgs(PACK - 1, slice(0, S))
         tab2_w = tile([P, T3], I32, "tab2_w")
         nc.sync.dma_start(out=tab2_w[:], in_=tab2_words[0].rearrange("p t i -> p (t i)").bitcast(I32))
         nc.sync.dma_start(idx4[:], offs4)
 
-        w2_c = tile([P, PASSES, 2 * H], U8, "w2_c")
-        w2_s = tile([P, PASSES, H], U8, "w2_s")
-        nc.vector.tensor_copy(
-            out=w2_c[:].bitcast(U16).rearrange("p a (t m) -> p a t m", t=PACK),
-            in_=w2_raw[:].bitcast(U16).rearrange("p a (m t) -> p a t m", t=PACK),
-        )
-        nc.vector.tensor_copy(
-            out=w2_s[:].rearrange("p a (t m) -> p a t m", t=PACK),
-            in_=w2_sc_raw[:].rearrange("p a (m t) -> p a t m", t=PACK),
-        )
-
-        v_sc = tile([P, S], U8, "v_sc")
-        nc.vector.tensor_copy(v_sc[:], tab_sc[:].indirect(idx[:]))
-        for a in range(1, PASSES):
+        v_rows = tile([P, S], U8, "v_rows")
+        v_s = tile([P, PASSES, S], U8, "v_s")
+        nc.vector.tensor_copy(v_rows[:], tab_sc[:].indirect(idx[:]))
+        for q in range(QUADS):
+            row = SCALE_ROWS[q // 2] + (q % 2) * 4 * PASSES
             nc.gpsimd.dma_start(
-                out=v_sc_low[0:SHIFT_ROWS, a - 1, :].bitcast(I32),
-                in_=v_sc[4 * a : 4 * a + SHIFT_ROWS, :].bitcast(I32),
+                out=v_s[32 * q : 32 * q + 4, :, :].bitcast(I32), in_=v_rows[row : row + 4 * PASSES, :].bitcast(I32)
             )
 
-        def v_plane(a, cols):
-            return v_sc[:, cols] if a == 0 else v_sc_low[:, a - 1, cols]
-
-        w1_c, w1_s, v_w = [], [], []
-        acc = {}
-
-        def first_stage_pass(t, hf, a):
-            if a == 0:
-                base = (t % 2) * 4 + hf * 2
-                acc[t, hf] = (bank(base, "acc_a%d%d" % (t, hf)), bank(base + 1, "acc_b%d%d" % (t, hf)))
-            acc_a, acc_b = acc[t, hf]
-            ch = slice(t * P, (t + 1) * P)
-            moving = v_w[a][:, half(hf)].bitcast(FP8X4)
-            nc.tensor.matmul_mx(
-                out=acc_a[:], lhsT=w1_c[a][:, ch].bitcast(FP8X4), lhsT_scale=w1_s[a][:, ch],
-                rhs=moving, rhs_scale=v_sc[4 * a : P, half(hf)], start=(a == 0), stop=(a == PASSES - 1),
-            )
-            nc.tensor.matmul_mx(
-                out=acc_b[:], lhsT=w2_c[:, a, 2 * t * P : 2 * (t + 1) * P].bitcast(FP4X4), lhsT_scale=w2_s[:, a, ch],
-                rhs=moving, rhs_scale=v_plane(a, half(hf)), start=(a == 0), stop=(a == PASSES - 1),
-            )
-
+        v_w = [tile([P, S], U32, "v_w%d" % a, tag="tab2_sc" if a == PASSES - 1 else None) for a in range(PASSES)]
         v2_s = tile([P, S2], U8, "v2_s")
-        for a in range(PASSES):
-            if a == 1:
-                nc.vector.tensor_copy(v2_s[:], tab2_sc[:].indirect(idx2[:]))
-            grouped = tile([P, H * PACK], BF16, "w1_grouped%d" % a, tag="w1_grouped%d" % (a % 2))
-            nc.scalar.copy(
-                out=grouped[:].rearrange("p (t m j) -> p m t j", t=PACK, j=PACK),
-                in_=w1_raw[a][:].rearrange("p j (m t) -> p m t j", t=PACK),
+        res_ps = [bank(j, "res%d" % j) for j in range(BLOCKS)]
+
+        def residual_pass(a, j):
+            nc.tensor.matmul_mx(
+                out=res_ps[j][:], lhsT=v_w[a][:, block(j)].bitcast(FP8X4), lhsT_scale=v_s[:, a, block(j)],
+                rhs=w2_c[:, a, :].bitcast(FP4X4), rhs_scale=w2_s[:, a, :], start=(a == 0), stop=(a == PASSES - 1),
             )
-            codes = tile([P, H], U32, "w1_c%d" % a)
-            scales = tile([P, H], U8, "w1_s%d" % a)
-            nc.vector.quantize_mx(out=codes[:].bitcast(FP8X4), scales=scales[:], in_=grouped[:])
-            w1_c.append(codes)
-            w1_s.append(scales)
-            picked = tile([P, S], U32, "v_w%d" % a)
-            v_w.append(picked)
+
+        for a in range(PASSES):
             window = tab_w[a][:].bitcast(U32)
             if a < PASSES - 1:
-                nc.vector.tensor_copy(picked[:], window.indirect(idx[:]))
+                nc.vector.tensor_copy(v_w[a][:], window.indirect(idx[:]))
             else:
                 for hf in range(2):
-                    nc.vector.tensor_copy(picked[:, half(hf)], window.indirect(idx[:, list_half(hf)]))
+                    nc.vector.tensor_copy(v_w[a][:, half(hf)], window.indirect(idx[:, list_half(hf)]))
+            if a == 0:
+                nc.vector.tensor_copy(v2_s[:], tab2_sc[:].indirect(idx2[:]))
+            for j in range(BLOCKS):
+                residual_pass(a, j)
+
+        ident = tile([P, P], F32, "ident")
+        make_identity(nc, ident[:])
+
+        w1_s = tile([P, PASSES, H], U8, "w1_s", tag="w2_s")
+        w1_c = {}
+        grouped = {}
+
+        def round_w1(a, u, engine_copy, tag):
+            grouped[a, u] = tile([P, H * PACK // 2], BF16, "grouped%d%d" % (a, u), tag=tag)
+            engine_copy(
+                out=grouped[a, u][:].rearrange("p (t m j) -> p m t j", t=2, j=PACK),
+                in_=w1_raw[a][:].rearrange("p j (m t) -> p m t j", t=PACK)[:, :, 2 * u : 2 * u + 2, :],
+            )
+
+        def quantize_w1(a, u):
+            w1_c[a, u] = tile([P, H // 2], U32, "w1_c%d%d" % (a, u))
+            nc.vector.quantize_mx(
+                out=w1_c[a, u][:].bitcast(FP8X4), scales=w1_s[:, a, u * H // 2 : (u + 1) * H // 2], in_=grouped[a, u][:]
+            )
+
+        for a in range(PASSES - 1):
+            for u in range(2):
+                round_w1(a, u, nc.scalar.copy, "grouped%d%d" % (a, u))
+
+        res = []
+        for j in range(BLOCKS):
+            rows = tile([P, NB], F32, "res_sb%d" % j)
+            copy = nc.vector.tensor_copy if j < VECTOR_BLOCKS else nc.scalar.copy
+            copy(out=rows[:].rearrange("p (t m) -> p t m", t=PACK), in_=res_ps[j][:].rearrange("p (m t) -> p t m", t=PACK))
+            res.append(rows)
+
+        acc = {}
+
+        def branch_pass(t, hf, a, b):
+            if (t, hf) not in acc:
+                acc[t, hf] = bank(b, "acc%d%d" % (t, hf))
+            ch = slice(t % 2 * P, (t % 2 + 1) * P)
+            nc.tensor.matmul_mx(
+                out=acc[t, hf][:], lhsT=w1_c[a, t // 2][:, ch].bitcast(FP8X4), lhsT_scale=w1_s[:, a, block(t)],
+                rhs=v_w[a][:, half(hf)].bitcast(FP8X4), rhs_scale=v_s[:, a, half(hf)],
+                start=(a == 0), stop=(a == PASSES - 1),
+            )
+
+        back = {}
+
+        def turn_residual(t, hf, b):
+            back[t, hf] = bank(b, "res_back%d%d" % (t, hf))
+            for i in range(NB // P):
+                nc.tensor.transpose(back[t, hf][:, block(i)], res[hf * NB // P + i][:, block(t)], ident[:])
+
+        turn_residual(0, 0, 0)
+        turn_residual(1, 0, 1)
+        quantize_w1(0, 0)
+        quantize_w1(0, 1)
+        quantize_w1(1, 0)
+        for a in range(PASSES - 1):
             for t in range(2):
                 for hf in range(2):
-                    first_stage_pass(t, hf, a)
+                    branch_pass(t, hf, a, 2 + 2 * t + hf)
+        last_a = PASSES - 1
+        round_w1(last_a, 0, nc.vector.tensor_copy, "w2_c")
+        quantize_w1(1, 1)
+        quantize_w1(last_a, 0)
+        for t in range(2):
+            for hf in range(2):
+                branch_pass(t, hf, last_a, 2 + 2 * t + hf)
+        round_w1(last_a, 1, nc.vector.tensor_copy, "w2_c")
+        quantize_w1(last_a, 1)
 
         lod_rows = lod.rearrange("(c p) m -> p c m", p=P)
         lod_sb = []
@@ -203,69 +233,54 @@ def tile_list_antivenom_panel_scores_kernel(
         h = {}
         page_bf = [tile([P, hi - lo, PACK], BF16, "page_bf%d" % i) if i not in (1, 2) else None for i, (lo, hi) in enumerate(PIECES)]
         pairs = [tile([P, 2, hi - lo, 2], BF16, "pairs%d" % i) for i, (lo, hi) in enumerate(PIECES[:PAIRED])]
+        acts = {}
 
-        def make_h(t, hf):
-            if hf == 0:
+        def silu(t, hf, cols):
+            if cols.start == 0:
+                acts[t, hf] = tile([P, NB], F32, "silu%d%d" % (t, hf), tag="silu%d%d" % (t % 2, hf))
+            nc.scalar.activation(out=acts[t, hf][:, cols], in_=acc[t, hf][:, cols], func=ACT.Silu)
+
+        def join(t, hf, cols):
+            if t not in h:
                 h[t] = tile([P, S], F32, "h%d" % t, tag="h%d" % (t % 2))
-            acc_a, acc_b = acc[t, hf]
-            act = tile([P, NB], F32, "silu%d%d" % (t, hf), tag="silu%d%d" % (t % 2, hf))
-            cuts = (0, FIRST, NB) if (t, hf) == (0, 0) else (0, NB)
-            for lo, hi in zip(cuts, cuts[1:]):
-                nc.scalar.activation(out=act[:, lo:hi], in_=acc_a[:, lo:hi], func=ACT.Silu)
-                nc.vector.scalar_tensor_tensor(
-                    out=h[t][:, hf * NB + lo : hf * NB + hi], in0=act[:, lo:hi], scalar=gain_sb[:, t : t + 1],
-                    in1=acc_b[:, lo:hi], op0=ALU.mult, op1=ALU.add,
-                )
-            if t + 2 < PACK:
-                for a in range(PASSES):
-                    first_stage_pass(t + 2, hf, a)
+            nc.vector.scalar_tensor_tensor(
+                out=h[t][:, hf * NB + cols.start : hf * NB + cols.stop], in0=acts[t, hf][:, cols],
+                scalar=gain_sb[:, t : t + 1], in1=back[t, hf][:, cols], op0=ALU.mult, op1=ALU.add,
+            )
 
-        ident = tile([P, P], F32, "ident", tag="tab2_sc")
-        make_identity(nc, ident[:])
         turned = {}
 
-        def blocks():
-            return [slice(i * P, (i + 1) * P) for i in range(NB // P)]
+        def turn_branch(t, hf):
+            silu(t, hf, slice(0, NB))
+            gained = tile([P, NB], F32, "gained%d%d" % (t, hf), tag="gained%d" % hf)
+            nc.scalar.activation(out=gained[:], in_=acts[t, hf][:], func=ACT.Copy, scale=gain_sb[:, t : t + 1])
+            turned[t, hf] = bank(6 + hf, "turned%d%d" % (t, hf))
+            for i in range(NB // P):
+                nc.tensor.transpose(turned[t, hf][:, block(i)], gained[:, block(i)], ident[:])
 
-        def sum_turned(t, hf):
-            acc_a, acc_b = acc[t, hf]
-            base = (t % 2) * 4 + hf * 2
-            act = tile([P, NB], F32, "silu%d%d" % (t, hf), tag="silu%d%d" % (t % 2, hf))
-            gained = tile([P, NB], F32, "gained%d%d" % (t, hf), tag="gained%d" % hf if t == 2 else "w1_grouped%d" % hf)
-            resid = tile([P, NB], F32, "resid%d%d" % (t, hf), tag="resid%d" % hf if t == 2 else "w1_c%d" % hf)
-            nc.scalar.activation(out=act[:], in_=acc_a[:], func=ACT.Silu)
-            nc.scalar.activation(out=gained[:], in_=act[:], func=ACT.Copy, scale=gain_sb[:, t : t + 1])
-            nc.scalar.copy(out=resid[:], in_=acc_b[:])
-            ps = bank(base, "sum_turned%d%d" % (t, hf))
-            for blk in blocks():
-                nc.tensor.matmul(ps[:, blk], lhsT=gained[:, blk], rhs=ident[:], is_transpose=True, start=True, stop=False)
-                nc.tensor.matmul(ps[:, blk], lhsT=resid[:, blk], rhs=ident[:], is_transpose=True, start=False, stop=True)
-            turned[t, hf] = ps
-
-        def turn_back(t, hf):
-            base = (t % 2) * 4 + hf * 2
-            rows = tile([P, NB], F32, "turned%d%d" % (t, hf), tag="silu%d%d" % (t % 2, hf))
+        def sum_back(t, hf, b):
+            rows = tile([P, NB], F32, "turned_sb%d%d" % (t, hf), tag="silu%d%d" % (t % 2, hf))
             nc.scalar.copy(out=rows[:], in_=turned[t, hf][:])
-            ps = bank(base + 1, "back%d%d" % (t, hf))
-            for blk in blocks():
-                nc.tensor.transpose(ps[:, blk], rows[:, blk], ident[:])
-            turned[t, hf] = ps
+            back[t, hf] = bank(b, "sum%d%d" % (t, hf))
+            for i in range(NB // P):
+                ps = back[t, hf][:, block(i)]
+                nc.tensor.matmul(ps, lhsT=rows[:, block(i)], rhs=ident[:], is_transpose=True, start=True, stop=False)
+                nc.tensor.matmul(
+                    ps, lhsT=res[hf * NB // P + i][:, block(t)], rhs=ident[:], is_transpose=True, start=False, stop=True
+                )
 
         def take_h(t, hf):
             if hf == 0:
                 h[t] = tile([P, S], F32, "h%d" % t, tag="h%d" % (t % 2))
-            nc.scalar.copy(out=h[t][:, half(hf)], in_=turned[t, hf][:])
-
-        def weights(t):
-            return wgs_sb[t][:]
+            nc.scalar.copy(out=h[t][:, half(hf)], in_=back[t, hf][:])
 
         def scatter(t, cols):
             nc.vector.tensor_tensor(
-                page[t][:].indirect(idx3[:, cols.start // 16 : cols.stop // 16]), h[t][:, cols], weights(t)[:, cols], ALU.mult
+                page[t][:].indirect(idx3[:, cols.start // 16 : cols.stop // 16]), h[t][:, cols], wgs_sb[t][:, cols], ALU.mult
             )
 
         first_plain = PIECES[PAIRED][0]
-        staged = tile([P, PACK - 1, T2 - first_plain], BF16, "staged")
+        staged = tile([P, PACK - 1, T2 - first_plain], BF16, "staged", tag="tab_sc")
 
         def round_plane(t):
             for i, (lo, hi) in enumerate(PIECES[:PAIRED]):
@@ -287,20 +302,40 @@ def tile_list_antivenom_panel_scores_kernel(
                 in_=pairs[i][:].rearrange("p u c e -> p u (c e)").bitcast(I32).rearrange("p u c -> p c u"),
             )
 
-        make_h(0, 0)
+        full = slice(0, NB)
+        late_banks = {(2, 0): 0, (2, 1): 4, (3, 0): 5, (3, 1): 1}
+
+        def late_branch(t, hf):
+            for a in range(PASSES):
+                branch_pass(t, hf, a, late_banks[t, hf])
+
+        for cols in (slice(0, FIRST), slice(FIRST, NB)):
+            silu(0, 0, cols)
+            join(0, 0, cols)
         scatter(0, slice(0, FIRST))
-        make_h(0, 1)
-        make_h(1, 0)
+        turn_residual(0, 1, 2)
+        silu(0, 1, full)
+        join(0, 1, full)
+        turn_residual(1, 1, 3)
+        late_branch(2, 0)
+        silu(1, 0, full)
+        join(1, 0, full)
+        late_branch(2, 1)
         scatter(0, slice(FIRST, S))
-        make_h(1, 1)
+        silu(1, 1, full)
+        join(1, 1, full)
+        late_branch(3, 0)
+        late_branch(3, 1)
         scatter(1, slice(0, S))
-        for step in (sum_turned, turn_back, take_h):
+        for t in (2, 3):
             for hf in range(2):
-                step(2, hf)
-        round_plane(0)
-        for step in (sum_turned, turn_back, take_h):
+                turn_branch(t, hf)
             for hf in range(2):
-                step(PACK - 1, hf)
+                sum_back(t, hf, late_banks[t, hf])
+            for hf in range(2):
+                take_h(t, hf)
+            if t == 2:
+                round_plane(0)
         scatter(2, slice(0, S))
         round_plane(1)
         scatter(3, slice(0, S))
@@ -317,7 +352,7 @@ def tile_list_antivenom_panel_scores_kernel(
 
         e_tags = ["tab_w0", "tab_w1", "tab_w2", "w1_raw2"]
         e = [tile([P, T2], F32, "e%d" % n, tag=e_tags[n]) for n in range(S2 // P)]
-        page_c = [tile([P, NB], U32, "page_c%d" % c) for c in range(CHUNKS)]
+        page_c = [tile([P, NB], U32, "page_c%d" % c, tag="grouped%d%d" % (c // 2, c % 2)) for c in range(CHUNKS)]
         page_s = [tile([P, NB], U8, "page_s%d" % c) for c in range(CHUNKS)]
 
         def quantize(i, lo, hi):
@@ -340,7 +375,6 @@ def tile_list_antivenom_panel_scores_kernel(
         def place(n, c, cols):
             return e[n][:, c * NB + cols.start : c * NB + cols.stop]
 
-        full = slice(0, NB)
         ends = [slice(0, NB // 2), slice(NB // 2, NB)]
         last_c = CHUNKS - 1
         round_plane(PACK - 1)
@@ -370,7 +404,7 @@ def tile_list_antivenom_panel_scores_kernel(
                 b = (5, 3, 4, 6)[c] if n == 1 else (7, 0, 1, 2)[c]
                 nc.scalar.copy(out=place(n, c, full), in_=scores(n, c, full, b))
 
-        x_tags = ["v_w0", "v_w1", "v_w2", "w1_grouped0"]
+        x_tags = ["v_w0", "v_w1", "tab2_sc", "h1"]
         x = [tile([P, M], F32, "x%d" % n, tag=x_tags[n]) for n in range(S2 // P)]
         last = S2 // P - 1
 

@@ -64,11 +64,14 @@ def tile_list_antivenom_panel_scores_kernel(
 
         tab_sc = tile([P, T], U8, "tab_sc")
         tab2_sc = tile([P, T3], U8, "tab2_sc")
-        nc.vector.memset(tab_sc[:].bitcast(I32), 0)
         nc.vector.memset(tab2_sc[:].bitcast(I32), 0)
+        for lo, hi in ((0, 8), (32, 64), (64, 72), (96, 128)):
+            nc.vector.memset(tab_sc[lo:hi, :].bitcast(I32), 0)
+        w2_c = tile([P, PASSES, 2 * H], U8, "w2_c")
+        nc.sync.dma_start(out=w2_c[:].bitcast(I32), in_=w2_words.rearrange("a p n -> p a n").bitcast(I32))
         by_row = tab_scales.rearrange("a q t -> q a t")
         for u, row in enumerate(SCALE_ROWS):
-            nc.gpsimd.dma_start(
+            nc.sync.dma_start(
                 out=tab_sc[row : row + 8 * PASSES, :].bitcast(I32), in_=by_row[8 * u : 8 * u + 8].bitcast(I32)
             )
         for q in range(QUADS):
@@ -79,7 +82,6 @@ def tile_list_antivenom_panel_scores_kernel(
 
         tab_w = [tile([P, T], I32, "tab_w%d" % a) for a in range(PASSES)]
         w1_raw = [tile([P, PACK, H], F32, "w1_raw%d" % a) for a in range(PASSES)]
-        w2_c = tile([P, PASSES, 2 * H], U8, "w2_c")
         w2_s = tile([P, PASSES, H], U8, "w2_s")
         gain_sb = tile([P, PACK], F32, "gain_sb")
         aff_sb = tile([P, S2 // P], F32, "aff_sb")
@@ -89,9 +91,9 @@ def tile_list_antivenom_panel_scores_kernel(
 
         nc.sync.dma_start(idx[:], offs)
         nc.sync.dma_start(idx2[:], offs2)
-        load_tab(0)
-        nc.sync.dma_start(out=w2_c[:].bitcast(I32), in_=w2_words.rearrange("a p n -> p a n").bitcast(I32))
         for r in range(4):
+            if r == 2:
+                load_tab(0)
             nc.sync.dma_start(
                 out=w2_s[r:P:32, :, :].bitcast(I32),
                 in_=w2_scales.rearrange("a (q r) n -> r q a n", r=4)[r].bitcast(I32),
@@ -126,7 +128,7 @@ def tile_list_antivenom_panel_scores_kernel(
         nc.vector.tensor_copy(v_rows[:], tab_sc[:].indirect(idx[:]))
         for q in range(QUADS):
             row = SCALE_ROWS[q // 2] + (q % 2) * 4 * PASSES
-            nc.gpsimd.dma_start(
+            nc.scalar.dma_start(
                 out=v_s[32 * q : 32 * q + 4, :, :].bitcast(I32), in_=v_rows[row : row + 4 * PASSES, :].bitcast(I32)
             )
 
@@ -176,12 +178,12 @@ def tile_list_antivenom_panel_scores_kernel(
             for u in range(2):
                 round_w1(a, u, nc.scalar.copy, "grouped%d%d" % (a, u))
 
-        res = []
+        res = [tile([P, NB], F32, "res_sb%d" % j)[:] for j in range(VECTOR_BLOCKS)]
+        res_late = tile([P, BLOCKS - VECTOR_BLOCKS, NB], F32, "res_late", tag="w1_raw1")
+        res.extend(res_late[:, j, :] for j in range(BLOCKS - VECTOR_BLOCKS))
         for j in range(BLOCKS):
-            rows = tile([P, NB], F32, "res_sb%d" % j)
             copy = nc.vector.tensor_copy if j < VECTOR_BLOCKS else nc.scalar.copy
-            copy(out=rows[:].rearrange("p (t m) -> p t m", t=PACK), in_=res_ps[j][:].rearrange("p (m t) -> p t m", t=PACK))
-            res.append(rows)
+            copy(out=res[j].rearrange("p (t m) -> p t m", t=PACK), in_=res_ps[j][:].rearrange("p (m t) -> p t m", t=PACK))
 
         acc = {}
 
@@ -220,15 +222,6 @@ def tile_list_antivenom_panel_scores_kernel(
                 branch_pass(t, hf, last_a, 2 + 2 * t + hf)
         round_w1(last_a, 1, nc.vector.tensor_copy, "w2_c")
         quantize_w1(last_a, 1)
-
-        lod_rows = lod.rearrange("(c p) m -> p c m", p=P)
-        lod_sb = []
-        for i in range(2):
-            floor = tile([P, 2, M], F32, "lod%d" % i, tag="w1_raw%d" % i)
-            nc.sync.dma_start(out=floor[:], in_=lod_rows[:, 2 * i : 2 * i + 2, :])
-            lod_sb.append(floor)
-        with nc.allow_non_contiguous_dma(reason="one offset for each partition and tile of antibodies"):
-            nc.sync.dma_start(out=aff_sb[:], in_=aff.rearrange("(c p) -> p c", p=P))
 
         h = {}
         page_bf = [tile([P, hi - lo, PACK], BF16, "page_bf%d" % i) if i not in (1, 2) else None for i, (lo, hi) in enumerate(PIECES)]
@@ -340,6 +333,15 @@ def tile_list_antivenom_panel_scores_kernel(
         round_plane(1)
         scatter(3, slice(0, S))
         round_plane(2)
+
+        lod_rows = lod.rearrange("(c p) m -> p c m", p=P)
+        lod_sb = []
+        for i in range(2):
+            floor = tile([P, 2, M], F32, "lod%d" % i, tag="w1_raw%d" % i)
+            nc.sync.dma_start(out=floor[:], in_=lod_rows[:, 2 * i : 2 * i + 2, :])
+            lod_sb.append(floor)
+        with nc.allow_non_contiguous_dma(reason="one offset for each partition and tile of antibodies"):
+            nc.sync.dma_start(out=aff_sb[:], in_=aff.rearrange("(c p) -> p c", p=P))
 
         v2_w = []
 

@@ -23,13 +23,17 @@ PASSES = K // (P * PACK)
 NB = 512
 QUADS = 4
 CHUNKS = T2 // NB
-BLOCKS = S // P
 FIRST = 256
 AB_ROW = 4
 SCALE_ROWS = (8, 72)
-VECTOR_BLOCKS = 6
 PIECES = ((0, 256), (256, 768), (768, 1280), (1280, 1536), (1536, 1792), (1792, 2048))
 PAIRED = 3
+EARLY = 3
+W1_KIB = (72, 0, 8)
+PAGE_KIB = (16, 40, 8, 49)
+WGS_KIB = (32, 36, 0, 57.5)
+RES_KIB = (None, 62, 66, 24)
+BACK_BANK = (None, None, 4, 2)
 
 
 def tile_list_antivenom_panel_scores_kernel(
@@ -40,10 +44,14 @@ def tile_list_antivenom_panel_scores_kernel(
     with ExitStack() as ctx:
         lists = ctx.enter_context(tc.tile_pool(name="lists", bufs=1))
         sb = ctx.enter_context(tc.tile_pool(name="sb", bufs=1))
+        shared = ctx.enter_context(tc.tile_pool(name="shared", bufs=1))
         psum = ctx.enter_context(tc.psum_pool(name="psum", bufs=1))
 
         def tile(shape, dtype, name, tag=None):
             return sb.tile(shape, dtype, name=name, tag=tag or name, align_bytes=64)
+
+        def placed(shape, dtype, name, kib):
+            return shared.tile(shape, dtype, name=name, offset=int(kib * 1024), align_bytes=64)
 
         def bank(i, name):
             return psum.tile([P, NB], F32, name=name, tag="bank%d" % i)
@@ -62,166 +70,192 @@ def tile_list_antivenom_panel_scores_kernel(
         idx3 = lists.tile([P, S // 16], U16, name="idx3")
         idx4 = lists.tile([P, M // 16], U16, name="idx4")
 
-        tab_sc = tile([P, T], U8, "tab_sc")
+        w2_s_raw = tile([P, PASSES, H], U8, "w2_s_raw")
         tab2_sc = tile([P, T3], U8, "tab2_sc")
+        tab_sc = placed([P, T], U8, "tab_sc", 32)
+        nc.vector.memset(w2_s_raw[:].bitcast(I32), 0)
         nc.vector.memset(tab2_sc[:].bitcast(I32), 0)
         for lo, hi in ((0, 8), (32, 64), (64, 72), (96, 128)):
             nc.vector.memset(tab_sc[lo:hi, :].bitcast(I32), 0)
-        w2_c = tile([P, PASSES, 2 * H], U8, "w2_c")
-        nc.sync.dma_start(out=w2_c[:].bitcast(I32), in_=w2_words.rearrange("a p n -> p a n").bitcast(I32))
-        by_row = tab_scales.rearrange("a q t -> q a t")
-        for u, row in enumerate(SCALE_ROWS):
-            nc.sync.dma_start(
-                out=tab_sc[row : row + 8 * PASSES, :].bitcast(I32), in_=by_row[8 * u : 8 * u + 8].bitcast(I32)
-            )
         for q in range(QUADS):
             nc.gpsimd.dma_start(
                 out=tab2_sc[32 * q + AB_ROW : 32 * q + AB_ROW + 4, :].bitcast(I32),
                 in_=tab2_scales[0, 4 * q : 4 * q + 4, :].bitcast(I32),
             )
 
-        tab_w = [tile([P, T], I32, "tab_w%d" % a) for a in range(PASSES)]
-        w1_raw = [tile([P, PACK, H], F32, "w1_raw%d" % a) for a in range(PASSES)]
-        w2_s = tile([P, PASSES, H], U8, "w2_s")
-        gain_sb = tile([P, PACK], F32, "gain_sb")
-        aff_sb = tile([P, S2 // P], F32, "aff_sb")
+        w1_raw, tab_w, page, wgs_sb = {}, {}, {}, {}
+
+        def load_w1(a):
+            w1_raw[a] = placed([P, PACK, H], F32, "w1_raw%d" % a, W1_KIB[a])
+            nc.sync.dma_start(out=w1_raw[a][:], in_=w1[a * 512 : (a + 1) * 512, :].rearrange("(p j) c -> p j c", j=PACK))
 
         def load_tab(a):
+            tab_w[a] = placed([P, T], I32, "tab_w%d" % a, 16 * a)
             nc.sync.dma_start(out=tab_w[a][:], in_=tab_words[a].rearrange("p t i -> p (t i)").bitcast(I32))
 
+        load_w1(0)
+        by_row = tab_scales.rearrange("a q t -> q a t")
+        for u, row in enumerate(SCALE_ROWS):
+            nc.sync.dma_start(
+                out=tab_sc[row : row + 8 * PASSES, :].bitcast(I32), in_=by_row[8 * u : 8 * u + 8].bitcast(I32)
+            )
         nc.sync.dma_start(idx[:], offs)
-        nc.sync.dma_start(idx2[:], offs2)
+        w2_raw = tile([P, PASSES, 2 * H], U8, "w2_raw")
+        nc.sync.dma_start(out=w2_raw[:].bitcast(I32), in_=w2_words.rearrange("a p n -> p a n").bitcast(I32))
         for r in range(4):
             if r == 2:
                 load_tab(0)
             nc.sync.dma_start(
-                out=w2_s[r:P:32, :, :].bitcast(I32),
+                out=w2_s_raw[r:P:32, :, :].bitcast(I32),
                 in_=w2_scales.rearrange("a (q r) n -> r q a n", r=4)[r].bitcast(I32),
             )
+        nc.sync.dma_start(idx2[:], offs2)
         load_tab(1)
-        load_tab(2)
-        nc.sync.dma_start(out=gain_sb[:], in_=gain.rearrange("(p t) -> p t", t=PACK))
         nc.sync.dma_start(idx3[:], offs3)
-        for a in range(PASSES):
-            nc.sync.dma_start(out=w1_raw[a][:], in_=w1[a * 512 : (a + 1) * 512, :].rearrange("(p j) c -> p j c", j=PACK))
-        page_rows = page0.rearrange("(p t) c -> t p c", t=PACK)
-        wgs_rows = wgs.rearrange("(m t) j -> m t j", t=PACK)
-        page = [tile([P, T2], F32, "page%d" % t) for t in range(PACK)]
-        wgs_sb = [tile([P, S], F32, "wgs%d" % t) for t in range(PACK)]
-
-        def load_wgs(t, cols):
-            for q in (0, 2, 1, 3):
-                nc.sync.dma_start(out=wgs_sb[t][32 * q : 32 * q + 32, cols], in_=wgs_rows[:, t, cols])
-
-        nc.sync.dma_start(out=page[0][:], in_=page_rows[0])
-        load_wgs(0, slice(0, FIRST))
-        load_wgs(0, slice(FIRST, S))
-        for t in range(1, PACK):
-            nc.sync.dma_start(out=page[t][:], in_=page_rows[t])
-            load_wgs(t, slice(0, S))
-        tab2_w = tile([P, T3], I32, "tab2_w")
-        nc.sync.dma_start(out=tab2_w[:], in_=tab2_words[0].rearrange("p t i -> p (t i)").bitcast(I32))
         nc.sync.dma_start(idx4[:], offs4)
 
-        v_rows = tile([P, S], U8, "v_rows")
+        v_rows = placed([P, S], U8, "v_rows", 70)
         v_s = tile([P, PASSES, S], U8, "v_s")
         nc.vector.tensor_copy(v_rows[:], tab_sc[:].indirect(idx[:]))
         for q in range(QUADS):
             row = SCALE_ROWS[q // 2] + (q % 2) * 4 * PASSES
-            nc.scalar.dma_start(
+            nc.sync.dma_start(
                 out=v_s[32 * q : 32 * q + 4, :, :].bitcast(I32), in_=v_rows[row : row + 4 * PASSES, :].bitcast(I32)
             )
+        load_tab(2)
+
+        page_rows = page0.rearrange("(p t) c -> t p c", t=PACK)
+        wgs_rows = wgs.rearrange("(m t) j -> m t j", t=PACK)
+
+        def load_page(t):
+            page[t] = placed([P, T2], F32, "page%d" % t, PAGE_KIB[t])
+            nc.sync.dma_start(out=page[t][:], in_=page_rows[t])
+
+        def load_wgs(t, cols):
+            if t not in wgs_sb:
+                wgs_sb[t] = placed([P, S], F32, "wgs%d" % t, WGS_KIB[t])
+            for q in (0, 2, 1, 3):
+                nc.sync.dma_start(out=wgs_sb[t][32 * q : 32 * q + 32, cols], in_=wgs_rows[:, t, cols])
+
+        w2_c = [placed([P, PASSES, EARLY, 2 * P], U8, "w2_c_early", 56), tile([P, PASSES, 1, 2 * P], U8, "w2_c_last")]
+        w2_s = [placed([P, PASSES, EARLY, P], U8, "w2_s_early", 80), tile([P, PASSES, 1, P], U8, "w2_s_last")]
+        for i, sets in enumerate((slice(0, EARLY), slice(EARLY, PACK))):
+            nc.vector.tensor_copy(
+                out=w2_c[i][:].bitcast(U16).rearrange("p a t (u m) -> p u a t m", u=2),
+                in_=w2_raw[:].bitcast(U16).rearrange("p a (u m t) -> p u a t m", u=2, t=PACK)[:, :, :, sets, :],
+            )
+            nc.vector.tensor_copy(
+                out=w2_s[i][:].rearrange("p a t (u m) -> p u a t m", u=2),
+                in_=w2_s_raw[:].rearrange("p a (u m t) -> p u a t m", u=2, t=PACK)[:, :, :, sets, :],
+            )
+
+        w1_c, w1_s, grouped = {}, {}, {}
+
+        def round_w1(a, sets, copy, dst):
+            grouped[a, sets.start] = dst
+            copy(
+                out=dst[:].rearrange("p (t m j) -> p m t j", m=P, j=PACK),
+                in_=w1_raw[a][:].rearrange("p j (m t) -> p m t j", t=PACK)[:, :, sets, :],
+            )
+
+        def quantize_w1(a, sets, scales):
+            codes = tile([P, (sets.stop - sets.start) * P], U32, "w1_c%d%d" % (a, sets.start))
+            nc.vector.quantize_mx(out=codes[:].bitcast(FP8X4), scales=scales, in_=grouped[a, sets.start][:])
+            for t in range(sets.start, sets.stop):
+                w1_c[a, t] = codes[:, block(t - sets.start)]
+                w1_s[a, t] = scales[:, block(t - sets.start)]
+
+        every, low, high = slice(0, PACK), slice(0, 2), slice(2, PACK)
+        round_w1(0, every, nc.scalar.copy, tile([P, H * PACK], BF16, "grouped0"))
+        quantize_w1(0, every, tile([P, H], U8, "w1_s0")[:])
 
         v_w = [tile([P, S], U32, "v_w%d" % a, tag="tab2_sc" if a == PASSES - 1 else None) for a in range(PASSES)]
         v2_s = tile([P, S2], U8, "v2_s")
-        res_ps = [bank(j, "res%d" % j) for j in range(BLOCKS)]
+        acc, res_ps = {}, {}
 
-        def residual_pass(a, j):
-            nc.tensor.matmul_mx(
-                out=res_ps[j][:], lhsT=v_w[a][:, block(j)].bitcast(FP8X4), lhsT_scale=v_s[:, a, block(j)],
-                rhs=w2_c[:, a, :].bitcast(FP4X4), rhs_scale=w2_s[:, a, :], start=(a == 0), stop=(a == PASSES - 1),
-            )
-
-        for a in range(PASSES):
-            window = tab_w[a][:].bitcast(U32)
-            if a < PASSES - 1:
-                nc.vector.tensor_copy(v_w[a][:], window.indirect(idx[:]))
-            else:
-                for hf in range(2):
-                    nc.vector.tensor_copy(v_w[a][:, half(hf)], window.indirect(idx[:, list_half(hf)]))
+        def residual_pass(t, hf, a, b):
             if a == 0:
-                nc.vector.tensor_copy(v2_s[:], tab2_sc[:].indirect(idx2[:]))
-            for j in range(BLOCKS):
-                residual_pass(a, j)
-
-        ident = tile([P, P], F32, "ident")
-        make_identity(nc, ident[:])
-
-        w1_s = tile([P, PASSES, H], U8, "w1_s", tag="w2_s")
-        w1_c = {}
-        grouped = {}
-
-        def round_w1(a, u, engine_copy, tag):
-            grouped[a, u] = tile([P, H * PACK // 2], BF16, "grouped%d%d" % (a, u), tag=tag)
-            engine_copy(
-                out=grouped[a, u][:].rearrange("p (t m j) -> p m t j", t=2, j=PACK),
-                in_=w1_raw[a][:].rearrange("p j (m t) -> p m t j", t=PACK)[:, :, 2 * u : 2 * u + 2, :],
-            )
-
-        def quantize_w1(a, u):
-            w1_c[a, u] = tile([P, H // 2], U32, "w1_c%d%d" % (a, u))
-            nc.vector.quantize_mx(
-                out=w1_c[a, u][:].bitcast(FP8X4), scales=w1_s[:, a, u * H // 2 : (u + 1) * H // 2], in_=grouped[a, u][:]
-            )
-
-        for a in range(PASSES - 1):
-            for u in range(2):
-                round_w1(a, u, nc.scalar.copy, "grouped%d%d" % (a, u))
-
-        res = [tile([P, NB], F32, "res_sb%d" % j)[:] for j in range(VECTOR_BLOCKS)]
-        res_late = tile([P, BLOCKS - VECTOR_BLOCKS, NB], F32, "res_late", tag="w1_raw1")
-        res.extend(res_late[:, j, :] for j in range(BLOCKS - VECTOR_BLOCKS))
-        for j in range(BLOCKS):
-            copy = nc.vector.tensor_copy if j < VECTOR_BLOCKS else nc.scalar.copy
-            copy(out=res[j].rearrange("p (t m) -> p t m", t=PACK), in_=res_ps[j][:].rearrange("p (m t) -> p t m", t=PACK))
-
-        acc = {}
-
-        def branch_pass(t, hf, a, b):
-            if (t, hf) not in acc:
-                acc[t, hf] = bank(b, "acc%d%d" % (t, hf))
-            ch = slice(t % 2 * P, (t % 2 + 1) * P)
+                res_ps[t, hf] = bank(b, "res%d%d" % (t, hf))
+            i, u = (0, t) if t < EARLY else (1, 0)
             nc.tensor.matmul_mx(
-                out=acc[t, hf][:], lhsT=w1_c[a, t // 2][:, ch].bitcast(FP8X4), lhsT_scale=w1_s[:, a, block(t)],
+                out=res_ps[t, hf][:], lhsT=w2_c[i][:, a, u, :].bitcast(FP4X4), lhsT_scale=w2_s[i][:, a, u, :],
                 rhs=v_w[a][:, half(hf)].bitcast(FP8X4), rhs_scale=v_s[:, a, half(hf)],
                 start=(a == 0), stop=(a == PASSES - 1),
             )
 
-        back = {}
+        def branch_pass(t, hf, a, b):
+            if a == 0:
+                acc[t, hf] = bank(b, "acc%d%d" % (t, hf))
+            nc.tensor.matmul_mx(
+                out=acc[t, hf][:], lhsT=w1_c[a, t].bitcast(FP8X4), lhsT_scale=w1_s[a, t],
+                rhs=v_w[a][:, half(hf)].bitcast(FP8X4), rhs_scale=v_s[:, a, half(hf)],
+                start=(a == 0), stop=(a == PASSES - 1),
+            )
 
-        def turn_residual(t, hf, b):
-            back[t, hf] = bank(b, "res_back%d%d" % (t, hf))
-            for i in range(NB // P):
-                nc.tensor.transpose(back[t, hf][:, block(i)], res[hf * NB // P + i][:, block(t)], ident[:])
+        def gather_words(a, cols):
+            nc.vector.tensor_copy(v_w[a][:, cols], tab_w[a][:].bitcast(U32).indirect(idx[:, cols.start // 16 : cols.stop // 16]))
 
-        turn_residual(0, 0, 0)
-        turn_residual(1, 0, 1)
-        quantize_w1(0, 0)
-        quantize_w1(0, 1)
-        quantize_w1(1, 0)
-        for a in range(PASSES - 1):
-            for t in range(2):
+        gather_words(0, slice(0, S))
+        load_w1(1)
+        load_w1(2)
+        gain_sb = placed([P, PACK], F32, "gain_sb", 70)
+        aff_sb = placed([P, S2 // P], F32, "aff_sb", 70.5)
+        nc.sync.dma_start(out=gain_sb[:], in_=gain.rearrange("(p t) -> p t", t=PACK))
+        with nc.allow_non_contiguous_dma(reason="one offset for each partition and tile of antibodies"):
+            nc.sync.dma_start(out=aff_sb[:], in_=aff.rearrange("(c p) -> p c", p=P))
+        gather_words(1, slice(0, S))
+        load_page(0)
+        nc.vector.tensor_copy(v2_s[:], tab2_sc[:].indirect(idx2[:]))
+        for hf in range(2):
+            gather_words(2, half(hf))
+        load_wgs(0, slice(0, FIRST))
+        load_wgs(0, slice(FIRST, S))
+        load_page(1)
+        load_wgs(1, slice(0, S))
+        for a in range(PASSES):
+            for hf in range(2):
+                for t in range(EARLY):
+                    residual_pass(t, hf, a, 2 * t + hf)
+            if a == 0:
                 for hf in range(2):
-                    branch_pass(t, hf, a, 2 + 2 * t + hf)
-        last_a = PASSES - 1
-        round_w1(last_a, 0, nc.vector.tensor_copy, "w2_c")
-        quantize_w1(1, 1)
-        quantize_w1(last_a, 0)
+                    branch_pass(0, hf, a, 6 + hf)
+
+        ident = tile([P, P], F32, "ident")
+        make_identity(nc, ident[:])
+
+        res = {}
+
+        def keep_residual(t, hf, copy):
+            res[t, hf] = placed([P, NB], F32, "res_sb%d%d" % (t, hf), RES_KIB[t] + 2 * hf)
+            copy(out=res[t, hf][:], in_=res_ps[t, hf][:])
+
+        for sets in (low, high):
+            round_w1(1, sets, nc.scalar.copy, tile([P, H * PACK // 2], BF16, "grouped1%d" % sets.start))
+        load_wgs(2, slice(0, S))
+        for hf in range(2):
+            for t in range(1, EARLY):
+                keep_residual(t, hf, nc.vector.tensor_copy)
+        late_s = placed([P, PASSES - 1, H], U8, "w1_s_late", 80)
+        quantize_w1(1, low, late_s[:, 0, 0 : 2 * P])
+        for hf in range(2):
+            branch_pass(0, hf, 1, 6 + hf)
+        for a in range(PASSES - 1):
+            for hf in range(2):
+                branch_pass(1, hf, a, 2 + hf)
+        round_w1(2, low, nc.vector.tensor_copy, placed([P, H * PACK // 2], BF16, "grouped20", 56))
+        quantize_w1(1, high, late_s[:, 0, 2 * P : H])
+        quantize_w1(2, low, late_s[:, 1, 0 : 2 * P])
         for t in range(2):
             for hf in range(2):
-                branch_pass(t, hf, last_a, 2 + 2 * t + hf)
-        round_w1(last_a, 1, nc.vector.tensor_copy, "w2_c")
-        quantize_w1(last_a, 1)
+                branch_pass(t, hf, 2, None)
+        round_w1(2, high, nc.vector.tensor_copy, placed([P, H * PACK // 2], BF16, "grouped22", 56))
+        quantize_w1(2, high, late_s[:, 1, 2 * P : H])
+        load_page(2)
+        load_page(3)
+        load_wgs(3, slice(0, S))
+        for hf in range(2):
+            for a in range(PASSES):
+                branch_pass(2, hf, a, 4 + hf)
 
         h = {}
         page_bf = [tile([P, hi - lo, PACK], BF16, "page_bf%d" % i) if i not in (1, 2) else None for i, (lo, hi) in enumerate(PIECES)]
@@ -233,39 +267,38 @@ def tile_list_antivenom_panel_scores_kernel(
                 acts[t, hf] = tile([P, NB], F32, "silu%d%d" % (t, hf), tag="silu%d%d" % (t % 2, hf))
             nc.scalar.activation(out=acts[t, hf][:, cols], in_=acc[t, hf][:, cols], func=ACT.Silu)
 
-        def join(t, hf, cols):
+        def join(t, hf, cols, residual):
             if t not in h:
                 h[t] = tile([P, S], F32, "h%d" % t, tag="h%d" % (t % 2))
             nc.vector.scalar_tensor_tensor(
                 out=h[t][:, hf * NB + cols.start : hf * NB + cols.stop], in0=acts[t, hf][:, cols],
-                scalar=gain_sb[:, t : t + 1], in1=back[t, hf][:, cols], op0=ALU.mult, op1=ALU.add,
+                scalar=gain_sb[:, t : t + 1], in1=residual[:, cols], op0=ALU.mult, op1=ALU.add,
             )
 
         turned = {}
 
-        def turn_branch(t, hf):
+        def sum_turned(t, hf):
             silu(t, hf, slice(0, NB))
             gained = tile([P, NB], F32, "gained%d%d" % (t, hf), tag="gained%d" % hf)
             nc.scalar.activation(out=gained[:], in_=acts[t, hf][:], func=ACT.Copy, scale=gain_sb[:, t : t + 1])
-            turned[t, hf] = bank(6 + hf, "turned%d%d" % (t, hf))
+            ps = bank(6 + hf, "turned%d%d" % (t, hf))
             for i in range(NB // P):
-                nc.tensor.transpose(turned[t, hf][:, block(i)], gained[:, block(i)], ident[:])
+                nc.tensor.matmul(ps[:, block(i)], lhsT=gained[:, block(i)], rhs=ident[:], is_transpose=True, start=True, stop=False)
+                nc.tensor.matmul(ps[:, block(i)], lhsT=res[t, hf][:, block(i)], rhs=ident[:], is_transpose=True, start=False, stop=True)
+            turned[t, hf] = ps
 
-        def sum_back(t, hf, b):
+        def turn_back(t, hf):
             rows = tile([P, NB], F32, "turned_sb%d%d" % (t, hf), tag="silu%d%d" % (t % 2, hf))
             nc.scalar.copy(out=rows[:], in_=turned[t, hf][:])
-            back[t, hf] = bank(b, "sum%d%d" % (t, hf))
+            ps = bank(BACK_BANK[t] + hf, "back%d%d" % (t, hf))
             for i in range(NB // P):
-                ps = back[t, hf][:, block(i)]
-                nc.tensor.matmul(ps, lhsT=rows[:, block(i)], rhs=ident[:], is_transpose=True, start=True, stop=False)
-                nc.tensor.matmul(
-                    ps, lhsT=res[hf * NB // P + i][:, block(t)], rhs=ident[:], is_transpose=True, start=False, stop=True
-                )
+                nc.tensor.transpose(ps[:, block(i)], rows[:, block(i)], ident[:])
+            turned[t, hf] = ps
 
         def take_h(t, hf):
             if hf == 0:
                 h[t] = tile([P, S], F32, "h%d" % t, tag="h%d" % (t % 2))
-            nc.scalar.copy(out=h[t][:, half(hf)], in_=back[t, hf][:])
+            nc.scalar.copy(out=h[t][:, half(hf)], in_=turned[t, hf][:])
 
         def scatter(t, cols):
             nc.vector.tensor_tensor(
@@ -273,7 +306,7 @@ def tile_list_antivenom_panel_scores_kernel(
             )
 
         first_plain = PIECES[PAIRED][0]
-        staged = tile([P, PACK - 1, T2 - first_plain], BF16, "staged", tag="tab_sc")
+        staged = tile([P, PACK - 1, T2 - first_plain], BF16, "staged")
 
         def round_plane(t):
             for i, (lo, hi) in enumerate(PIECES[:PAIRED]):
@@ -296,37 +329,31 @@ def tile_list_antivenom_panel_scores_kernel(
             )
 
         full = slice(0, NB)
-        late_banks = {(2, 0): 0, (2, 1): 4, (3, 0): 5, (3, 1): 1}
-
-        def late_branch(t, hf):
-            for a in range(PASSES):
-                branch_pass(t, hf, a, late_banks[t, hf])
-
         for cols in (slice(0, FIRST), slice(FIRST, NB)):
             silu(0, 0, cols)
-            join(0, 0, cols)
+            join(0, 0, cols, res_ps[0, 0])
         scatter(0, slice(0, FIRST))
-        turn_residual(0, 1, 2)
         silu(0, 1, full)
-        join(0, 1, full)
-        turn_residual(1, 1, 3)
-        late_branch(2, 0)
+        join(0, 1, full, res_ps[0, 1])
         silu(1, 0, full)
-        join(1, 0, full)
-        late_branch(2, 1)
+        join(1, 0, full, res[1, 0])
         scatter(0, slice(FIRST, S))
         silu(1, 1, full)
-        join(1, 1, full)
-        late_branch(3, 0)
-        late_branch(3, 1)
+        join(1, 1, full, res[1, 1])
+        for hf in range(2):
+            for a in range(PASSES):
+                residual_pass(EARLY, hf, a, hf)
+            for a in range(PASSES):
+                branch_pass(EARLY, hf, a, 2 + hf)
         scatter(1, slice(0, S))
         for t in (2, 3):
             for hf in range(2):
-                turn_branch(t, hf)
-            for hf in range(2):
-                sum_back(t, hf, late_banks[t, hf])
-            for hf in range(2):
-                take_h(t, hf)
+                if t == EARLY:
+                    keep_residual(t, hf, nc.scalar.copy)
+                sum_turned(t, hf)
+            for step in (turn_back, take_h):
+                for hf in range(2):
+                    step(t, hf)
             if t == 2:
                 round_plane(0)
         scatter(2, slice(0, S))
@@ -334,14 +361,12 @@ def tile_list_antivenom_panel_scores_kernel(
         scatter(3, slice(0, S))
         round_plane(2)
 
+        tab2_w = placed([P, T3], I32, "tab2_w", 62)
+        nc.sync.dma_start(out=tab2_w[:], in_=tab2_words[0].rearrange("p t i -> p (t i)").bitcast(I32))
         lod_rows = lod.rearrange("(c p) m -> p c m", p=P)
-        lod_sb = []
+        lod_sb = [placed([P, 2, M], F32, "lod%d" % i, (32, 24)[i]) for i in range(2)]
         for i in range(2):
-            floor = tile([P, 2, M], F32, "lod%d" % i, tag="w1_raw%d" % i)
-            nc.sync.dma_start(out=floor[:], in_=lod_rows[:, 2 * i : 2 * i + 2, :])
-            lod_sb.append(floor)
-        with nc.allow_non_contiguous_dma(reason="one offset for each partition and tile of antibodies"):
-            nc.sync.dma_start(out=aff_sb[:], in_=aff.rearrange("(c p) -> p c", p=P))
+            nc.sync.dma_start(out=lod_sb[i][:], in_=lod_rows[:, 2 * i : 2 * i + 2, :])
 
         v2_w = []
 
@@ -352,9 +377,8 @@ def tile_list_antivenom_panel_scores_kernel(
 
         gather_antibodies(0, "h0")
 
-        e_tags = ["tab_w0", "tab_w1", "tab_w2", "w1_raw2"]
-        e = [tile([P, T2], F32, "e%d" % n, tag=e_tags[n]) for n in range(S2 // P)]
-        page_c = [tile([P, NB], U32, "page_c%d" % c, tag="grouped%d%d" % (c // 2, c % 2)) for c in range(CHUNKS)]
+        e = [placed([P, T2], F32, "e%d" % n, PAGE_KIB[n]) for n in range(S2 // P)]
+        page_c = [tile([P, NB], U32, "page_c%d" % c) for c in range(CHUNKS)]
         page_s = [tile([P, NB], U8, "page_s%d" % c) for c in range(CHUNKS)]
 
         def quantize(i, lo, hi):

@@ -25,7 +25,7 @@ QUADS = 4
 CHUNKS = T2 // NB
 FIRST = 256
 AB_ROW = 4
-SCALE_ROWS = (8, 72)
+SCALE_ROW = 48
 PIECES = ((0, 256), (256, 768), (768, 1280), (1280, 1536), (1536, 1792), (1792, 2048))
 PAIRED = 3
 EARLY = 3
@@ -75,7 +75,7 @@ def tile_list_antivenom_panel_scores_kernel(
         tab_sc = placed([P, T], U8, "tab_sc", 32)
         nc.vector.memset(w2_s_raw[:].bitcast(I32), 0)
         nc.vector.memset(tab2_sc[:].bitcast(I32), 0)
-        for lo, hi in ((0, 8), (32, 64), (64, 72), (96, 128)):
+        for lo, hi in ((0, SCALE_ROW), (SCALE_ROW + 16 * PASSES, P)):
             nc.vector.memset(tab_sc[lo:hi, :].bitcast(I32), 0)
         for q in range(QUADS):
             nc.gpsimd.dma_start(
@@ -94,16 +94,15 @@ def tile_list_antivenom_panel_scores_kernel(
             nc.sync.dma_start(out=tab_w[a][:], in_=tab_words[a].rearrange("p t i -> p (t i)").bitcast(I32))
 
         load_w1(0)
-        by_row = tab_scales.rearrange("a q t -> q a t")
-        for u, row in enumerate(SCALE_ROWS):
-            nc.sync.dma_start(
-                out=tab_sc[row : row + 8 * PASSES, :].bitcast(I32), in_=by_row[8 * u : 8 * u + 8].bitcast(I32)
-            )
+        nc.sync.dma_start(
+            out=tab_sc[SCALE_ROW : SCALE_ROW + 16 * PASSES, :].bitcast(I32),
+            in_=tab_scales.rearrange("a q t -> q a t").bitcast(I32),
+        )
         nc.sync.dma_start(idx[:], offs)
         w2_raw = tile([P, PASSES, 2 * H], U8, "w2_raw")
         nc.sync.dma_start(out=w2_raw[:].bitcast(I32), in_=w2_words.rearrange("a p n -> p a n").bitcast(I32))
         for r in range(4):
-            if r == 2:
+            if r == 3:
                 load_tab(0)
             nc.sync.dma_start(
                 out=w2_s_raw[r:P:32, :, :].bitcast(I32),
@@ -118,8 +117,8 @@ def tile_list_antivenom_panel_scores_kernel(
         v_s = tile([P, PASSES, S], U8, "v_s")
         nc.vector.tensor_copy(v_rows[:], tab_sc[:].indirect(idx[:]))
         for q in range(QUADS):
-            row = SCALE_ROWS[q // 2] + (q % 2) * 4 * PASSES
-            nc.sync.dma_start(
+            row = SCALE_ROW + q * 4 * PASSES
+            nc.gpsimd.dma_start(
                 out=v_s[32 * q : 32 * q + 4, :, :].bitcast(I32), in_=v_rows[row : row + 4 * PASSES, :].bitcast(I32)
             )
         load_tab(2)
@@ -141,8 +140,8 @@ def tile_list_antivenom_panel_scores_kernel(
         w2_s = [placed([P, PASSES, EARLY, P], U8, "w2_s_early", 80), tile([P, PASSES, 1, P], U8, "w2_s_last")]
         for i, sets in enumerate((slice(0, EARLY), slice(EARLY, PACK))):
             nc.vector.tensor_copy(
-                out=w2_c[i][:].bitcast(U16).rearrange("p a t (u m) -> p u a t m", u=2),
-                in_=w2_raw[:].bitcast(U16).rearrange("p a (u m t) -> p u a t m", u=2, t=PACK)[:, :, :, sets, :],
+                out=w2_c[i][:].bitcast(U16),
+                in_=w2_raw[:].bitcast(U16).rearrange("p a (m t) -> p a t m", t=PACK)[:, :, sets, :],
             )
             nc.vector.tensor_copy(
                 out=w2_s[i][:].rearrange("p a t (u m) -> p u a t m", u=2),
@@ -167,7 +166,7 @@ def tile_list_antivenom_panel_scores_kernel(
 
         every, low, high = slice(0, PACK), slice(0, 2), slice(2, PACK)
         round_w1(0, every, nc.scalar.copy, tile([P, H * PACK], BF16, "grouped0"))
-        quantize_w1(0, every, tile([P, H], U8, "w1_s0")[:])
+        quantize_w1(0, every, placed([P, H], U8, "w1_s0", 81.5)[:])
 
         v_w = [tile([P, S], U32, "v_w%d" % a, tag="tab2_sc" if a == PASSES - 1 else None) for a in range(PASSES)]
         v2_s = tile([P, S2], U8, "v2_s")
@@ -198,11 +197,8 @@ def tile_list_antivenom_panel_scores_kernel(
         gather_words(0, slice(0, S))
         load_w1(1)
         load_w1(2)
-        gain_sb = placed([P, PACK], F32, "gain_sb", 70)
-        aff_sb = placed([P, S2 // P], F32, "aff_sb", 70.5)
+        gain_sb = placed([P, PACK], F32, "gain_sb", W1_KIB[0])
         nc.sync.dma_start(out=gain_sb[:], in_=gain.rearrange("(p t) -> p t", t=PACK))
-        with nc.allow_non_contiguous_dma(reason="one offset for each partition and tile of antibodies"):
-            nc.sync.dma_start(out=aff_sb[:], in_=aff.rearrange("(c p) -> p c", p=P))
         gather_words(1, slice(0, S))
         load_page(0)
         nc.vector.tensor_copy(v2_s[:], tab2_sc[:].indirect(idx2[:]))
@@ -363,6 +359,9 @@ def tile_list_antivenom_panel_scores_kernel(
 
         tab2_w = placed([P, T3], I32, "tab2_w", 62)
         nc.sync.dma_start(out=tab2_w[:], in_=tab2_words[0].rearrange("p t i -> p (t i)").bitcast(I32))
+        aff_sb = placed([P, S2 // P], F32, "aff_sb", 81.5)
+        with nc.allow_non_contiguous_dma(reason="one offset for each partition and tile of antibodies"):
+            nc.sync.dma_start(out=aff_sb[:], in_=aff.rearrange("(c p) -> p c", p=P))
         lod_rows = lod.rearrange("(c p) m -> p c m", p=P)
         lod_sb = [placed([P, 2, M], F32, "lod%d" % i, (32, 24)[i]) for i in range(2)]
         for i in range(2):

@@ -33,7 +33,7 @@ W1_KIB = (72, 0, 8)
 PAGE_KIB = (16, 40, 8, 49)
 WGS_KIB = (32, 36, 0, 57.5)
 RES_KIB = (None, 62, 66, 24)
-BACK_BANK = (None, None, 4, 2)
+BACK_BANK = (None, 2, 4, 2)
 
 
 def tile_list_antivenom_panel_scores_kernel(
@@ -99,7 +99,7 @@ def tile_list_antivenom_panel_scores_kernel(
             in_=tab_scales.rearrange("a q t -> q a t").bitcast(I32),
         )
         nc.sync.dma_start(idx[:], offs)
-        w2_raw = tile([P, PASSES, 2 * H], U8, "w2_raw")
+        w2_raw = placed([P, PASSES, 2 * H], U8, "w2_raw", 36)
         nc.sync.dma_start(out=w2_raw[:].bitcast(I32), in_=w2_words.rearrange("a p n -> p a n").bitcast(I32))
         for r in range(4):
             if r == 3:
@@ -121,7 +121,6 @@ def tile_list_antivenom_panel_scores_kernel(
             nc.gpsimd.dma_start(
                 out=v_s[32 * q : 32 * q + 4, :, :].bitcast(I32), in_=v_rows[row : row + 4 * PASSES, :].bitcast(I32)
             )
-        load_tab(2)
 
         page_rows = page0.rearrange("(p t) c -> t p c", t=PACK)
         wgs_rows = wgs.rearrange("(m t) j -> m t j", t=PACK)
@@ -147,6 +146,8 @@ def tile_list_antivenom_panel_scores_kernel(
                 out=w2_s[i][:].rearrange("p a t (u m) -> p u a t m", u=2),
                 in_=w2_s_raw[:].rearrange("p a (u m t) -> p u a t m", u=2, t=PACK)[:, :, :, sets, :],
             )
+
+        load_tab(2)
 
         w1_c, w1_s, grouped = {}, {}, {}
 
@@ -334,8 +335,9 @@ def tile_list_antivenom_panel_scores_kernel(
         silu(1, 0, full)
         join(1, 0, full, res[1, 0])
         scatter(0, slice(FIRST, S))
-        silu(1, 1, full)
-        join(1, 1, full, res[1, 1])
+        sum_turned(1, 1)
+        turn_back(1, 1)
+        take_h(1, 1)
         for hf in range(2):
             for a in range(PASSES):
                 residual_pass(EARLY, hf, a, hf)

@@ -31,8 +31,8 @@ PAIRED = 3
 EARLY = 3
 W1_KIB = (72, 0, 8)
 PAGE_KIB = (16, 40, 8, 49)
-WGS_KIB = (32, 36, 0, 57.5)
-RES_KIB = (None, 62, 66, 24)
+WGS_KIB = (28, 36, 0, 57.5)
+RES_KIB = (None, (62, 66), (64, 68), (24, 26))
 BACK_BANK = (None, 2, 4, 2)
 
 
@@ -69,6 +69,10 @@ def tile_list_antivenom_panel_scores_kernel(
         idx2 = lists.tile([P, S2 // 16], U16, name="idx2")
         idx3 = lists.tile([P, S // 16], U16, name="idx3")
         idx4 = lists.tile([P, M // 16], U16, name="idx4")
+
+        warm = tile([P, 2], F32, "warm")
+        nc.vector.memset(warm[:], 0.0)
+        nc.scalar.activation(out=warm[:, 1:2], in_=warm[:, 0:1], func=ACT.Silu)
 
         w2_s_raw = tile([P, PASSES, H], U8, "w2_s_raw")
         tab2_sc = tile([P, T3], U8, "tab2_sc")
@@ -201,12 +205,12 @@ def tile_list_antivenom_panel_scores_kernel(
         gain_sb = placed([P, PACK], F32, "gain_sb", W1_KIB[0])
         nc.sync.dma_start(out=gain_sb[:], in_=gain.rearrange("(p t) -> p t", t=PACK))
         gather_words(1, slice(0, S))
+        load_wgs(0, slice(0, FIRST))
         load_page(0)
+        load_wgs(0, slice(FIRST, S))
         nc.vector.tensor_copy(v2_s[:], tab2_sc[:].indirect(idx2[:]))
         for hf in range(2):
             gather_words(2, half(hf))
-        load_wgs(0, slice(0, FIRST))
-        load_wgs(0, slice(FIRST, S))
         load_page(1)
         load_wgs(1, slice(0, S))
         for a in range(PASSES):
@@ -223,28 +227,29 @@ def tile_list_antivenom_panel_scores_kernel(
         res = {}
 
         def keep_residual(t, hf, copy):
-            res[t, hf] = placed([P, NB], F32, "res_sb%d%d" % (t, hf), RES_KIB[t] + 2 * hf)
+            res[t, hf] = placed([P, NB], F32, "res_sb%d%d" % (t, hf), RES_KIB[t][hf])
             copy(out=res[t, hf][:], in_=res_ps[t, hf][:])
 
         for sets in (low, high):
-            round_w1(1, sets, nc.scalar.copy, tile([P, H * PACK // 2], BF16, "grouped1%d" % sets.start))
+            round_w1(1, sets, nc.scalar.copy, placed([P, H * PACK // 2], BF16, "grouped1%d" % sets.start, 84 if sets.start == 0 else 67))
         load_wgs(2, slice(0, S))
-        for hf in range(2):
-            for t in range(1, EARLY):
-                keep_residual(t, hf, nc.vector.tensor_copy)
+        for t in range(1, EARLY):
+            keep_residual(t, 0, nc.vector.tensor_copy)
         late_s = placed([P, PASSES - 1, H], U8, "w1_s_late", 80)
         quantize_w1(1, low, late_s[:, 0, 0 : 2 * P])
         for hf in range(2):
             branch_pass(0, hf, 1, 6 + hf)
         for a in range(PASSES - 1):
-            for hf in range(2):
-                branch_pass(1, hf, a, 2 + hf)
+            branch_pass(1, 0, a, 2)
         round_w1(2, low, nc.vector.tensor_copy, placed([P, H * PACK // 2], BF16, "grouped20", 56))
         quantize_w1(1, high, late_s[:, 0, 2 * P : H])
+        for t in range(1, EARLY):
+            keep_residual(t, 1, nc.scalar.copy)
         quantize_w1(2, low, late_s[:, 1, 0 : 2 * P])
-        for t in range(2):
-            for hf in range(2):
-                branch_pass(t, hf, 2, None)
+        for t, hf in ((0, 0), (0, 1), (1, 0)):
+            branch_pass(t, hf, 2, None)
+        for a in range(PASSES):
+            branch_pass(1, 1, a, 3)
         round_w1(2, high, nc.vector.tensor_copy, placed([P, H * PACK // 2], BF16, "grouped22", 56))
         quantize_w1(2, high, late_s[:, 1, 2 * P : H])
         load_page(2)

@@ -24,16 +24,16 @@ NB = 512
 QUADS = 4
 CHUNKS = T2 // NB
 FIRST = 256
-AB_ROW = 4
 SCALE_ROW = 48
+AB_ROW = 112
 PIECES = ((0, 256), (256, 768), (768, 1280), (1280, 1536), (1536, 1792), (1792, 2048))
 PAIRED = 3
-EARLY = 3
-W1_KIB = (72, 0, 8)
-PAGE_KIB = (16, 40, 8, 49)
-WGS_KIB = (28, 36, 0, 57.5)
-RES_KIB = (None, (62, 66), (64, 68), (24, 26))
-BACK_BANK = (None, 2, 4, 2)
+W1_KIB = (0, 8, 16)
+PAGE_KIB = (36, 0, 16, 52)
+WGS_KIB = (32, 8, 12, 60)
+GROUPED_KIB = 48
+RES_KIB = 72
+CODES_KIB = ((89, 64, 60), (56, 57, 90))
 
 
 def tile_list_antivenom_panel_scores_kernel(
@@ -59,9 +59,6 @@ def tile_list_antivenom_panel_scores_kernel(
         def half(i):
             return slice(i * NB, (i + 1) * NB)
 
-        def list_half(i):
-            return slice(i * NB // 16, (i + 1) * NB // 16)
-
         def block(i):
             return slice(i * P, (i + 1) * P)
 
@@ -78,14 +75,9 @@ def tile_list_antivenom_panel_scores_kernel(
         tab2_sc = tile([P, T3], U8, "tab2_sc")
         tab_sc = placed([P, T], U8, "tab_sc", 32)
         nc.vector.memset(w2_s_raw[:].bitcast(I32), 0)
-        nc.vector.memset(tab2_sc[:].bitcast(I32), 0)
         for lo, hi in ((0, SCALE_ROW), (SCALE_ROW + 16 * PASSES, P)):
             nc.vector.memset(tab_sc[lo:hi, :].bitcast(I32), 0)
-        for q in range(QUADS):
-            nc.gpsimd.dma_start(
-                out=tab2_sc[32 * q + AB_ROW : 32 * q + AB_ROW + 4, :].bitcast(I32),
-                in_=tab2_scales[0, 4 * q : 4 * q + 4, :].bitcast(I32),
-            )
+        nc.vector.memset(tab2_sc[0:AB_ROW, :].bitcast(I32), 0)
 
         w1_raw, tab_w, page, wgs_sb = {}, {}, {}, {}
 
@@ -97,32 +89,31 @@ def tile_list_antivenom_panel_scores_kernel(
             tab_w[a] = placed([P, T], I32, "tab_w%d" % a, 16 * a)
             nc.sync.dma_start(out=tab_w[a][:], in_=tab_words[a].rearrange("p t i -> p (t i)").bitcast(I32))
 
-        load_w1(0)
+        w2_raw = placed([P, PASSES, 2 * H], U8, "w2_raw", 36)
+        nc.sync.dma_start(out=w2_raw[:].bitcast(I32), in_=w2_words.rearrange("a p n -> p a n").bitcast(I32))
         nc.sync.dma_start(
             out=tab_sc[SCALE_ROW : SCALE_ROW + 16 * PASSES, :].bitcast(I32),
             in_=tab_scales.rearrange("a q t -> q a t").bitcast(I32),
         )
         nc.sync.dma_start(idx[:], offs)
-        w2_raw = placed([P, PASSES, 2 * H], U8, "w2_raw", 36)
-        nc.sync.dma_start(out=w2_raw[:].bitcast(I32), in_=w2_words.rearrange("a p n -> p a n").bitcast(I32))
         for r in range(4):
-            if r == 3:
-                load_tab(0)
             nc.sync.dma_start(
                 out=w2_s_raw[r:P:32, :, :].bitcast(I32),
                 in_=w2_scales.rearrange("a (q r) n -> r q a n", r=4)[r].bitcast(I32),
             )
+        load_tab(0)
+        nc.sync.dma_start(out=tab2_sc[AB_ROW:P, :].bitcast(I32), in_=tab2_scales[0].bitcast(I32))
         nc.sync.dma_start(idx2[:], offs2)
         load_tab(1)
         nc.sync.dma_start(idx3[:], offs3)
         nc.sync.dma_start(idx4[:], offs4)
 
-        v_rows = placed([P, S], U8, "v_rows", 70)
+        v_rows = tile([P, S], U8, "v_rows")
         v_s = tile([P, PASSES, S], U8, "v_s")
         nc.vector.tensor_copy(v_rows[:], tab_sc[:].indirect(idx[:]))
         for q in range(QUADS):
             row = SCALE_ROW + q * 4 * PASSES
-            nc.gpsimd.dma_start(
+            nc.sync.dma_start(
                 out=v_s[32 * q : 32 * q + 4, :, :].bitcast(I32), in_=v_rows[row : row + 4 * PASSES, :].bitcast(I32)
             )
 
@@ -139,125 +130,104 @@ def tile_list_antivenom_panel_scores_kernel(
             for q in (0, 2, 1, 3):
                 nc.sync.dma_start(out=wgs_sb[t][32 * q : 32 * q + 32, cols], in_=wgs_rows[:, t, cols])
 
-        w2_c = [placed([P, PASSES, EARLY, 2 * P], U8, "w2_c_early", 56), tile([P, PASSES, 1, 2 * P], U8, "w2_c_last")]
-        w2_s = [placed([P, PASSES, EARLY, P], U8, "w2_s_early", 80), tile([P, PASSES, 1, P], U8, "w2_s_last")]
-        for i, sets in enumerate((slice(0, EARLY), slice(EARLY, PACK))):
-            nc.vector.tensor_copy(
-                out=w2_c[i][:].bitcast(U16),
-                in_=w2_raw[:].bitcast(U16).rearrange("p a (m t) -> p a t m", t=PACK)[:, :, sets, :],
-            )
-            nc.vector.tensor_copy(
-                out=w2_s[i][:].rearrange("p a t (u m) -> p u a t m", u=2),
-                in_=w2_s_raw[:].rearrange("p a (u m t) -> p u a t m", u=2, t=PACK)[:, :, :, sets, :],
-            )
-
+        w2_c = tile([P, PASSES, PACK, 2 * P], U8, "w2_c")
+        w2_s = tile([P, PASSES, PACK, P], U8, "w2_s")
+        nc.vector.tensor_copy(
+            out=w2_c[:].bitcast(U16), in_=w2_raw[:].bitcast(U16).rearrange("p a (m t) -> p a t m", t=PACK)
+        )
+        nc.vector.tensor_copy(out=w2_s[:], in_=w2_s_raw[:].rearrange("p a (m t) -> p a t m", t=PACK))
         load_tab(2)
 
-        w1_c, w1_s, grouped = {}, {}, {}
-
-        def round_w1(a, sets, copy, dst):
-            grouped[a, sets.start] = dst
-            copy(
-                out=dst[:].rearrange("p (t m j) -> p m t j", m=P, j=PACK),
-                in_=w1_raw[a][:].rearrange("p j (m t) -> p m t j", t=PACK)[:, :, sets, :],
-            )
-
-        def quantize_w1(a, sets, scales):
-            codes = tile([P, (sets.stop - sets.start) * P], U32, "w1_c%d%d" % (a, sets.start))
-            nc.vector.quantize_mx(out=codes[:].bitcast(FP8X4), scales=scales, in_=grouped[a, sets.start][:])
-            for t in range(sets.start, sets.stop):
-                w1_c[a, t] = codes[:, block(t - sets.start)]
-                w1_s[a, t] = scales[:, block(t - sets.start)]
-
-        every, low, high = slice(0, PACK), slice(0, 2), slice(2, PACK)
-        round_w1(0, every, nc.scalar.copy, tile([P, H * PACK], BF16, "grouped0"))
-        quantize_w1(0, every, placed([P, H], U8, "w1_s0", 81.5)[:])
-
         v_w = [tile([P, S], U32, "v_w%d" % a, tag="tab2_sc" if a == PASSES - 1 else None) for a in range(PASSES)]
-        v2_s = tile([P, S2], U8, "v2_s")
-        acc, res_ps = {}, {}
-
-        def residual_pass(t, hf, a, b):
-            if a == 0:
-                res_ps[t, hf] = bank(b, "res%d%d" % (t, hf))
-            i, u = (0, t) if t < EARLY else (1, 0)
-            nc.tensor.matmul_mx(
-                out=res_ps[t, hf][:], lhsT=w2_c[i][:, a, u, :].bitcast(FP4X4), lhsT_scale=w2_s[i][:, a, u, :],
-                rhs=v_w[a][:, half(hf)].bitcast(FP8X4), rhs_scale=v_s[:, a, half(hf)],
-                start=(a == 0), stop=(a == PASSES - 1),
-            )
-
-        def branch_pass(t, hf, a, b):
-            if a == 0:
-                acc[t, hf] = bank(b, "acc%d%d" % (t, hf))
-            nc.tensor.matmul_mx(
-                out=acc[t, hf][:], lhsT=w1_c[a, t].bitcast(FP8X4), lhsT_scale=w1_s[a, t],
-                rhs=v_w[a][:, half(hf)].bitcast(FP8X4), rhs_scale=v_s[:, a, half(hf)],
-                start=(a == 0), stop=(a == PASSES - 1),
-            )
+        v2_rows = tile([P, S2], U8, "v2_rows")
+        acc, res_ps, res = {}, {}, {}
 
         def gather_words(a, cols):
             nc.vector.tensor_copy(v_w[a][:, cols], tab_w[a][:].bitcast(U32).indirect(idx[:, cols.start // 16 : cols.stop // 16]))
 
+        def residual_pass(t, hf, a):
+            if a == 0:
+                res_ps[t, hf] = bank(2 * t + hf, "res%d%d" % (t, hf))
+            nc.tensor.matmul_mx(
+                out=res_ps[t, hf][:], lhsT=w2_c[:, a, t, :].bitcast(FP4X4), lhsT_scale=w2_s[:, a, t, :],
+                rhs=v_w[a][:, half(hf)].bitcast(FP8X4), rhs_scale=v_s[:, a, half(hf)],
+                start=(a == 0), stop=(a == PASSES - 1),
+            )
+
         gather_words(0, slice(0, S))
+        load_w1(0)
         load_w1(1)
-        load_w1(2)
-        gain_sb = placed([P, PACK], F32, "gain_sb", W1_KIB[0])
-        nc.sync.dma_start(out=gain_sb[:], in_=gain.rearrange("(p t) -> p t", t=PACK))
         gather_words(1, slice(0, S))
+        load_w1(2)
+        gain_sb = placed([P, PACK], F32, "gain_sb", 24)
+        nc.sync.dma_start(out=gain_sb[:], in_=gain.rearrange("(p t) -> p t", t=PACK))
+        nc.vector.tensor_copy(v2_rows[:], tab2_sc[:].indirect(idx2[:]))
+        for hf in range(2):
+            gather_words(2, half(hf))
         load_wgs(0, slice(0, FIRST))
         load_page(0)
         load_wgs(0, slice(FIRST, S))
-        nc.vector.tensor_copy(v2_s[:], tab2_sc[:].indirect(idx2[:]))
-        for hf in range(2):
-            gather_words(2, half(hf))
-        load_page(1)
-        load_wgs(1, slice(0, S))
-        for a in range(PASSES):
+        for a in range(PASSES - 1):
             for hf in range(2):
-                for t in range(EARLY):
-                    residual_pass(t, hf, a, 2 * t + hf)
-            if a == 0:
-                for hf in range(2):
-                    branch_pass(0, hf, a, 6 + hf)
+                for t in range(PACK):
+                    residual_pass(t, hf, a)
+        for t, hf in ((0, 0), (1, 0), (2, 0), (3, 0), (0, 1), (1, 1), (2, 1), (3, 1)):
+            residual_pass(t, hf, PASSES - 1)
+        for u in range(2):
+            for hf in range(2):
+                for t in (2 * u, 2 * u + 1):
+                    res[t, hf] = placed([P, NB], F32, "res_sb%d%d" % (t, hf), RES_KIB + 4 * t + 2 * hf)
+                    nc.scalar.copy(out=res[t, hf][:], in_=res_ps[t, hf][:])
 
         ident = tile([P, P], F32, "ident")
         make_identity(nc, ident[:])
 
-        res = {}
+        w1_c, w1_s, grouped = {}, {}, {}
+        codes = {}
+        scales = [tile([P, H], U8, "w1_s0"), tile([P, H], U8, "w1_s1"), placed([P, H], U8, "w1_s2", 88.25)]
 
-        def keep_residual(t, hf, copy):
-            res[t, hf] = placed([P, NB], F32, "res_sb%d%d" % (t, hf), RES_KIB[t][hf])
-            copy(out=res[t, hf][:], in_=res_ps[t, hf][:])
+        def round_w1(a, u, copy):
+            grouped[a, u] = placed([P, H * PACK // 2], BF16, "grouped%d%d" % (a, u), GROUPED_KIB + 4 * a + 2 * u)
+            copy(
+                out=grouped[a, u][:].rearrange("p (t m j) -> p m t j", m=P, j=PACK),
+                in_=w1_raw[a][:].rearrange("p j (m t) -> p m t j", t=PACK)[:, :, 2 * u : 2 * u + 2, :],
+            )
 
-        for sets in (low, high):
-            round_w1(1, sets, nc.scalar.copy, placed([P, H * PACK // 2], BF16, "grouped1%d" % sets.start, 84 if sets.start == 0 else 67))
-        load_wgs(2, slice(0, S))
-        for t in range(1, EARLY):
-            keep_residual(t, 0, nc.vector.tensor_copy)
-        late_s = placed([P, PASSES - 1, H], U8, "w1_s_late", 80)
-        quantize_w1(1, low, late_s[:, 0, 0 : 2 * P])
-        for hf in range(2):
-            branch_pass(0, hf, 1, 6 + hf)
-        for a in range(PASSES - 1):
-            branch_pass(1, 0, a, 2)
-        round_w1(2, low, nc.vector.tensor_copy, placed([P, H * PACK // 2], BF16, "grouped20", 56))
-        quantize_w1(1, high, late_s[:, 0, 2 * P : H])
-        for t in range(1, EARLY):
-            keep_residual(t, 1, nc.scalar.copy)
-        quantize_w1(2, low, late_s[:, 1, 0 : 2 * P])
-        for t, hf in ((0, 0), (0, 1), (1, 0)):
-            branch_pass(t, hf, 2, None)
+        def quantize_w1(a, u):
+            cols = slice(2 * u * P, 2 * (u + 1) * P)
+            codes[a, u] = placed([P, 2 * P], U32, "w1_c%d%d" % (a, u), CODES_KIB[u][a])
+            nc.vector.quantize_mx(out=codes[a, u][:].bitcast(FP8X4), scales=scales[a][:, cols], in_=grouped[a, u][:])
+
+        def branch_pass(t, hf, a):
+            if a == 0:
+                acc[t, hf] = bank(2 * t + hf, "acc%d%d" % (t, hf))
+            nc.tensor.matmul_mx(
+                out=acc[t, hf][:], lhsT=codes[a, t // 2][:, block(t % 2)].bitcast(FP8X4), lhsT_scale=scales[a][:, block(t)],
+                rhs=v_w[a][:, half(hf)].bitcast(FP8X4), rhs_scale=v_s[:, a, half(hf)],
+                start=(a == 0), stop=(a == PASSES - 1),
+            )
+
+        def branch_passes(a, u):
+            for t in (2 * u, 2 * u + 1):
+                for hf in range(2):
+                    branch_pass(t, hf, a)
+
         for a in range(PASSES):
-            branch_pass(1, 1, a, 3)
-        round_w1(2, high, nc.vector.tensor_copy, placed([P, H * PACK // 2], BF16, "grouped22", 56))
-        quantize_w1(2, high, late_s[:, 1, 2 * P : H])
+            round_w1(a, 0, nc.vector.tensor_copy)
+            round_w1(a, 1, nc.vector.tensor_copy if a < PASSES - 1 else nc.scalar.copy)
+            quantize_w1(a, 0)
+            branch_passes(a, 0)
+            if a == 0:
+                load_page(1)
+            if a == 1:
+                load_wgs(1, slice(0, S))
+        for a in range(PASSES):
+            quantize_w1(a, 1)
+            branch_passes(a, 1)
         load_page(2)
+        load_wgs(2, slice(0, S))
         load_page(3)
         load_wgs(3, slice(0, S))
-        for hf in range(2):
-            for a in range(PASSES):
-                branch_pass(2, hf, a, 4 + hf)
 
         h = {}
         page_bf = [tile([P, hi - lo, PACK], BF16, "page_bf%d" % i) if i not in (1, 2) else None for i, (lo, hi) in enumerate(PIECES)]
@@ -283,7 +253,7 @@ def tile_list_antivenom_panel_scores_kernel(
             silu(t, hf, slice(0, NB))
             gained = tile([P, NB], F32, "gained%d%d" % (t, hf), tag="gained%d" % hf)
             nc.scalar.activation(out=gained[:], in_=acts[t, hf][:], func=ACT.Copy, scale=gain_sb[:, t : t + 1])
-            ps = bank(6 + hf, "turned%d%d" % (t, hf))
+            ps = bank(hf, "turned%d%d" % (t, hf))
             for i in range(NB // P):
                 nc.tensor.matmul(ps[:, block(i)], lhsT=gained[:, block(i)], rhs=ident[:], is_transpose=True, start=True, stop=False)
                 nc.tensor.matmul(ps[:, block(i)], lhsT=res[t, hf][:, block(i)], rhs=ident[:], is_transpose=True, start=False, stop=True)
@@ -292,7 +262,7 @@ def tile_list_antivenom_panel_scores_kernel(
         def turn_back(t, hf):
             rows = tile([P, NB], F32, "turned_sb%d%d" % (t, hf), tag="silu%d%d" % (t % 2, hf))
             nc.scalar.copy(out=rows[:], in_=turned[t, hf][:])
-            ps = bank(BACK_BANK[t] + hf, "back%d%d" % (t, hf))
+            ps = bank(2 * t + hf, "back%d%d" % (t, hf))
             for i in range(NB // P):
                 nc.tensor.transpose(ps[:, block(i)], rows[:, block(i)], ident[:])
             turned[t, hf] = ps
@@ -333,26 +303,19 @@ def tile_list_antivenom_panel_scores_kernel(
         full = slice(0, NB)
         for cols in (slice(0, FIRST), slice(FIRST, NB)):
             silu(0, 0, cols)
-            join(0, 0, cols, res_ps[0, 0])
+            join(0, 0, cols, res[0, 0])
         scatter(0, slice(0, FIRST))
         silu(0, 1, full)
-        join(0, 1, full, res_ps[0, 1])
+        join(0, 1, full, res[0, 1])
         silu(1, 0, full)
         join(1, 0, full, res[1, 0])
         scatter(0, slice(FIRST, S))
         sum_turned(1, 1)
         turn_back(1, 1)
         take_h(1, 1)
-        for hf in range(2):
-            for a in range(PASSES):
-                residual_pass(EARLY, hf, a, hf)
-            for a in range(PASSES):
-                branch_pass(EARLY, hf, a, 2 + hf)
         scatter(1, slice(0, S))
         for t in (2, 3):
             for hf in range(2):
-                if t == EARLY:
-                    keep_residual(t, hf, nc.scalar.copy)
                 sum_turned(t, hf)
             for step in (turn_back, take_h):
                 for hf in range(2):
@@ -364,13 +327,17 @@ def tile_list_antivenom_panel_scores_kernel(
         scatter(3, slice(0, S))
         round_plane(2)
 
-        tab2_w = placed([P, T3], I32, "tab2_w", 62)
+        tab2_w = placed([P, T3], I32, "tab2_w", 64)
         nc.sync.dma_start(out=tab2_w[:], in_=tab2_words[0].rearrange("p t i -> p (t i)").bitcast(I32))
-        aff_sb = placed([P, S2 // P], F32, "aff_sb", 81.5)
+        v2_s = placed([P, S2], U8, "v2_s", 88)
+        for q in range(QUADS):
+            row = AB_ROW + 4 * q
+            nc.sync.dma_start(out=v2_s[32 * q : 32 * q + 4, :].bitcast(I32), in_=v2_rows[row : row + 4, :].bitcast(I32))
+        aff_sb = placed([P, S2 // P], F32, "aff_sb", 88.5)
         with nc.allow_non_contiguous_dma(reason="one offset for each partition and tile of antibodies"):
             nc.sync.dma_start(out=aff_sb[:], in_=aff.rearrange("(c p) -> p c", p=P))
         lod_rows = lod.rearrange("(c p) m -> p c m", p=P)
-        lod_sb = [placed([P, 2, M], F32, "lod%d" % i, (32, 24)[i]) for i in range(2)]
+        lod_sb = [placed([P, 2, M], F32, "lod%d" % i, RES_KIB + 8 * i) for i in range(2)]
         for i in range(2):
             nc.sync.dma_start(out=lod_sb[i][:], in_=lod_rows[:, 2 * i : 2 * i + 2, :])
 
@@ -399,7 +366,7 @@ def tile_list_antivenom_panel_scores_kernel(
                 ps = bank(b, "score%d%d%d" % (n, c, cols.start))
             rows = slice(n % 2 * P, (n % 2 + 1) * P)
             nc.tensor.matmul_mx(
-                out=ps[:, cols], lhsT=v2_w[n // 2][:, rows].bitcast(FP8X4), lhsT_scale=v2_s[AB_ROW:P, n * P : (n + 1) * P],
+                out=ps[:, cols], lhsT=v2_w[n // 2][:, rows].bitcast(FP8X4), lhsT_scale=v2_s[:, n * P : (n + 1) * P],
                 rhs=page_c[c][:, cols].bitcast(FP8X4), rhs_scale=page_s[c][:, cols], start=True, stop=True,
             )
             return ps[:, cols]

@@ -96,12 +96,12 @@ def tile_list_antivenom_panel_scores_kernel(
             in_=tab_scales.rearrange("a q t -> q a t").bitcast(I32),
         )
         nc.sync.dma_start(idx[:], offs)
+        load_tab(0)
         for r in range(4):
             nc.sync.dma_start(
                 out=w2_s_raw[r:P:32, :, :].bitcast(I32),
                 in_=w2_scales.rearrange("a (q r) n -> r q a n", r=4)[r].bitcast(I32),
             )
-        load_tab(0)
         nc.sync.dma_start(out=tab2_sc[AB_ROW:P, :].bitcast(I32), in_=tab2_scales[0].bitcast(I32))
         nc.sync.dma_start(idx2[:], offs2)
         load_tab(1)
@@ -132,10 +132,10 @@ def tile_list_antivenom_panel_scores_kernel(
 
         w2_c = tile([P, PASSES, PACK, 2 * P], U8, "w2_c")
         w2_s = tile([P, PASSES, PACK, P], U8, "w2_s")
-        nc.vector.tensor_copy(
-            out=w2_c[:].bitcast(U16), in_=w2_raw[:].bitcast(U16).rearrange("p a (m t) -> p a t m", t=PACK)
-        )
-        nc.vector.tensor_copy(out=w2_s[:], in_=w2_s_raw[:].rearrange("p a (m t) -> p a t m", t=PACK))
+        for dst, src in ((w2_c[:].bitcast(U16), w2_raw[:].bitcast(U16)), (w2_s[:], w2_s_raw[:])):
+            nc.vector.tensor_copy(
+                out=dst.rearrange("p a t (u m) -> p u a m t", u=2), in_=src.rearrange("p a (u m t) -> p u a m t", u=2, t=PACK)
+            )
         load_tab(2)
 
         v_w = [tile([P, S], U32, "v_w%d" % a, tag="tab2_sc" if a == PASSES - 1 else None) for a in range(PASSES)]
@@ -307,19 +307,15 @@ def tile_list_antivenom_panel_scores_kernel(
         scatter(0, slice(0, FIRST))
         silu(0, 1, full)
         join(0, 1, full, res[0, 1])
-        silu(1, 0, full)
-        join(1, 0, full, res[1, 0])
         scatter(0, slice(FIRST, S))
-        sum_turned(1, 1)
-        turn_back(1, 1)
-        take_h(1, 1)
-        scatter(1, slice(0, S))
-        for t in (2, 3):
+        for t in (1, 2, 3):
             for hf in range(2):
                 sum_turned(t, hf)
             for step in (turn_back, take_h):
                 for hf in range(2):
                     step(t, hf)
+            if t == 1:
+                scatter(1, slice(0, S))
             if t == 2:
                 round_plane(0)
         scatter(2, slice(0, S))

@@ -24,15 +24,22 @@ NB = 512
 QUADS = 4
 CHUNKS = T2 // NB
 FIRST = 256
+FIRST_BANK = 7
+SHARE = (88, 48)
+LATE = ((2, 1),)
+LAST = (3, 1)
 SCALE_ROW = 48
 AB_ROW = 112
-PIECES = ((0, 256), (256, 768), (768, 1280), (1280, 1536), (1536, 1792), (1792, 2048))
-PAIRED = 3
+PIECES = ((0, 256), (256, 512), (512, 1024), (1024, 1536), (1536, 1792), (1792, 2048))
+PAIRED = 4
 W1_KIB = (0, 8, 16)
 PAGE_KIB = (36, 0, 16, 52)
 WGS_KIB = (32, 8, 12, 60)
 GROUPED_KIB = 48
-RES_KIB = 72
+RES_KIB = ((72, 74), (76, 78), (80, 97), (103, 109))
+PAIRS_KIB = (96, 98, 100, 104)
+STAGED_KIB = 108
+LOD_KIB = (72, 80)
 CODES_KIB = ((89, 64, 60), (56, 57, 90))
 
 
@@ -145,13 +152,13 @@ def tile_list_antivenom_panel_scores_kernel(
         def gather_words(a, cols):
             nc.vector.tensor_copy(v_w[a][:, cols], tab_w[a][:].bitcast(U32).indirect(idx[:, cols.start // 16 : cols.stop // 16]))
 
-        def residual_pass(t, hf, a):
+        def residual_pass(t, hf, a, closes):
             if a == 0:
                 res_ps[t, hf] = bank(2 * t + hf, "res%d%d" % (t, hf))
             nc.tensor.matmul_mx(
                 out=res_ps[t, hf][:], lhsT=w2_c[:, a, t, :].bitcast(FP4X4), lhsT_scale=w2_s[:, a, t, :],
                 rhs=v_w[a][:, half(hf)].bitcast(FP8X4), rhs_scale=v_s[:, a, half(hf)],
-                start=(a == 0), stop=(a == PASSES - 1),
+                start=(a == 0), stop=closes,
             )
 
         gather_words(0, slice(0, S))
@@ -170,14 +177,23 @@ def tile_list_antivenom_panel_scores_kernel(
         for a in range(PASSES - 1):
             for hf in range(2):
                 for t in range(PACK):
-                    residual_pass(t, hf, a)
-        for t, hf in ((0, 0), (1, 0), (2, 0), (3, 0), (0, 1), (1, 1), (2, 1), (3, 1)):
-            residual_pass(t, hf, PASSES - 1)
-        for u in range(2):
-            for hf in range(2):
-                for t in (2 * u, 2 * u + 1):
-                    res[t, hf] = placed([P, NB], F32, "res_sb%d%d" % (t, hf), RES_KIB + 4 * t + 2 * hf)
-                    nc.scalar.copy(out=res[t, hf][:], in_=res_ps[t, hf][:])
+                    if (t, hf) != LAST and (a == 0 or (t, hf) not in LATE):
+                        residual_pass(t, hf, a, False)
+        for hf in range(2):
+            for t in range(PACK):
+                if (t, hf) != LAST:
+                    residual_pass(t, hf, PASSES - 1, (t, hf) not in LATE)
+                if (t, hf) in LATE:
+                    residual_pass(t, hf, 1, True)
+
+        def keep_residual(t, hf):
+            res[t, hf] = placed([P, NB], F32, "res_sb%d%d" % (t, hf), RES_KIB[t][hf])
+            nc.scalar.copy(out=res[t, hf][:], in_=res_ps[t, hf][:])
+
+        for hf in range(2):
+            for t in range(PACK):
+                if (t, hf) != LAST:
+                    keep_residual(t, hf)
 
         ident = tile([P, P], F32, "ident")
         make_identity(nc, ident[:])
@@ -186,26 +202,37 @@ def tile_list_antivenom_panel_scores_kernel(
         codes = {}
         scales = [tile([P, H], U8, "w1_s0"), tile([P, H], U8, "w1_s1"), placed([P, H], U8, "w1_s2", 88.25)]
 
-        def round_w1(a, u, copy):
-            grouped[a, u] = placed([P, H * PACK // 2], BF16, "grouped%d%d" % (a, u), GROUPED_KIB + 4 * a + 2 * u)
+        def round_w1(a, u, copy, ms):
+            if (a, u) not in grouped:
+                grouped[a, u] = placed([P, H * PACK // 2], BF16, "grouped%d%d" % (a, u), GROUPED_KIB + 4 * a + 2 * u)
             copy(
-                out=grouped[a, u][:].rearrange("p (t m j) -> p m t j", m=P, j=PACK),
-                in_=w1_raw[a][:].rearrange("p j (m t) -> p m t j", t=PACK)[:, :, 2 * u : 2 * u + 2, :],
+                out=grouped[a, u][:].rearrange("p (t m j) -> p m t j", m=P, j=PACK)[:, ms, :, :],
+                in_=w1_raw[a][:].rearrange("p j (m t) -> p m t j", t=PACK)[:, ms, 2 * u : 2 * u + 2, :],
             )
 
         def quantize_w1(a, u):
             cols = slice(2 * u * P, 2 * (u + 1) * P)
             codes[a, u] = placed([P, 2 * P], U32, "w1_c%d%d" % (a, u), CODES_KIB[u][a])
-            nc.vector.quantize_mx(out=codes[a, u][:].bitcast(FP8X4), scales=scales[a][:, cols], in_=grouped[a, u][:])
+            parts = 2 if (a, u) == (PASSES - 1, 0) else 1
+            width = 2 * P // parts
+            for i in range(parts):
+                nc.vector.quantize_mx(
+                    out=codes[a, u][:, i * width : (i + 1) * width].bitcast(FP8X4),
+                    scales=scales[a][:, cols.start + i * width : cols.start + (i + 1) * width],
+                    in_=grouped[a, u][:, i * width * PACK : (i + 1) * width * PACK],
+                )
 
         def branch_pass(t, hf, a):
-            if a == 0:
-                acc[t, hf] = bank(2 * t + hf, "acc%d%d" % (t, hf))
-            nc.tensor.matmul_mx(
-                out=acc[t, hf][:], lhsT=codes[a, t // 2][:, block(t % 2)].bitcast(FP8X4), lhsT_scale=scales[a][:, block(t)],
-                rhs=v_w[a][:, half(hf)].bitcast(FP8X4), rhs_scale=v_s[:, a, half(hf)],
-                start=(a == 0), stop=(a == PASSES - 1),
-            )
+            parts = ((0, FIRST, FIRST_BANK), (FIRST, NB, 0)) if (t, hf) == (0, 0) else ((0, NB, 2 * t + hf),)
+            for lo, hi, b in parts:
+                if a == 0:
+                    acc[t, hf, lo] = bank(b, "acc%d%d%d" % (t, hf, lo))
+                cols = slice(hf * NB + lo, hf * NB + hi)
+                nc.tensor.matmul_mx(
+                    out=acc[t, hf, lo][:, lo:hi], lhsT=codes[a, t // 2][:, block(t % 2)].bitcast(FP8X4),
+                    lhsT_scale=scales[a][:, block(t)], rhs=v_w[a][:, cols].bitcast(FP8X4), rhs_scale=v_s[:, a, cols],
+                    start=(a == 0), stop=(a == PASSES - 1),
+                )
 
         def branch_passes(a, u):
             for t in (2 * u, 2 * u + 1):
@@ -213,8 +240,11 @@ def tile_list_antivenom_panel_scores_kernel(
                     branch_pass(t, hf, a)
 
         for a in range(PASSES):
-            round_w1(a, 0, nc.vector.tensor_copy)
-            round_w1(a, 1, nc.vector.tensor_copy if a < PASSES - 1 else nc.scalar.copy)
+            for u in range(2):
+                cut = P if a < PASSES - 1 else SHARE[u]
+                round_w1(a, u, nc.vector.tensor_copy, slice(0, cut))
+                if cut < P:
+                    round_w1(a, u, nc.scalar.copy, slice(cut, P))
             quantize_w1(a, 0)
             branch_passes(a, 0)
             if a == 0:
@@ -223,21 +253,20 @@ def tile_list_antivenom_panel_scores_kernel(
                 load_wgs(1, slice(0, S))
         for a in range(PASSES):
             quantize_w1(a, 1)
-            branch_passes(a, 1)
         load_page(2)
         load_wgs(2, slice(0, S))
         load_page(3)
         load_wgs(3, slice(0, S))
 
         h = {}
-        page_bf = [tile([P, hi - lo, PACK], BF16, "page_bf%d" % i) if i not in (1, 2) else None for i, (lo, hi) in enumerate(PIECES)]
-        pairs = [tile([P, 2, hi - lo, 2], BF16, "pairs%d" % i) for i, (lo, hi) in enumerate(PIECES[:PAIRED])]
+        page_bf = [tile([P, hi - lo, PACK], BF16, "page_bf%d" % i) if i != 3 else None for i, (lo, hi) in enumerate(PIECES)]
+        pairs = [placed([P, 2, hi - lo, 2], BF16, "pairs%d" % i, PAIRS_KIB[i]) for i, (lo, hi) in enumerate(PIECES[:PAIRED])]
         acts = {}
 
         def silu(t, hf, cols):
             if cols.start == 0:
                 acts[t, hf] = tile([P, NB], F32, "silu%d%d" % (t, hf), tag="silu%d%d" % (t % 2, hf))
-            nc.scalar.activation(out=acts[t, hf][:, cols], in_=acc[t, hf][:, cols], func=ACT.Silu)
+            nc.scalar.activation(out=acts[t, hf][:, cols], in_=acc[t, hf, cols.start][:, cols], func=ACT.Silu)
 
         def join(t, hf, cols, residual):
             if t not in h:
@@ -278,7 +307,7 @@ def tile_list_antivenom_panel_scores_kernel(
             )
 
         first_plain = PIECES[PAIRED][0]
-        staged = tile([P, PACK - 1, T2 - first_plain], BF16, "staged")
+        staged = placed([P, PACK - 1, T2 - first_plain], BF16, "staged", STAGED_KIB)
 
         def round_plane(t):
             for i, (lo, hi) in enumerate(PIECES[:PAIRED]):
@@ -315,9 +344,13 @@ def tile_list_antivenom_panel_scores_kernel(
                 for hf in range(2):
                     step(t, hf)
             if t == 1:
+                for a in range(PASSES):
+                    residual_pass(*LAST, a, a == PASSES - 1)
+                keep_residual(*LAST)
+                for a in range(PASSES):
+                    branch_passes(a, 1)
                 scatter(1, slice(0, S))
-            if t == 2:
-                round_plane(0)
+        round_plane(0)
         scatter(2, slice(0, S))
         round_plane(1)
         scatter(3, slice(0, S))
@@ -333,7 +366,7 @@ def tile_list_antivenom_panel_scores_kernel(
         with nc.allow_non_contiguous_dma(reason="one offset for each partition and tile of antibodies"):
             nc.sync.dma_start(out=aff_sb[:], in_=aff.rearrange("(c p) -> p c", p=P))
         lod_rows = lod.rearrange("(c p) m -> p c m", p=P)
-        lod_sb = [placed([P, 2, M], F32, "lod%d" % i, RES_KIB + 8 * i) for i in range(2)]
+        lod_sb = [placed([P, 2, M], F32, "lod%d" % i, LOD_KIB[i]) for i in range(2)]
         for i in range(2):
             nc.sync.dma_start(out=lod_sb[i][:], in_=lod_rows[:, 2 * i : 2 * i + 2, :])
 
@@ -371,32 +404,32 @@ def tile_list_antivenom_panel_scores_kernel(
             return e[n][:, c * NB + cols.start : c * NB + cols.stop]
 
         ends = [slice(0, NB // 2), slice(NB // 2, NB)]
-        last_c = CHUNKS - 1
         round_plane(PACK - 1)
         weave(0)
-        quantize(0, 0, 256)
-        page_bf[1] = tile([P, PIECES[1][1] - PIECES[1][0], PACK], BF16, "page_bf1", tag="pairs0")
         weave(1)
-        page_bf[2] = tile([P, PIECES[2][1] - PIECES[2][0], PACK], BF16, "page_bf2", tag="page_bf0")
+        quantize(0, 0, 256)
         weave(2)
         quantize(1, 256, 512)
-        quantize(1, 512, 768)
+        page_bf[3] = tile([P, PIECES[3][1] - PIECES[3][0], PACK], BF16, "page_bf3", tag="page_bf0")
+        weave(3)
+        quantize(2, 512, 1024)
+        quantize(3, 1024, 1280)
         quantize(3, 1280, 1536)
-        quantize(2, 768, 1024)
-        quantize(2, 1024, 1280)
         quantize(4, 1536, 1792)
         quantize(5, 1792, 2048)
         gather_antibodies(1, "page_bf4")
-        thirds = [bank(c, "score0%d" % c) for c in range(last_c)]
-        for c, i in ((0, 0), (0, 1), (1, 0), (2, 1), (1, 1), (2, 0)):
-            scores(0, c, ends[i], c, thirds[c])
-        for c in range(last_c):
-            nc.scalar.copy(out=place(0, c, full), in_=thirds[c][:])
-        for i, cols in enumerate(ends):
-            nc.vector.tensor_copy(out=place(0, last_c, cols), in_=scores(0, last_c, cols, last_c + i))
+        front = bank(0, "score00")
+        for cols in ends:
+            scores(0, 0, cols, 0, front)
+        nc.scalar.copy(out=place(0, 0, full), in_=front[:])
+        nc.scalar.copy(out=place(0, 1, full), in_=scores(0, 1, full, 1))
+        for c in (2, 3):
+            for i, cols in enumerate(ends):
+                copy = nc.vector.tensor_copy if (c, i) == (3, 1) else nc.scalar.copy
+                copy(out=place(0, c, cols), in_=scores(0, c, cols, 2 * c - 2 + i))
         for n in range(1, S2 // P):
             for c in range(CHUNKS):
-                b = (5, 3, 4, 6)[c] if n == 1 else (7, 0, 1, 2)[c]
+                b = ((0, 1, 4, 5), (6, 7, 2, 3))[n % 2][c]
                 nc.scalar.copy(out=place(n, c, full), in_=scores(n, c, full, b))
 
         x_tags = ["v_w0", "v_w1", "tab2_sc", "h1"]

@@ -25,6 +25,7 @@ QUADS = 4
 CHUNKS = T2 // NB
 FIRST = 256
 FIRST_BANK = 7
+RING = (6, 2, 3, 4, 5)
 SHARE = (88, 48)
 LATE = ((2, 1),)
 LAST = (3, 1)
@@ -259,7 +260,8 @@ def tile_list_antivenom_panel_scores_kernel(
         load_wgs(3, slice(0, S))
 
         h = {}
-        page_bf = [tile([P, hi - lo, PACK], BF16, "page_bf%d" % i) if i != 3 else None for i, (lo, hi) in enumerate(PIECES)]
+        page_bf = [tile([P, hi - lo, PACK], BF16, "page_bf%d" % i) if i != 3 else None for i, (lo, hi) in enumerate(PIECES[:-1])]
+        page_bf.append(placed([P, PIECES[-1][1] - PIECES[-1][0], PACK], BF16, "page_bf5", PAGE_KIB[1]))
         pairs = [placed([P, 2, hi - lo, 2], BF16, "pairs%d" % i, PAIRS_KIB[i]) for i, (lo, hi) in enumerate(PIECES[:PAIRED])]
         acts = {}
 
@@ -421,16 +423,17 @@ def tile_list_antivenom_panel_scores_kernel(
         front = bank(0, "score00")
         for cols in ends:
             scores(0, 0, cols, 0, front)
+        early = scores(1, 0, full, RING[0])
         nc.scalar.copy(out=place(0, 0, full), in_=front[:])
         nc.scalar.copy(out=place(0, 1, full), in_=scores(0, 1, full, 1))
         for c in (2, 3):
             for i, cols in enumerate(ends):
-                copy = nc.vector.tensor_copy if (c, i) == (3, 1) else nc.scalar.copy
+                copy = nc.vector.tensor_copy if (c, i) == (CHUNKS - 1, 1) else nc.scalar.copy
                 copy(out=place(0, c, cols), in_=scores(0, c, cols, 2 * c - 2 + i))
         for n in range(1, S2 // P):
             for c in range(CHUNKS):
-                b = ((0, 1, 4, 5), (6, 7, 2, 3))[n % 2][c]
-                nc.scalar.copy(out=place(n, c, full), in_=scores(n, c, full, b))
+                ps = early if (n, c) == (1, 0) else scores(n, c, full, RING[(CHUNKS * (n - 1) + c) % len(RING)])
+                nc.scalar.copy(out=place(n, c, full), in_=ps)
 
         x_tags = ["v_w0", "v_w1", "tab2_sc", "h1"]
         x = [tile([P, M], F32, "x%d" % n, tag=x_tags[n]) for n in range(S2 // P)]

from contextlib import ExitStack

import concourse.mybir as mybir
from concourse.masks import make_identity

K, H, T, S, T2, S2, T3, M = 1536, 512, 4096, 1024, 2048, 512, 2048, 1024
FLOPS = 2 * (2 * K * H * S + H * S2 * T2)

F32 = mybir.dt.float32
BF16 = mybir.dt.bfloat16
I32 = mybir.dt.int32
U32 = mybir.dt.uint32
U16 = mybir.dt.uint16
U8 = mybir.dt.uint8
FP8X4 = mybir.dt.float8_e4m3fn_x4
FP4X4 = mybir.dt.float4_e2m1fn_x4
ALU = mybir.AluOpType
ACT = mybir.ActivationFunctionType

P = 128
PACK = 4
PASSES = K // (P * PACK)
NB = 512
QUADS = 4
CHUNKS = T2 // NB
FIRST = 256
FIRST_BANK = 7
RING = (6, 2, 3, 4, 5)
SHARE = (88, 48)
LATE = ((2, 1),)
LAST = (3, 1)
SCALE_ROW = 48
AB_ROW = 112
PIECES = ((0, 256), (256, 512), (512, 1024), (1024, 1536), (1536, 1792), (1792, 2048))
PAIRED = 4
W1_KIB = (0, 8, 16)
PAGE_KIB = (36, 0, 16, 52)
WGS_KIB = (32, 8, 12, 60)
GROUPED_KIB = 48
RES_KIB = ((72, 74), (76, 78), (80, 97), (103, 109))
PAIRS_KIB = (96, 98, 100, 104)
STAGED_KIB = 108
LOD_KIB = (72, 80)
CODES_KIB = ((89, 64, 60), (56, 57, 90))


def tile_list_antivenom_panel_scores_kernel(
    tc, tab_words, tab_scales, offs, w1, w2_words, w2_scales, gain, page0, wgs, offs3,
    tab2_words, tab2_scales, offs2, aff, lod, offs4, out,
):
    nc = tc.nc
    with ExitStack() as ctx:
        lists = ctx.enter_context(tc.tile_pool(name="lists", bufs=1))
        sb = ctx.enter_context(tc.tile_pool(name="sb", bufs=1))
        shared = ctx.enter_context(tc.tile_pool(name="shared", bufs=1))
        psum = ctx.enter_context(tc.psum_pool(name="psum", bufs=1))

        def tile(shape, dtype, name, tag=None):
            return sb.tile(shape, dtype, name=name, tag=tag or name, align_bytes=64)

        def placed(shape, dtype, name, kib):
            return shared.tile(shape, dtype, name=name, offset=int(kib * 1024), align_bytes=64)

        def bank(i, name):
            return psum.tile([P, NB], F32, name=name, tag="bank%d" % i)

        def half(i):
            return slice(i * NB, (i + 1) * NB)

        def block(i):
            return slice(i * P, (i + 1) * P)

        idx = lists.tile([P, S // 16], U16, name="idx")
        idx2 = lists.tile([P, S2 // 16], U16, name="idx2")
        idx3 = lists.tile([P, S // 16], U16, name="idx3")
        idx4 = lists.tile([P, M // 16], U16, name="idx4")

        warm = tile([P, 2], F32, "warm")
        nc.vector.memset(warm[:], 0.0)
        nc.scalar.activation(out=warm[:, 1:2], in_=warm[:, 0:1], func=ACT.Silu)

        w2_s_raw = tile([P, PASSES, H], U8, "w2_s_raw")
        tab2_sc = tile([P, T3], U8, "tab2_sc")
        tab_sc = placed([P, T], U8, "tab_sc", 32)
        nc.vector.memset(w2_s_raw[:].bitcast(I32), 0)
        for lo, hi in ((0, SCALE_ROW), (SCALE_ROW + 16 * PASSES, P)):
            nc.vector.memset(tab_sc[lo:hi, :].bitcast(I32), 0)
        nc.vector.memset(tab2_sc[0:AB_ROW, :].bitcast(I32), 0)

        w1_raw, tab_w, page, wgs_sb = {}, {}, {}, {}

        def load_w1(a):
            w1_raw[a] = placed([P, PACK, H], F32, "w1_raw%d" % a, W1_KIB[a])
            nc.sync.dma_start(out=w1_raw[a][:], in_=w1[a * 512 : (a + 1) * 512, :].rearrange("(p j) c -> p j c", j=PACK))

        def load_tab(a):
            tab_w[a] = placed([P, T], I32, "tab_w%d" % a, 16 * a)
            nc.sync.dma_start(out=tab_w[a][:], in_=tab_words[a].rearrange("p t i -> p (t i)").bitcast(I32))

        w2_raw = placed([P, PASSES, 2 * H], U8, "w2_raw", 36)
        nc.sync.dma_start(out=w2_raw[:].bitcast(I32), in_=w2_words.rearrange("a p n -> p a n").bitcast(I32))
        nc.sync.dma_start(
            out=tab_sc[SCALE_ROW : SCALE_ROW + 16 * PASSES, :].bitcast(I32),
            in_=tab_scales.rearrange("a q t -> q a t").bitcast(I32),
        )
        nc.sync.dma_start(idx[:], offs)
        load_tab(0)
        for r in range(4):
            nc.sync.dma_start(
                out=w2_s_raw[r:P:32, :, :].bitcast(I32),
                in_=w2_scales.rearrange("a (q r) n -> r q a n", r=4)[r].bitcast(I32),
            )
        nc.sync.dma_start(out=tab2_sc[AB_ROW:P, :].bitcast(I32), in_=tab2_scales[0].bitcast(I32))
        nc.sync.dma_start(idx2[:], offs2)
        load_tab(1)
        nc.sync.dma_start(idx3[:], offs3)
        nc.sync.dma_start(idx4[:], offs4)

        v_rows = tile([P, S], U8, "v_rows")
        v_s = tile([P, PASSES, S], U8, "v_s")
        nc.vector.tensor_copy(v_rows[:], tab_sc[:].indirect(idx[:]))
        for q in range(QUADS):
            row = SCALE_ROW + q * 4 * PASSES
            nc.sync.dma_start(
                out=v_s[32 * q : 32 * q + 4, :, :].bitcast(I32), in_=v_rows[row : row + 4 * PASSES, :].bitcast(I32)
            )

        page_rows = page0.rearrange("(p t) c -> t p c", t=PACK)
        wgs_rows = wgs.rearrange("(m t) j -> m t j", t=PACK)

        def load_page(t):
            page[t] = placed([P, T2], F32, "page%d" % t, PAGE_KIB[t])
            nc.sync.dma_start(out=page[t][:], in_=page_rows[t])

        def load_wgs(t, cols):
            if t not in wgs_sb:
                wgs_sb[t] = placed([P, S], F32, "wgs%d" % t, WGS_KIB[t])
            for q in (0, 2, 1, 3):
                nc.sync.dma_start(out=wgs_sb[t][32 * q : 32 * q + 32, cols], in_=wgs_rows[:, t, cols])

        w2_c = tile([P, PASSES, PACK, 2 * P], U8, "w2_c")
        w2_s = tile([P, PASSES, PACK, P], U8, "w2_s")
        for dst, src in ((w2_c[:].bitcast(U16), w2_raw[:].bitcast(U16)), (w2_s[:], w2_s_raw[:])):
            nc.vector.tensor_copy(
                out=dst.rearrange("p a t (u m) -> p u a m t", u=2), in_=src.rearrange("p a (u m t) -> p u a m t", u=2, t=PACK)
            )
        load_tab(2)

        v_w = [tile([P, S], U32, "v_w%d" % a, tag="tab2_sc" if a == PASSES - 1 else None) for a in range(PASSES)]
        v2_rows = tile([P, S2], U8, "v2_rows")
        acc, res_ps, res = {}, {}, {}

        def gather_words(a, cols):
            nc.vector.tensor_copy(v_w[a][:, cols], tab_w[a][:].bitcast(U32).indirect(idx[:, cols.start // 16 : cols.stop // 16]))

        def residual_pass(t, hf, a, closes):
            if a == 0:
                res_ps[t, hf] = bank(2 * t + hf, "res%d%d" % (t, hf))
            nc.tensor.matmul_mx(
                out=res_ps[t, hf][:], lhsT=w2_c[:, a, t, :].bitcast(FP4X4), lhsT_scale=w2_s[:, a, t, :],
                rhs=v_w[a][:, half(hf)].bitcast(FP8X4), rhs_scale=v_s[:, a, half(hf)],
                start=(a == 0), stop=closes,
            )

        gather_words(0, slice(0, S))
        load_w1(0)
        load_w1(1)
        gather_words(1, slice(0, S))
        load_w1(2)
        gain_sb = placed([P, PACK], F32, "gain_sb", 24)
        nc.sync.dma_start(out=gain_sb[:], in_=gain.rearrange("(p t) -> p t", t=PACK))
        nc.vector.tensor_copy(v2_rows[:], tab2_sc[:].indirect(idx2[:]))
        for hf in range(2):
            gather_words(2, half(hf))
        load_wgs(0, slice(0, FIRST))
        load_page(0)
        load_wgs(0, slice(FIRST, S))
        for a in range(PASSES - 1):
            for hf in range(2):
                for t in range(PACK):
                    if (t, hf) != LAST and (a == 0 or (t, hf) not in LATE):
                        residual_pass(t, hf, a, False)
        for hf in range(2):
            for t in range(PACK):
                if (t, hf) != LAST:
                    residual_pass(t, hf, PASSES - 1, (t, hf) not in LATE)
                if (t, hf) in LATE:
                    residual_pass(t, hf, 1, True)

        def keep_residual(t, hf):
            res[t, hf] = placed([P, NB], F32, "res_sb%d%d" % (t, hf), RES_KIB[t][hf])
            nc.scalar.copy(out=res[t, hf][:], in_=res_ps[t, hf][:])

        for hf in range(2):
            for t in range(PACK):
                if (t, hf) != LAST:
                    keep_residual(t, hf)

        ident = tile([P, P], F32, "ident")
        make_identity(nc, ident[:])

        w1_c, w1_s, grouped = {}, {}, {}
        codes = {}
        scales = [tile([P, H], U8, "w1_s0"), tile([P, H], U8, "w1_s1"), placed([P, H], U8, "w1_s2", 88.25)]

        def round_w1(a, u, copy, ms):
            if (a, u) not in grouped:
                grouped[a, u] = placed([P, H * PACK // 2], BF16, "grouped%d%d" % (a, u), GROUPED_KIB + 4 * a + 2 * u)
            copy(
                out=grouped[a, u][:].rearrange("p (t m j) -> p m t j", m=P, j=PACK)[:, ms, :, :],
                in_=w1_raw[a][:].rearrange("p j (m t) -> p m t j", t=PACK)[:, ms, 2 * u : 2 * u + 2, :],
            )

        def quantize_w1(a, u):
            cols = slice(2 * u * P, 2 * (u + 1) * P)
            codes[a, u] = placed([P, 2 * P], U32, "w1_c%d%d" % (a, u), CODES_KIB[u][a])
            parts = 2 if (a, u) == (PASSES - 1, 0) else 1
            width = 2 * P // parts
            for i in range(parts):
                nc.vector.quantize_mx(
                    out=codes[a, u][:, i * width : (i + 1) * width].bitcast(FP8X4),
                    scales=scales[a][:, cols.start + i * width : cols.start + (i + 1) * width],
                    in_=grouped[a, u][:, i * width * PACK : (i + 1) * width * PACK],
                )

        def branch_pass(t, hf, a):
            parts = ((0, FIRST, FIRST_BANK), (FIRST, NB, 0)) if (t, hf) == (0, 0) else ((0, NB, 2 * t + hf),)
            for lo, hi, b in parts:
                if a == 0:
                    acc[t, hf, lo] = bank(b, "acc%d%d%d" % (t, hf, lo))
                cols = slice(hf * NB + lo, hf * NB + hi)
                nc.tensor.matmul_mx(
                    out=acc[t, hf, lo][:, lo:hi], lhsT=codes[a, t // 2][:, block(t % 2)].bitcast(FP8X4),
                    lhsT_scale=scales[a][:, block(t)], rhs=v_w[a][:, cols].bitcast(FP8X4), rhs_scale=v_s[:, a, cols],
                    start=(a == 0), stop=(a == PASSES - 1),
                )

        def branch_passes(a, u):
            for t in (2 * u, 2 * u + 1):
                for hf in range(2):
                    branch_pass(t, hf, a)

        for a in range(PASSES):
            for u in range(2):
                cut = P if a < PASSES - 1 else SHARE[u]
                round_w1(a, u, nc.vector.tensor_copy, slice(0, cut))
                if cut < P:
                    round_w1(a, u, nc.scalar.copy, slice(cut, P))
            quantize_w1(a, 0)
            branch_passes(a, 0)
            if a == 0:
                load_page(1)
            if a == 1:
                load_wgs(1, slice(0, S))
        for a in range(PASSES):
            quantize_w1(a, 1)
        load_page(2)
        load_wgs(2, slice(0, S))
        load_page(3)
        load_wgs(3, slice(0, S))

        h = {}
        page_bf = [tile([P, hi - lo, PACK], BF16, "page_bf%d" % i) if i != 3 else None for i, (lo, hi) in enumerate(PIECES[:-1])]
        page_bf.append(placed([P, PIECES[-1][1] - PIECES[-1][0], PACK], BF16, "page_bf5", PAGE_KIB[1]))
        pairs = [placed([P, 2, hi - lo, 2], BF16, "pairs%d" % i, PAIRS_KIB[i]) for i, (lo, hi) in enumerate(PIECES[:PAIRED])]
        acts = {}

        def silu(t, hf, cols):
            if cols.start == 0:
                acts[t, hf] = tile([P, NB], F32, "silu%d%d" % (t, hf), tag="silu%d%d" % (t % 2, hf))
            nc.scalar.activation(out=acts[t, hf][:, cols], in_=acc[t, hf, cols.start][:, cols], func=ACT.Silu)

        def join(t, hf, cols, residual):
            if t not in h:
                h[t] = tile([P, S], F32, "h%d" % t, tag="h%d" % (t % 2))
            nc.vector.scalar_tensor_tensor(
                out=h[t][:, hf * NB + cols.start : hf * NB + cols.stop], in0=acts[t, hf][:, cols],
                scalar=gain_sb[:, t : t + 1], in1=residual[:, cols], op0=ALU.mult, op1=ALU.add,
            )

        turned = {}

        def sum_turned(t, hf):
            silu(t, hf, slice(0, NB))
            gained = tile([P, NB], F32, "gained%d%d" % (t, hf), tag="gained%d" % hf)
            nc.scalar.activation(out=gained[:], in_=acts[t, hf][:], func=ACT.Copy, scale=gain_sb[:, t : t + 1])
            ps = bank(hf, "turned%d%d" % (t, hf))
            for i in range(NB // P):
                nc.tensor.matmul(ps[:, block(i)], lhsT=gained[:, block(i)], rhs=ident[:], is_transpose=True, start=True, stop=False)
                nc.tensor.matmul(ps[:, block(i)], lhsT=res[t, hf][:, block(i)], rhs=ident[:], is_transpose=True, start=False, stop=True)
            turned[t, hf] = ps

        def turn_back(t, hf):
            rows = tile([P, NB], F32, "turned_sb%d%d" % (t, hf), tag="silu%d%d" % (t % 2, hf))
            nc.scalar.copy(out=rows[:], in_=turned[t, hf][:])
            ps = bank(2 * t + hf, "back%d%d" % (t, hf))
            for i in range(NB // P):
                nc.tensor.transpose(ps[:, block(i)], rows[:, block(i)], ident[:])
            turned[t, hf] = ps

        def take_h(t, hf):
            if hf == 0:
                h[t] = tile([P, S], F32, "h%d" % t, tag="h%d" % (t % 2))
            nc.scalar.copy(out=h[t][:, half(hf)], in_=turned[t, hf][:])

        def scatter(t, cols):
            nc.vector.tensor_tensor(
                page[t][:].indirect(idx3[:, cols.start // 16 : cols.stop // 16]), h[t][:, cols], wgs_sb[t][:, cols], ALU.mult
            )

        first_plain = PIECES[PAIRED][0]
        staged = placed([P, PACK - 1, T2 - first_plain], BF16, "staged", STAGED_KIB)

        def round_plane(t):
            for i, (lo, hi) in enumerate(PIECES[:PAIRED]):
                nc.scalar.copy(out=pairs[i][:, t // 2, :, t % 2], in_=page[t][:, lo:hi])
            if t < PACK - 1:
                nc.scalar.copy(out=staged[:, t, :], in_=page[t][:, first_plain:T2])
            for i, (lo, hi) in list(enumerate(PIECES))[PAIRED:]:
                if t == PACK - 2:
                    nc.scalar.copy(
                        out=page_bf[i][:, :, 0 : PACK - 1].rearrange("p (c i) t -> p c t i", i=PACK),
                        in_=staged[:, :, lo - first_plain : hi - first_plain].rearrange("p t (c i) -> p c t i", i=PACK),
                    )
                elif t == PACK - 1:
                    nc.scalar.copy(out=page_bf[i][:, :, t], in_=page[t][:, lo:hi])

        def weave(i):
            nc.vector.tensor_copy(
                out=page_bf[i][:].rearrange("p c t -> p (c t)").bitcast(I32).rearrange("p (c u) -> p c u", u=2),
                in_=pairs[i][:].rearrange("p u c e -> p u (c e)").bitcast(I32).rearrange("p u c -> p c u"),
            )

        full = slice(0, NB)
        for cols in (slice(0, FIRST), slice(FIRST, NB)):
            silu(0, 0, cols)
            join(0, 0, cols, res[0, 0])
        scatter(0, slice(0, FIRST))
        silu(0, 1, full)
        join(0, 1, full, res[0, 1])
        scatter(0, slice(FIRST, S))
        for t in (1, 2, 3):
            for hf in range(2):
                sum_turned(t, hf)
            for step in (turn_back, take_h):
                for hf in range(2):
                    step(t, hf)
            if t == 1:
                for a in range(PASSES):
                    residual_pass(*LAST, a, a == PASSES - 1)
                keep_residual(*LAST)
                for a in range(PASSES):
                    branch_passes(a, 1)
                scatter(1, slice(0, S))
        round_plane(0)
        scatter(2, slice(0, S))
        round_plane(1)
        scatter(3, slice(0, S))
        round_plane(2)

        tab2_w = placed([P, T3], I32, "tab2_w", 64)
        nc.sync.dma_start(out=tab2_w[:], in_=tab2_words[0].rearrange("p t i -> p (t i)").bitcast(I32))
        v2_s = placed([P, S2], U8, "v2_s", 88)
        for q in range(QUADS):
            row = AB_ROW + 4 * q
            nc.sync.dma_start(out=v2_s[32 * q : 32 * q + 4, :].bitcast(I32), in_=v2_rows[row : row + 4, :].bitcast(I32))
        aff_sb = placed([P, S2 // P], F32, "aff_sb", 88.5)
        with nc.allow_non_contiguous_dma(reason="one offset for each partition and tile of antibodies"):
            nc.sync.dma_start(out=aff_sb[:], in_=aff.rearrange("(c p) -> p c", p=P))
        lod_rows = lod.rearrange("(c p) m -> p c m", p=P)
        lod_sb = [placed([P, 2, M], F32, "lod%d" % i, LOD_KIB[i]) for i in range(2)]
        for i in range(2):
            nc.sync.dma_start(out=lod_sb[i][:], in_=lod_rows[:, 2 * i : 2 * i + 2, :])

        v2_w = []

        def gather_antibodies(i, tag):
            picked = tile([P, S2 // 2], U32, "v2_w%d" % i, tag=tag)
            nc.vector.tensor_copy(picked[:], tab2_w[:].bitcast(U32).indirect(idx2[:, i * S2 // 32 : (i + 1) * S2 // 32]))
            v2_w.append(picked)

        gather_antibodies(0, "h0")

        e = [placed([P, T2], F32, "e%d" % n, PAGE_KIB[n]) for n in range(S2 // P)]
        page_c = [tile([P, NB], U32, "page_c%d" % c) for c in range(CHUNKS)]
        page_s = [tile([P, NB], U8, "page_s%d" % c) for c in range(CHUNKS)]

        def quantize(i, lo, hi):
            c, cols = lo // NB, slice(lo % NB, lo % NB + hi - lo)
            nc.vector.quantize_mx(
                out=page_c[c][:, cols].bitcast(FP8X4), scales=page_s[c][:, cols],
                in_=page_bf[i][:, lo - PIECES[i][0] : hi - PIECES[i][0], :].rearrange("p c t -> p (c t)"),
            )

        def scores(n, c, cols, b, ps=None):
            if ps is None:
                ps = bank(b, "score%d%d%d" % (n, c, cols.start))
            rows = slice(n % 2 * P, (n % 2 + 1) * P)
            nc.tensor.matmul_mx(
                out=ps[:, cols], lhsT=v2_w[n // 2][:, rows].bitcast(FP8X4), lhsT_scale=v2_s[:, n * P : (n + 1) * P],
                rhs=page_c[c][:, cols].bitcast(FP8X4), rhs_scale=page_s[c][:, cols], start=True, stop=True,
            )
            return ps[:, cols]

        def place(n, c, cols):
            return e[n][:, c * NB + cols.start : c * NB + cols.stop]

        ends = [slice(0, NB // 2), slice(NB // 2, NB)]
        round_plane(PACK - 1)
        weave(0)
        weave(1)
        quantize(0, 0, 256)
        weave(2)
        quantize(1, 256, 512)
        page_bf[3] = tile([P, PIECES[3][1] - PIECES[3][0], PACK], BF16, "page_bf3", tag="page_bf0")
        weave(3)
        quantize(2, 512, 1024)
        quantize(3, 1024, 1280)
        quantize(3, 1280, 1536)
        quantize(4, 1536, 1792)
        quantize(5, 1792, 2048)
        gather_antibodies(1, "page_bf4")
        front = bank(0, "score00")
        for cols in ends:
            scores(0, 0, cols, 0, front)
        early = scores(1, 0, full, RING[0])
        nc.scalar.copy(out=place(0, 0, full), in_=front[:])
        nc.scalar.copy(out=place(0, 1, full), in_=scores(0, 1, full, 1))
        for c in (2, 3):
            for i, cols in enumerate(ends):
                copy = nc.vector.tensor_copy if (c, i) == (CHUNKS - 1, 1) else nc.scalar.copy
                copy(out=place(0, c, cols), in_=scores(0, c, cols, 2 * c - 2 + i))
        for n in range(1, S2 // P):
            for c in range(CHUNKS):
                ps = early if (n, c) == (1, 0) else scores(n, c, full, RING[(CHUNKS * (n - 1) + c) % len(RING)])
                nc.scalar.copy(out=place(n, c, full), in_=ps)

        x_tags = ["v_w0", "v_w1", "tab2_sc", "h1"]
        x = [tile([P, M], F32, "x%d" % n, tag=x_tags[n]) for n in range(S2 // P)]
        last = S2 // P - 1

        def pick(n, cols):
            nc.vector.tensor_copy(x[n][:, cols], e[n][:].indirect(idx4[:, cols.start // 16 : cols.stop // 16]))

        def finish(n, cols):
            nc.vector.scalar_tensor_tensor(
                out=x[n][:, cols], in0=x[n][:, cols], scalar=aff_sb[:, n : n + 1], in1=lod_sb[n // 2][:, n % 2, cols],
                op0=ALU.add, op1=ALU.max,
            )
            nc.sync.dma_start(out=out[n * P : (n + 1) * P, cols], in_=x[n][:, cols])

        pieces = [(n, slice(0, M)) for n in range(last)]
        pieces.extend((last, cols) for cols in (slice(0, M // 2), slice(M // 2, 3 * M // 4), slice(3 * M // 4, M)))
        pick(*pieces[0])
        for done, ahead in zip(pieces, pieces[1:]):
            pick(*ahead)
            finish(*done)
        finish(*pieces[-1])
